import numpy as np
import ml_dtypes


def mxq(x, axis, fmt="e4m3"):
    dtype, down = {"e4m3": (ml_dtypes.float8_e4m3fn, 7), "e5m2": (ml_dtypes.float8_e5m2, 14)}[fmt]
    v = np.moveaxis(np.asarray(x, np.float32).astype(ml_dtypes.bfloat16).astype(np.float64), axis, -1)
    blocks = v.reshape(v.shape[:-1] + (-1, 32))
    amax = np.abs(blocks).max(-1, keepdims=True)
    byte = np.maximum(np.where(amax > 0, np.frexp(amax)[1] - 1 + 127, 0) - down, 1)
    scale = np.exp2(byte - 127.0)
    codes = (blocks / scale).astype(np.float32).astype(dtype).astype(np.float64)
    return np.moveaxis((codes * scale).reshape(v.shape), -1, axis)


WIDE = False


def mx_kscale(k):
    if not WIDE:
        return np.ones(k)
    levels = np.array([30, -30])
    if k % 512:
        return np.exp2(np.random.permutation(np.resize(levels, k // 32))).repeat(32)
    a = np.empty((k // 512, 16))
    for p in range(k // 512):
        a[p, :8] = np.random.permutation(np.resize(levels, 8))
        for g in range(8):
            far = levels[np.abs(levels - a[p, g]) >= 10]
            a[p, g + 8] = far[np.random.randint(len(far))]
    return np.exp2(a.ravel()).repeat(32)


def f64(x):
    return np.asarray(x).astype(np.float64)


def striped(idx):
    return np.tile(idx.reshape(-1, 16).T, (8, 1)).astype(np.uint16)


def unstriped(offs):
    return offs[:16].T.reshape(-1).astype(np.int64)


E2M1 = np.array([0.0, 0.5, 1.0, 1.5, 2.0, 3.0, 4.0, 6.0, -0.0, -0.5, -1.0, -1.5, -2.0, -3.0, -4.0, -6.0])


def pack_weight(w, fmt):
    k, n = w.shape
    w = f64(np.asarray(w, np.float32).astype(ml_dtypes.bfloat16)).reshape(k // 32, 32, n)
    amax = np.abs(w).max(1)
    if fmt == "e4m3":
        byte = np.frexp(amax)[1] - 1 + 127 - 7
    else:
        mant, ex = np.frexp(amax / 6.0)
        byte = np.where(mant > 0.5, ex, ex - 1) + 127
    byte = np.clip(np.where(amax > 0, byte, 1), 1, 254)
    scaled = (w * np.exp2(127.0 - byte)[:, None, :]).reshape(k, n).astype(np.float32)
    by_word = np.ascontiguousarray(scaled.reshape(k // 512, 128, 4, n).transpose(0, 1, 3, 2))
    if fmt == "e4m3":
        words = by_word.astype(ml_dtypes.float8_e4m3fn).view(np.uint8)
    else:
        c = by_word.astype(ml_dtypes.float4_e2m1fn).view(np.uint8) & 0xF
        words = (c[..., 0::2] | (c[..., 1::2] << 4)).reshape(k // 512, 128, 2 * n)
    return np.ascontiguousarray(words), np.ascontiguousarray(byte.astype(np.uint8).reshape(k // 512, 16, n))


def unpack_weight(words, scales, fmt):
    g, _, n = scales.shape
    words = np.ascontiguousarray(words).reshape(g, 128, n, -1)
    if fmt == "e4m3":
        vals = words.view(ml_dtypes.float8_e4m3fn).astype(np.float64)
    else:
        nib = np.empty((g, 128, n, 4), np.uint8)
        nib[..., 0::2] = words & 0xF
        nib[..., 1::2] = words >> 4
        vals = E2M1[nib]
    vals = vals * np.repeat(np.exp2(scales.astype(np.float64) - 127.0), 8, axis=1)[..., None]
    return vals.transpose(0, 1, 3, 2).reshape(g * 512, n)


K, N, T, J = 1024, 1024, 2048, 1024


def setup_inputs():
    n = np.random.standard_normal
    s = mx_kscale(K)[:, None]
    m = np.exp(0.5 * n((1, J)))
    w = n((K, N)) / np.sqrt(K) / s
    p_w4 = pack_weight(w[512:], "e2m1")
    return {
        "dy": (m * n((K, J)) * s).astype(np.float32),
        "w8": (w[:512]).astype(np.float32),
        "w4_words": p_w4[0],
        "w4_scales": p_w4[1],
        "d": (0.5 + 0.3 * n((N, J))).astype(np.float32),
        "wgo": np.tile(np.random.uniform(0.5, 2.0, J), (128, 1)).astype(np.float32),
        "offs": striped(np.random.permutation(T)[:J]),
    }


def reference(dy, w8, w4_words, w4_scales, d, wgo, offs):
    idx = unstriped(offs)
    dy_ = mxq(f64(dy), 0, "e5m2")
    w8_ = mxq(f64(w8), 0, "e4m3")
    w4_ = unpack_weight(w4_words, w4_scales, "e2m1")
    dx = w8_.T @ dy_[:512] + w4_.T @ dy_[512:]
    out = np.zeros((N, T))
    out[:, idx] = f64(wgo)[0] * (dx * f64(d))
    return out

@@ -1,0 +1,250 @@
+from contextlib import ExitStack
+
+import concourse.mybir as mybir
+from concourse.masks import make_identity
+
+K, N, T, J = 1024, 1024, 2048, 1024
+FLOPS = 2 * K * N * J
+
+F32 = mybir.dt.float32
+BF16 = mybir.dt.bfloat16
+I32 = mybir.dt.int32
+U32 = mybir.dt.uint32
+U16 = mybir.dt.uint16
+U8 = mybir.dt.uint8
+E4M3X4 = mybir.dt.float8_e4m3fn_x4
+E5M2X4 = mybir.dt.float8_e5m2_x4
+E2M1X4 = mybir.dt.float4_e2m1fn_x4
+COPY = mybir.ActivationFunctionType.Copy
+MULT = mybir.AluOpType.mult
+
+P = 128
+PACK = 4
+K_PASS = P * PACK
+HALF = 512
+QUART = 256
+PAGES = 4
+
+
+def interleave(engine_copy, grouped, raw):
+    engine_copy(
+        grouped.rearrange("p (c i) t -> p c t i", i=4),
+        raw.rearrange("p t (c i) -> p c t i", i=4),
+    )
+
+
+def tile_list_embg_qf_mul_kernel(tc, dy, w8, w4_words, w4_scales, d, wgo, offs, out):
+    nc = tc.nc
+    vcopy = nc.vector.tensor_copy
+    scopy = nc.scalar.copy
+
+    with ExitStack() as ctx:
+        keep = ctx.enter_context(tc.tile_pool(name="keep", bufs=1))
+        ring = ctx.enter_context(tc.tile_pool(name="ring", bufs=10))
+        psum_mm = ctx.enter_context(tc.psum_pool(name="psum_mm", bufs=4))
+        psum_tr = ctx.enter_context(tc.psum_pool(name="psum_tr", bufs=4))
+
+        offsets = keep.tile([P, J // 16], U16, name="offsets")
+        w4_plane = keep.tile([P, N], U8, name="w4_plane", align_bytes=64)
+        wgo_rows = keep.tile([P, P], F32, name="wgo_rows")
+        wgo_cols = keep.tile([P, J // P], F32, name="wgo_cols")
+        ident = keep.tile([P, P], F32, name="ident")
+        w8_raw = [keep.tile([P, PACK, QUART], F32, name="w8_raw%d" % c, tag="w8_raw%d" % c) for c in range(4)]
+        w8_bf = [keep.tile([P, QUART, PACK], BF16, name="w8_bf%d" % c, align_bytes=64) for c in range(4)]
+        w8_codes = [keep.tile([P, HALF], U32, name="w8_codes%d" % h, align_bytes=64) for h in range(2)]
+        w8_plane = [keep.tile([P, HALF], U8, name="w8_plane%d" % h, align_bytes=64) for h in range(2)]
+        w4_codes = [keep.tile([P, 2 * HALF], U8, name="w4_codes%d" % h, align_bytes=64) for h in range(2)]
+        dy_raw, dy_bf, dy_codes, dy_plane = {}, {}, {}, {}
+        for q in range(4):
+            for a in range(2):
+                dy_raw[q, a] = keep.tile([P, PACK, QUART], F32, name="dy_raw%d%d" % (q, a), tag="dy_raw%d%d" % (q, a))
+                dy_bf[q, a] = keep.tile([P, QUART, PACK], BF16, name="dy_bf%d%d" % (q, a), align_bytes=64)
+                dy_codes[q, a] = keep.tile([P, QUART], U32, name="dy_codes%d%d" % (q, a), align_bytes=64)
+                dy_plane[q, a] = keep.tile([P, QUART], U8, name="dy_plane%d%d" % (q, a), align_bytes=64)
+        d_first = keep.tile([P, QUART], F32, name="d_first")
+        d_rest = keep.tile([P, 3, QUART], F32, name="d_rest")
+        d_q = [None] + [keep.tile([P, 4, QUART], F32, name="d_q%d" % q) for q in range(1, 4)]
+        d_hi = [keep.tile([P, J], F32, name="d_hi%d" % r) for r in range(4)]
+        dx_lo = {}
+        dx_hi = [keep.tile([P, J], F32, name="dx_hi%d" % r) for r in range(4)]
+        pages = [keep.tile([P, T], F32, name="page%d" % i) for i in range(PAGES)]
+
+        def load_w8(c):
+            nc.sync.dma_start(
+                out=w8_raw[c][:], in_=w8[:, c * QUART : (c + 1) * QUART].rearrange("(p t) n -> p t n", t=PACK)
+            )
+
+        def load_dy(q, a):
+            rows = dy[a * K_PASS : (a + 1) * K_PASS, q * QUART : (q + 1) * QUART]
+            nc.sync.dma_start(out=dy_raw[q, a][:], in_=rows.rearrange("(p t) j -> p t j", t=PACK))
+
+        def load_w4(h):
+            nc.sync.dma_start(
+                out=w4_codes[h][:].bitcast(I32), in_=w4_words[0][:, 2 * HALF * h : 2 * HALF * (h + 1)].bitcast(I32)
+            )
+
+        def load_d(tile, r0, r1, q):
+            rows = d[r0 * P : r1 * P, q * QUART : (q + 1) * QUART]
+            nc.sync.dma_start(out=tile[:], in_=rows.rearrange("(r p) j -> p r j", p=P))
+
+        nc.vector.memset(w4_plane[:].bitcast(I32), 0)
+        nc.vector.memset(wgo_rows[:], 0.0)
+        make_identity(nc, ident[:])
+
+        load_w8(0)
+        load_w8(1)
+        for quad in range(4):
+            nc.sync.dma_start(
+                out=w4_plane[32 * quad : 32 * quad + 4, :].bitcast(I32),
+                in_=w4_scales[0][4 * quad : 4 * quad + 4, :].bitcast(I32),
+            )
+        nc.sync.dma_start(out=wgo_rows[0 : J // P, :], in_=wgo[0].rearrange("(c p) -> c p", p=P))
+        load_dy(0, 0)
+        load_w4(0)
+        load_dy(0, 1)
+        nc.sync.dma_start(offsets[:], offs)
+        nc.sync.dma_start(out=d_first[:], in_=d[0:P, 0:QUART])
+        load_dy(1, 0)
+        load_dy(1, 1)
+        load_d(d_rest, 1, 4, 0)
+        load_dy(2, 0)
+        load_dy(2, 1)
+        load_d(d_q[1], 0, 4, 1)
+        load_dy(3, 0)
+        load_dy(3, 1)
+        load_w8(2)
+        load_w8(3)
+        load_d(d_q[2], 0, 4, 2)
+        load_w4(1)
+        load_d(d_q[3], 0, 4, 3)
+        for r in range(4):
+            nc.sync.dma_start(out=d_hi[r][:], in_=d[(4 + r) * P : (5 + r) * P, :])
+
+        def quantize_w8(c):
+            cols = slice((c % 2) * QUART, (c % 2 + 1) * QUART)
+            nc.vector.quantize_mx(
+                out=w8_codes[c // 2][:, cols].bitcast(E4M3X4),
+                scales=w8_plane[c // 2][:, cols],
+                in_=w8_bf[c][:].rearrange("p n t -> p (n t)"),
+            )
+
+        def quantize_dy(q, a, cols):
+            nc.vector.quantize_mx(
+                out=dy_codes[q, a][:, cols].bitcast(E5M2X4),
+                scales=dy_plane[q, a][:, cols],
+                in_=dy_bf[q, a][:, cols, :].rearrange("p j t -> p (j t)"),
+            )
+
+        def mm_pass(acc, jt, h, a):
+            q, cols = jt // 2, slice((jt % 2) * P, (jt % 2 + 1) * P)
+            if a == 0:
+                rhs, rhs_scale = w8_codes[h][:].bitcast(E4M3X4), w8_plane[h][:]
+            else:
+                rhs, rhs_scale = w4_codes[h][:].bitcast(E2M1X4), w4_plane[:, h * HALF : (h + 1) * HALF]
+            nc.tensor.matmul_mx(
+                out=acc[:],
+                lhsT=dy_codes[q, a][:, cols].bitcast(E5M2X4),
+                lhsT_scale=dy_plane[q, a][:, cols],
+                rhs=rhs,
+                rhs_scale=rhs_scale,
+                start=(a == 0),
+                stop=(a == 1),
+            )
+
+        def weigh(scaled, acc, jt, cols):
+            nc.scalar.activation(out=scaled[:, cols], in_=acc[:, cols], func=COPY, scale=wgo_cols[:, jt : jt + 1])
+
+        def turn(dst, scaled_tiles, r):
+            width = P * len(scaled_tiles)
+            turned = psum_tr.tile([P, HALF], F32, name="turned")
+            for i, scaled in enumerate(scaled_tiles):
+                nc.tensor.transpose(turned[:, i * P : (i + 1) * P], scaled[:, r * P : (r + 1) * P], ident[:])
+            nc.scalar.copy(dst, turned[:, 0:width])
+
+        def products(jts, h):
+            accs = [psum_mm.tile([P, HALF], F32, name="acc") for jt in jts]
+            for a in range(2):
+                for acc, jt in zip(accs, jts):
+                    mm_pass(acc, jt, h, a)
+            return accs
+
+        def scatter(page, dx_part, d_part, lo, hi):
+            nc.vector.tensor_tensor(page[:].indirect(offsets[:, lo // 16 : hi // 16]), dx_part, d_part, MULT)
+
+        whole = slice(0, QUART)
+        left, right = slice(0, P), slice(P, QUART)
+
+        wgo_turned = psum_tr.tile([P, HALF], F32, name="turned")
+        nc.tensor.transpose(wgo_turned[:, 0:P], wgo_rows[:], ident[:])
+        nc.scalar.activation(out=wgo_cols[:], in_=wgo_turned[:, 0 : J // P], func=COPY)
+
+        for c in range(2):
+            interleave(scopy, w8_bf[c][:], w8_raw[c][:])
+            quantize_w8(c)
+        interleave(scopy, dy_bf[0, 0][:], dy_raw[0, 0][:])
+        quantize_dy(0, 0, whole)
+        interleave(vcopy, dy_bf[0, 1][:, left, :], dy_raw[0, 1][:, :, left])
+        interleave(scopy, dy_bf[0, 1][:, right, :], dy_raw[0, 1][:, :, right])
+        quantize_dy(0, 1, left)
+        quantize_dy(0, 1, right)
+        for page in pages:
+            nc.vector.memset(page[:].bitcast(I32), 0)
+
+        for q in range(4):
+            jts = [2 * q, 2 * q + 1]
+            accs = products(jts, 0)
+            scaled_tiles = [ring.tile([P, HALF], F32, name="scaled") for jt in jts]
+            if q == 0:
+                for part in (slice(0, P), slice(P, HALF)):
+                    for scaled, acc, jt in zip(scaled_tiles, accs, jts):
+                        weigh(scaled, acc, jt, part)
+                    if part.start == 0:
+                        dx_lo[0, 0] = keep.tile([P, QUART], F32, name="dx_lo00")
+                        turn(dx_lo[0, 0][:], scaled_tiles, 0)
+                for r in range(1, 4):
+                    dx_lo[0, r] = keep.tile([P, QUART], F32, name="dx_lo0%d" % r)
+                    turn(dx_lo[0, r][:], scaled_tiles, r)
+                for a in range(2):
+                    interleave(vcopy, dy_bf[1, a][:], dy_raw[1, a][:])
+                    quantize_dy(1, a, whole)
+            else:
+                for scaled, acc, jt in zip(scaled_tiles, accs, jts):
+                    weigh(scaled, acc, jt, slice(0, HALF))
+                for r in range(4):
+                    tag = "dx_lo%d%d" % (q, r)
+                    if r < 2 and q < 3:
+                        interleave(scopy, dy_bf[q + 1, r][:], dy_raw[q + 1, r][:])
+                        quantize_dy(q + 1, r, whole)
+                        tag = "dy_raw%d%d" % (q + 1, r)
+                    elif q == 2:
+                        interleave(scopy, w8_bf[r][:], w8_raw[r][:])
+                        quantize_w8(r)
+                        tag = "w8_raw%d" % r
+                    dx_lo[q, r] = keep.tile([P, QUART], F32, name="dx_lo%d%d" % (q, r), tag=tag)
+                    turn(dx_lo[q, r][:], scaled_tiles, r)
+            for r in range(4):
+                if q == 0:
+                    d_part = d_first[:] if r == 0 else d_rest[:, r - 1, :]
+                else:
+                    d_part = d_q[q][:, r, :]
+                scatter(pages[r], dx_lo[q, r][:], d_part, q * QUART, (q + 1) * QUART)
+                if q == 3:
+                    nc.sync.dma_start(out=out[r * P : (r + 1) * P, :], in_=pages[r][:])
+
+        scaled_half = []
+        for u in range(2):
+            scaled_tiles = []
+            for pair in range(2):
+                jts = [4 * u + 2 * pair, 4 * u + 2 * pair + 1]
+                accs = products(jts, 1)
+                for acc, jt in zip(accs, jts):
+                    scaled = ring.tile([P, HALF], F32, name="scaled")
+                    weigh(scaled, acc, jt, slice(0, HALF))
+                    scaled_tiles.append(scaled)
+            scaled_half.append(scaled_tiles)
+        for r in range(4):
+            for u in range(2):
+                turn(dx_hi[r][:, u * HALF : (u + 1) * HALF], scaled_half[u], r)
+            page = pages[(4 + r) % PAGES]
+            scatter(page, dx_hi[r][:], d_hi[r][:], 0, J)
+            nc.sync.dma_start(out=out[(4 + r) * P : (5 + r) * P, :], in_=page[:])

@@ -23,7 +23,7 @@ PACK = 4
 K_PASS = P * PACK
 HALF = 512
 QUART = 256
-PAGES = 4
+PAGES = 5
 
 
 def interleave(engine_copy, grouped, raw):
@@ -40,34 +40,34 @@ def tile_list_embg_qf_mul_kernel(tc, dy, w8, w4_words, w4_scales, d, wgo, offs, 
 
     with ExitStack() as ctx:
         keep = ctx.enter_context(tc.tile_pool(name="keep", bufs=1))
-        ring = ctx.enter_context(tc.tile_pool(name="ring", bufs=10))
-        psum_mm = ctx.enter_context(tc.psum_pool(name="psum_mm", bufs=4))
-        psum_tr = ctx.enter_context(tc.psum_pool(name="psum_tr", bufs=4))
+        psum_mm = ctx.enter_context(tc.psum_pool(name="psum_mm", bufs=1))
+        psum_tr = ctx.enter_context(tc.psum_pool(name="psum_tr", bufs=1))
 
         offsets = keep.tile([P, J // 16], U16, name="offsets")
         w4_plane = keep.tile([P, N], U8, name="w4_plane", align_bytes=64)
         wgo_rows = keep.tile([P, P], F32, name="wgo_rows")
         wgo_cols = keep.tile([P, J // P], F32, name="wgo_cols")
         ident = keep.tile([P, P], F32, name="ident")
-        w8_raw = [keep.tile([P, PACK, QUART], F32, name="w8_raw%d" % c, tag="w8_raw%d" % c) for c in range(4)]
-        w8_bf = [keep.tile([P, QUART, PACK], BF16, name="w8_bf%d" % c, align_bytes=64) for c in range(4)]
-        w8_codes = [keep.tile([P, HALF], U32, name="w8_codes%d" % h, align_bytes=64) for h in range(2)]
+        w8_raw = [keep.tile([P, PACK, QUART], F32, name="w8_raw%d" % c, tag="w8_raw%d" % c, align_bytes=64) for c in range(4)]
+        w8_bf = [keep.tile([P, QUART, PACK], BF16, name="w8_bf%d" % c, align_bytes=64) for c in range(2)]
+        w8_codes = [keep.tile([P, HALF], U32, name="w8_codes0", align_bytes=64)]
         w8_plane = [keep.tile([P, HALF], U8, name="w8_plane%d" % h, align_bytes=64) for h in range(2)]
         w4_codes = [keep.tile([P, 2 * HALF], U8, name="w4_codes%d" % h, align_bytes=64) for h in range(2)]
         dy_raw, dy_bf, dy_codes, dy_plane = {}, {}, {}, {}
         for q in range(4):
             for a in range(2):
-                dy_raw[q, a] = keep.tile([P, PACK, QUART], F32, name="dy_raw%d%d" % (q, a), tag="dy_raw%d%d" % (q, a))
-                dy_bf[q, a] = keep.tile([P, QUART, PACK], BF16, name="dy_bf%d%d" % (q, a), align_bytes=64)
-                dy_codes[q, a] = keep.tile([P, QUART], U32, name="dy_codes%d%d" % (q, a), align_bytes=64)
+                dy_raw[q, a] = keep.tile([P, PACK, QUART], F32, name="dy_raw%d%d" % (q, a), tag="dy_raw%d%d" % (q, a), align_bytes=64)
+                if q < 2:
+                    dy_bf[q, a] = keep.tile([P, QUART, PACK], BF16, name="dy_bf%d%d" % (q, a), tag="dy_bf%d%d" % (q, a), align_bytes=64)
+                    dy_codes[q, a] = keep.tile([P, QUART], U32, name="dy_codes%d%d" % (q, a), align_bytes=64)
                 dy_plane[q, a] = keep.tile([P, QUART], U8, name="dy_plane%d%d" % (q, a), align_bytes=64)
-        d_first = keep.tile([P, QUART], F32, name="d_first")
+        d_first = keep.tile([P, QUART], F32, name="d_first", tag="d_first", align_bytes=64)
         d_rest = keep.tile([P, 3, QUART], F32, name="d_rest")
         d_q = [None] + [keep.tile([P, 4, QUART], F32, name="d_q%d" % q) for q in range(1, 4)]
         d_hi = [keep.tile([P, J], F32, name="d_hi%d" % r) for r in range(4)]
         dx_lo = {}
         dx_hi = [keep.tile([P, J], F32, name="dx_hi%d" % r) for r in range(4)]
-        pages = [keep.tile([P, T], F32, name="page%d" % i) for i in range(PAGES)]
+        pages = [keep.tile([P, T], F32, name="page%d" % i) for i in range(2)]
 
         def load_w8(c):
             nc.sync.dma_start(
@@ -90,22 +90,24 @@ def tile_list_embg_qf_mul_kernel(tc, dy, w8, w4_words, w4_scales, d, wgo, offs, 
         nc.vector.memset(w4_plane[:].bitcast(I32), 0)
         nc.vector.memset(wgo_rows[:], 0.0)
         make_identity(nc, ident[:])
+        for page in pages:
+            nc.vector.memset(page[:].bitcast(I32), 0)
 
         load_w8(0)
+        nc.sync.dma_start(out=wgo_rows[0 : J // P, :], in_=wgo[0].rearrange("(c p) -> c p", p=P))
         load_w8(1)
         for quad in range(4):
             nc.sync.dma_start(
                 out=w4_plane[32 * quad : 32 * quad + 4, :].bitcast(I32),
                 in_=w4_scales[0][4 * quad : 4 * quad + 4, :].bitcast(I32),
             )
-        nc.sync.dma_start(out=wgo_rows[0 : J // P, :], in_=wgo[0].rearrange("(c p) -> c p", p=P))
         load_dy(0, 0)
-        load_w4(0)
         load_dy(0, 1)
+        load_w4(0)
         nc.sync.dma_start(offsets[:], offs)
-        nc.sync.dma_start(out=d_first[:], in_=d[0:P, 0:QUART])
         load_dy(1, 0)
         load_dy(1, 1)
+        nc.sync.dma_start(out=d_first[:], in_=d[0:P, 0:QUART])
         load_d(d_rest, 1, 4, 0)
         load_dy(2, 0)
         load_dy(2, 1)
@@ -154,15 +156,15 @@ def tile_list_embg_qf_mul_kernel(tc, dy, w8, w4_words, w4_scales, d, wgo, offs, 
         def weigh(scaled, acc, jt, cols):
             nc.scalar.activation(out=scaled[:, cols], in_=acc[:, cols], func=COPY, scale=wgo_cols[:, jt : jt + 1])
 
-        def turn(dst, scaled_tiles, r):
+        def turn(scaled_tiles, r, bank):
             width = P * len(scaled_tiles)
-            turned = psum_tr.tile([P, HALF], F32, name="turned")
+            turned = psum_tr.tile([P, HALF], F32, name="turned%d" % bank)
             for i, scaled in enumerate(scaled_tiles):
                 nc.tensor.transpose(turned[:, i * P : (i + 1) * P], scaled[:, r * P : (r + 1) * P], ident[:])
-            nc.scalar.copy(dst, turned[:, 0:width])
+            return turned[:, 0:width]
 
         def products(jts, h):
-            accs = [psum_mm.tile([P, HALF], F32, name="acc") for jt in jts]
+            accs = [psum_mm.tile([P, HALF], F32, name="acc%d" % (jt % 2 if h == 0 and jt < 4 else (jt + 2 * h) % 4)) for jt in jts]
             for a in range(2):
                 for acc, jt in zip(accs, jts):
                     mm_pass(acc, jt, h, a)
@@ -171,65 +173,112 @@ def tile_list_embg_qf_mul_kernel(tc, dy, w8, w4_words, w4_scales, d, wgo, offs, 
         def scatter(page, dx_part, d_part, lo, hi):
             nc.vector.tensor_tensor(page[:].indirect(offsets[:, lo // 16 : hi // 16]), dx_part, d_part, MULT)
 
+        def late_page(tag):
+            page = keep.tile([P, T], F32, name="page%d" % len(pages), tag=tag, align_bytes=64)
+            nc.gpsimd.memset(page[:].bitcast(I32), 0)
+            pages.append(page)
+
         whole = slice(0, QUART)
         left, right = slice(0, P), slice(P, QUART)
 
-        wgo_turned = psum_tr.tile([P, HALF], F32, name="turned")
+        wgo_turned = psum_tr.tile([P, HALF], F32, name="turned3")
         nc.tensor.transpose(wgo_turned[:, 0:P], wgo_rows[:], ident[:])
         nc.scalar.activation(out=wgo_cols[:], in_=wgo_turned[:, 0 : J // P], func=COPY)
 
         for c in range(2):
             interleave(scopy, w8_bf[c][:], w8_raw[c][:])
             quantize_w8(c)
-        interleave(scopy, dy_bf[0, 0][:], dy_raw[0, 0][:])
+        interleave(vcopy, dy_bf[0, 0][:], dy_raw[0, 0][:])
         quantize_dy(0, 0, whole)
         interleave(vcopy, dy_bf[0, 1][:, left, :], dy_raw[0, 1][:, :, left])
         interleave(scopy, dy_bf[0, 1][:, right, :], dy_raw[0, 1][:, :, right])
         quantize_dy(0, 1, left)
         quantize_dy(0, 1, right)
-        for page in pages:
-            nc.vector.memset(page[:].bitcast(I32), 0)
 
+        def slot(shape, dtype, name, tag):
+            return keep.tile(shape, dtype, name=name, tag=tag, align_bytes=64)
+
+        dx_tag = {(0, 0): "dy_raw11", (1, 0): "dy_raw20", (1, 1): "dy_raw21", (1, 2): "dy_raw30", (1, 3): "dy_raw31",
+                  (2, 0): "w8_raw2", (2, 1): "w8_raw3"}
         for q in range(4):
+            for r in range(4):
+                dx_tag.setdefault((q, r), "dx_lo%d%d" % (q, r))
+
+        def late_dy(q, a, bf_tag, codes_tag):
+            dy_bf[q, a] = slot([P, QUART, PACK], BF16, "dy_bf%d%d" % (q, a), bf_tag)
+            dy_codes[q, a] = slot([P, QUART], U32, "dy_codes%d%d" % (q, a), codes_tag)
+            interleave(scopy, dy_bf[q, a][:], dy_raw[q, a][:])
+            quantize_dy(q, a, whole)
+
+        def late_w8(c):
+            w8_bf.append(slot([P, QUART, PACK], BF16, "w8_bf%d" % c, "scaled%d" % (c + 2)))
+            interleave(scopy, w8_bf[c][:], w8_raw[c][:])
+            quantize_w8(c)
+
+        def copy_out(q, r, turned):
+            dx_lo[q, r] = slot([P, QUART], F32, "dx_lo%d%d" % (q, r), dx_tag[q, r])
+            scopy(dx_lo[q, r][:], turned)
+
+        def place(q, r):
+            if q == 0:
+                d_part = d_first[:] if r == 0 else d_rest[:, r - 1, :]
+            else:
+                d_part = d_q[q][:, r, :]
+            scatter(pages[r], dx_lo[q, r][:], d_part, q * QUART, (q + 1) * QUART)
+
+        def weighed(q):
             jts = [2 * q, 2 * q + 1]
             accs = products(jts, 0)
-            scaled_tiles = [ring.tile([P, HALF], F32, name="scaled") for jt in jts]
-            if q == 0:
-                for part in (slice(0, P), slice(P, HALF)):
-                    for scaled, acc, jt in zip(scaled_tiles, accs, jts):
-                        weigh(scaled, acc, jt, part)
-                    if part.start == 0:
-                        dx_lo[0, 0] = keep.tile([P, QUART], F32, name="dx_lo00")
-                        turn(dx_lo[0, 0][:], scaled_tiles, 0)
-                for r in range(1, 4):
-                    dx_lo[0, r] = keep.tile([P, QUART], F32, name="dx_lo0%d" % r)
-                    turn(dx_lo[0, r][:], scaled_tiles, r)
-                for a in range(2):
-                    interleave(vcopy, dy_bf[1, a][:], dy_raw[1, a][:])
-                    quantize_dy(1, a, whole)
-            else:
-                for scaled, acc, jt in zip(scaled_tiles, accs, jts):
-                    weigh(scaled, acc, jt, slice(0, HALF))
-                for r in range(4):
-                    tag = "dx_lo%d%d" % (q, r)
-                    if r < 2 and q < 3:
-                        interleave(scopy, dy_bf[q + 1, r][:], dy_raw[q + 1, r][:])
-                        quantize_dy(q + 1, r, whole)
-                        tag = "dy_raw%d%d" % (q + 1, r)
-                    elif q == 2:
-                        interleave(scopy, w8_bf[r][:], w8_raw[r][:])
-                        quantize_w8(r)
-                        tag = "w8_raw%d" % r
-                    dx_lo[q, r] = keep.tile([P, QUART], F32, name="dx_lo%d%d" % (q, r), tag=tag)
-                    turn(dx_lo[q, r][:], scaled_tiles, r)
-            for r in range(4):
-                if q == 0:
-                    d_part = d_first[:] if r == 0 else d_rest[:, r - 1, :]
-                else:
-                    d_part = d_q[q][:, r, :]
-                scatter(pages[r], dx_lo[q, r][:], d_part, q * QUART, (q + 1) * QUART)
-                if q == 3:
-                    nc.sync.dma_start(out=out[r * P : (r + 1) * P, :], in_=pages[r][:])
+            tiles = [slot([P, HALF], F32, "scaled%d" % jt, "scaled%d" % jt) for jt in jts]
+            for scaled, acc, jt in zip(tiles, accs, jts):
+                weigh(scaled, acc, jt, slice(0, HALF))
+            return tiles
+
+        accs = products([0, 1], 0)
+        for a in range(2):
+            interleave(vcopy, dy_bf[1, a][:], dy_raw[1, a][:])
+            quantize_dy(1, a, whole)
+        late_page("dy_bf11")
+        scaled_tiles = [slot([P, HALF], F32, "scaled%d" % jt, "scaled%d" % jt) for jt in (0, 1)]
+        for part in (slice(0, P), slice(P, HALF)):
+            for jt in (0, 1):
+                weigh(scaled_tiles[jt], accs[jt], jt, part)
+            for r in range(part.start // P, part.stop // P):
+                copy_out(0, r, turn(scaled_tiles, r, 0))
+        place(0, 0)
+        late_page("d_first")
+        for r in range(1, 4):
+            place(0, r)
+
+        scaled_tiles = weighed(1)
+        turned = [turn(scaled_tiles, r, r) for r in range(4)]
+        for a in range(2):
+            late_dy(2, a, "scaled%d" % a, dx_tag[0, 2 + a])
+            copy_out(1, a, turned[a])
+        for a in range(2):
+            place(1, a)
+            late_dy(3, a, "scaled%d" % (2 + a), dx_tag[1, a])
+            copy_out(1, 2 + a, turned[2 + a])
+        for r in (2, 3):
+            place(1, r)
+
+        scaled_tiles = weighed(2)
+        turned = [turn(scaled_tiles, r, r) for r in range(4)]
+        w8_codes.append(slot([P, HALF], U32, "w8_codes1", dx_tag[1, 3]))
+        for r in range(4):
+            if r < 2:
+                late_w8(2 + r)
+            copy_out(2, r, turned[r])
+        late_page("scaled5")
+        for r in range(4):
+            place(2, r)
+
+        scaled_tiles = weighed(3)
+        for r in range(4):
+            copy_out(3, r, turn(scaled_tiles, r, r))
+        for r in range(4):
+            place(3, r)
+            nc.sync.dma_start(out=out[r * P : (r + 1) * P, :], in_=pages[r][:])
 
         scaled_half = []
         for u in range(2):
@@ -238,13 +287,13 @@ def tile_list_embg_qf_mul_kernel(tc, dy, w8, w4_words, w4_scales, d, wgo, offs, 
                 jts = [4 * u + 2 * pair, 4 * u + 2 * pair + 1]
                 accs = products(jts, 1)
                 for acc, jt in zip(accs, jts):
-                    scaled = ring.tile([P, HALF], F32, name="scaled")
+                    scaled = slot([P, HALF], F32, "scaled_hi%d" % jt, "scaled6" if jt == 0 else "scaled_hi%d" % jt)
                     weigh(scaled, acc, jt, slice(0, HALF))
                     scaled_tiles.append(scaled)
             scaled_half.append(scaled_tiles)
         for r in range(4):
             for u in range(2):
-                turn(dx_hi[r][:, u * HALF : (u + 1) * HALF], scaled_half[u], r)
+                scopy(dx_hi[r][:, u * HALF : (u + 1) * HALF], turn(scaled_half[u], r, (2 * r + u) % 4))
             page = pages[(4 + r) % PAGES]
             scatter(page, dx_hi[r][:], d_hi[r][:], 0, J)
             nc.sync.dma_start(out=out[(4 + r) * P : (5 + r) * P, :], in_=page[:])

@@ -48,8 +48,12 @@ def tile_list_embg_qf_mul_kernel(tc, dy, w8, w4_words, w4_scales, d, wgo, offs, 
         wgo_rows = keep.tile([P, P], F32, name="wgo_rows")
         wgo_cols = keep.tile([P, J // P], F32, name="wgo_cols")
         ident = keep.tile([P, P], F32, name="ident")
-        w8_raw = [keep.tile([P, PACK, QUART], F32, name="w8_raw%d" % c, tag="w8_raw%d" % c, align_bytes=64) for c in range(4)]
-        w8_bf = [keep.tile([P, QUART, PACK], BF16, name="w8_bf%d" % c, align_bytes=64) for c in range(2)]
+        w8_cols = [slice(0, 128), slice(128, 512), slice(512, 768), slice(768, 1024)]
+        w8_raw = [keep.tile([P, PACK, c.stop - c.start], F32, name="w8_raw%d" % i, tag="w8_raw%d" % i, align_bytes=64) for i, c in enumerate(w8_cols)]
+        w8_bf = [keep.tile([P, c.stop - c.start, PACK], BF16, name="w8_bf%d" % i, tag="w8_bf%d" % i, align_bytes=64) for i, c in enumerate(w8_cols[:2])]
+        lead_codes = [keep.tile([P, HALF], U32, name="lead_codes%d" % a, align_bytes=64) for a in range(2)]
+        lead_plane = [keep.tile([P, HALF], U8, name="lead_plane%d" % a, align_bytes=64) for a in range(2)]
+        wgo_first = keep.tile([P, QUART], F32, name="wgo_first")
         w8_codes = [keep.tile([P, HALF], U32, name="w8_codes0", align_bytes=64)]
         w8_plane = [keep.tile([P, HALF], U8, name="w8_plane%d" % h, align_bytes=64) for h in range(2)]
         w4_codes = [keep.tile([P, 2 * HALF], U8, name="w4_codes%d" % h, align_bytes=64) for h in range(2)]
@@ -59,8 +63,10 @@ def tile_list_embg_qf_mul_kernel(tc, dy, w8, w4_words, w4_scales, d, wgo, offs, 
                 dy_raw[q, a] = keep.tile([P, PACK, QUART], F32, name="dy_raw%d%d" % (q, a), tag="dy_raw%d%d" % (q, a), align_bytes=64)
                 if q < 2:
                     dy_bf[q, a] = keep.tile([P, QUART, PACK], BF16, name="dy_bf%d%d" % (q, a), tag="dy_bf%d%d" % (q, a), align_bytes=64)
-                    dy_codes[q, a] = keep.tile([P, QUART], U32, name="dy_codes%d%d" % (q, a), align_bytes=64)
-                dy_plane[q, a] = keep.tile([P, QUART], U8, name="dy_plane%d%d" % (q, a), align_bytes=64)
+                    dy_codes[q, a] = lead_codes[a][:, q * QUART : (q + 1) * QUART]
+                    dy_plane[q, a] = lead_plane[a][:, q * QUART : (q + 1) * QUART]
+                else:
+                    dy_plane[q, a] = keep.tile([P, QUART], U8, name="dy_plane%d%d" % (q, a), align_bytes=64)
         d_first = keep.tile([P, QUART], F32, name="d_first", tag="d_first", align_bytes=64)
         d_rest = keep.tile([P, 3, QUART], F32, name="d_rest")
         d_q = [None] + [keep.tile([P, 4, QUART], F32, name="d_q%d" % q) for q in range(1, 4)]
@@ -71,7 +77,7 @@ def tile_list_embg_qf_mul_kernel(tc, dy, w8, w4_words, w4_scales, d, wgo, offs, 
 
         def load_w8(c):
             nc.sync.dma_start(
-                out=w8_raw[c][:], in_=w8[:, c * QUART : (c + 1) * QUART].rearrange("(p t) n -> p t n", t=PACK)
+                out=w8_raw[c][:], in_=w8[:, w8_cols[c]].rearrange("(p t) n -> p t n", t=PACK)
             )
 
         def load_dy(q, a):
@@ -89,25 +95,29 @@ def tile_list_embg_qf_mul_kernel(tc, dy, w8, w4_words, w4_scales, d, wgo, offs, 
 
         nc.vector.memset(w4_plane[:].bitcast(I32), 0)
         nc.vector.memset(wgo_rows[:], 0.0)
+        for a in range(2):
+            nc.vector.memset(lead_codes[a][:, QUART:HALF], 0)
+            nc.vector.memset(lead_plane[a][:, QUART:HALF].bitcast(I32), 0)
         make_identity(nc, ident[:])
         for page in pages:
             nc.vector.memset(page[:].bitcast(I32), 0)
 
         load_w8(0)
-        nc.sync.dma_start(out=wgo_rows[0 : J // P, :], in_=wgo[0].rearrange("(c p) -> c p", p=P))
-        load_w8(1)
+        load_dy(0, 0)
         for quad in range(4):
             nc.sync.dma_start(
                 out=w4_plane[32 * quad : 32 * quad + 4, :].bitcast(I32),
                 in_=w4_scales[0][4 * quad : 4 * quad + 4, :].bitcast(I32),
             )
-        load_dy(0, 0)
         load_dy(0, 1)
         load_w4(0)
+        nc.sync.dma_start(out=wgo_rows[0 : J // P, :], in_=wgo[0].rearrange("(c p) -> c p", p=P))
+        load_w8(1)
+        nc.sync.dma_start(out=d_first[:], in_=d[0:P, 0:QUART])
+        nc.sync.dma_start(out=wgo_first[:], in_=wgo[:, 0:QUART])
         nc.sync.dma_start(offsets[:], offs)
         load_dy(1, 0)
         load_dy(1, 1)
-        nc.sync.dma_start(out=d_first[:], in_=d[0:P, 0:QUART])
         load_d(d_rest, 1, 4, 0)
         load_dy(2, 0)
         load_dy(2, 1)
@@ -122,12 +132,13 @@ def tile_list_embg_qf_mul_kernel(tc, dy, w8, w4_words, w4_scales, d, wgo, offs, 
         for r in range(4):
             nc.sync.dma_start(out=d_hi[r][:], in_=d[(4 + r) * P : (5 + r) * P, :])
 
-        def quantize_w8(c):
-            cols = slice((c % 2) * QUART, (c % 2 + 1) * QUART)
+        def quantize_w8(c, part):
+            h, base = divmod(w8_cols[c].start, HALF)
+            cols = slice(base + part.start, base + part.stop)
             nc.vector.quantize_mx(
-                out=w8_codes[c // 2][:, cols].bitcast(E4M3X4),
-                scales=w8_plane[c // 2][:, cols],
-                in_=w8_bf[c][:].rearrange("p n t -> p (n t)"),
+                out=w8_codes[h][:, cols].bitcast(E4M3X4),
+                scales=w8_plane[h][:, cols],
+                in_=w8_bf[c][:, part, :].rearrange("p n t -> p (n t)"),
             )
 
         def quantize_dy(q, a, cols):
@@ -137,7 +148,7 @@ def tile_list_embg_qf_mul_kernel(tc, dy, w8, w4_words, w4_scales, d, wgo, offs, 
                 in_=dy_bf[q, a][:, cols, :].rearrange("p j t -> p (j t)"),
             )
 
-        def mm_pass(acc, jt, h, a):
+        def mm_pass(acc, jt, h, a, first):
             q, cols = jt // 2, slice((jt % 2) * P, (jt % 2 + 1) * P)
             if a == 0:
                 rhs, rhs_scale = w8_codes[h][:].bitcast(E4M3X4), w8_plane[h][:]
@@ -149,8 +160,8 @@ def tile_list_embg_qf_mul_kernel(tc, dy, w8, w4_words, w4_scales, d, wgo, offs, 
                 lhsT_scale=dy_plane[q, a][:, cols],
                 rhs=rhs,
                 rhs_scale=rhs_scale,
-                start=(a == 0),
-                stop=(a == 1),
+                start=(a == first),
+                stop=(a != first),
             )
 
         def weigh(scaled, acc, jt, cols):
@@ -165,9 +176,10 @@ def tile_list_embg_qf_mul_kernel(tc, dy, w8, w4_words, w4_scales, d, wgo, offs, 
 
         def products(jts, h):
             accs = [psum_mm.tile([P, HALF], F32, name="acc%d" % (jt % 2 if h == 0 and jt < 4 else (jt + 2 * h) % 4)) for jt in jts]
-            for a in range(2):
+            first = 1 if jts[0] == 0 else 0
+            for a in (first, 1 - first):
                 for acc, jt in zip(accs, jts):
-                    mm_pass(acc, jt, h, a)
+                    mm_pass(acc, jt, h, a, first)
             return accs
 
         def scatter(page, dx_part, d_part, lo, hi):
@@ -179,26 +191,42 @@ def tile_list_embg_qf_mul_kernel(tc, dy, w8, w4_words, w4_scales, d, wgo, offs, 
             pages.append(page)
 
         whole = slice(0, QUART)
-        left, right = slice(0, P), slice(P, QUART)
+        left, right = slice(0, 160), slice(160, QUART)
+
+        interleave(scopy, w8_bf[0][:], w8_raw[0][:])
+        quantize_w8(0, slice(0, P))
+        interleave(vcopy, dy_bf[0, 0][:], dy_raw[0, 0][:])
+        quantize_dy(0, 0, whole)
+        interleave(vcopy, dy_bf[0, 1][:, left, :], dy_raw[0, 1][:, :, left])
+        interleave(scopy, dy_bf[0, 1][:, right, :], dy_raw[0, 1][:, :, right])
+        quantize_dy(0, 1, whole)
+        lead = psum_mm.tile([P, HALF], F32, name="acc2")
+        nc.tensor.matmul_mx(
+            out=lead[:], lhsT=w8_codes[0][:, 0:P].bitcast(E4M3X4), lhsT_scale=w8_plane[0][:, 0:P],
+            rhs=lead_codes[0][:].bitcast(E5M2X4), rhs_scale=lead_plane[0][:], start=True, stop=False,
+        )
+        nc.tensor.matmul_mx(
+            out=lead[:], lhsT=w4_codes[0][:, 0 : 2 * P].bitcast(E2M1X4), lhsT_scale=w4_plane[:, 0:P],
+            rhs=lead_codes[1][:].bitcast(E5M2X4), rhs_scale=lead_plane[1][:], start=False, stop=True,
+        )
+        parts = [(scopy, slice(0, P)), (vcopy, slice(P, 3 * P))]
+        for copy, part in parts:
+            interleave(copy, w8_bf[1][:, part, :], w8_raw[1][:, :, part])
+        for copy, part in parts:
+            quantize_w8(1, part)
+        late_page("w8_bf1")
+        dx_lo[0, 0] = keep.tile([P, QUART], F32, name="dx_lo00", tag="w8_raw1", align_bytes=64)
+        nc.vector.tensor_tensor(dx_lo[0, 0][:], lead[:, 0:QUART], d_first[:], MULT)
+        scatter(pages[0], dx_lo[0, 0][:], wgo_first[:], 0, QUART)
 
         wgo_turned = psum_tr.tile([P, HALF], F32, name="turned3")
         nc.tensor.transpose(wgo_turned[:, 0:P], wgo_rows[:], ident[:])
         nc.scalar.activation(out=wgo_cols[:], in_=wgo_turned[:, 0 : J // P], func=COPY)
 
-        for c in range(2):
-            interleave(scopy, w8_bf[c][:], w8_raw[c][:])
-            quantize_w8(c)
-        interleave(vcopy, dy_bf[0, 0][:], dy_raw[0, 0][:])
-        quantize_dy(0, 0, whole)
-        interleave(vcopy, dy_bf[0, 1][:, left, :], dy_raw[0, 1][:, :, left])
-        interleave(scopy, dy_bf[0, 1][:, right, :], dy_raw[0, 1][:, :, right])
-        quantize_dy(0, 1, left)
-        quantize_dy(0, 1, right)
-
         def slot(shape, dtype, name, tag):
             return keep.tile(shape, dtype, name=name, tag=tag, align_bytes=64)
 
-        dx_tag = {(0, 0): "dy_raw11", (1, 0): "dy_raw20", (1, 1): "dy_raw21", (1, 2): "dy_raw30", (1, 3): "dy_raw31",
+        dx_tag = {(0, 1): "dy_raw11", (1, 0): "dy_raw20", (1, 1): "dy_raw21", (1, 2): "dy_raw30", (1, 3): "dy_raw31",
                   (2, 0): "w8_raw2", (2, 1): "w8_raw3"}
         for q in range(4):
             for r in range(4):
@@ -213,7 +241,7 @@ def tile_list_embg_qf_mul_kernel(tc, dy, w8, w4_words, w4_scales, d, wgo, offs, 
         def late_w8(c):
             w8_bf.append(slot([P, QUART, PACK], BF16, "w8_bf%d" % c, "scaled%d" % (c + 2)))
             interleave(scopy, w8_bf[c][:], w8_raw[c][:])
-            quantize_w8(c)
+            quantize_w8(c, whole)
 
         def copy_out(q, r, turned):
             dx_lo[q, r] = slot([P, QUART], F32, "dx_lo%d%d" % (q, r), dx_tag[q, r])
@@ -221,7 +249,7 @@ def tile_list_embg_qf_mul_kernel(tc, dy, w8, w4_words, w4_scales, d, wgo, offs, 
 
         def place(q, r):
             if q == 0:
-                d_part = d_first[:] if r == 0 else d_rest[:, r - 1, :]
+                d_part = d_rest[:, r - 1, :]
             else:
                 d_part = d_q[q][:, r, :]
             scatter(pages[r], dx_lo[q, r][:], d_part, q * QUART, (q + 1) * QUART)
@@ -236,17 +264,15 @@ def tile_list_embg_qf_mul_kernel(tc, dy, w8, w4_words, w4_scales, d, wgo, offs, 
 
         accs = products([0, 1], 0)
         for a in range(2):
-            interleave(vcopy, dy_bf[1, a][:], dy_raw[1, a][:])
+            interleave(vcopy if a else scopy, dy_bf[1, a][:], dy_raw[1, a][:])
             quantize_dy(1, a, whole)
         late_page("dy_bf11")
         scaled_tiles = [slot([P, HALF], F32, "scaled%d" % jt, "scaled%d" % jt) for jt in (0, 1)]
-        for part in (slice(0, P), slice(P, HALF)):
+        for part in (slice(P, 2 * P), slice(2 * P, HALF)):
             for jt in (0, 1):
                 weigh(scaled_tiles[jt], accs[jt], jt, part)
             for r in range(part.start // P, part.stop // P):
                 copy_out(0, r, turn(scaled_tiles, r, 0))
-        place(0, 0)
-        late_page("d_first")
         for r in range(1, 4):
             place(0, r)
 

@@ -23,12 +23,13 @@ PACK = 4
 K_PASS = P * PACK
 HALF = 512
 QUART = 256
-PAGES = 5
+PAGES = 4
+W8, W4 = 0, 1
 
 
-def interleave(engine_copy, grouped, raw):
+def round_and_weave(engine_copy, woven, raw):
     engine_copy(
-        grouped.rearrange("p (c i) t -> p c t i", i=4),
+        woven.rearrange("p (c i) t -> p c t i", i=4),
         raw.rearrange("p t (c i) -> p c t i", i=4),
     )
 
@@ -40,286 +41,221 @@ def tile_list_embg_qf_mul_kernel(tc, dy, w8, w4_words, w4_scales, d, wgo, offs, 
 
     with ExitStack() as ctx:
         keep = ctx.enter_context(tc.tile_pool(name="keep", bufs=1))
-        psum_mm = ctx.enter_context(tc.psum_pool(name="psum_mm", bufs=1))
-        psum_tr = ctx.enter_context(tc.psum_pool(name="psum_tr", bufs=1))
+        psum = ctx.enter_context(tc.psum_pool(name="psum", bufs=1))
+
+        def slot(shape, dtype, name, tag=None):
+            return keep.tile(shape, dtype, name=name, tag=tag or name, align_bytes=64)
 
         offsets = keep.tile([P, J // 16], U16, name="offsets")
-        w4_plane = keep.tile([P, N], U8, name="w4_plane", align_bytes=64)
-        wgo_rows = keep.tile([P, P], F32, name="wgo_rows")
-        wgo_cols = keep.tile([P, J // P], F32, name="wgo_cols")
-        ident = keep.tile([P, P], F32, name="ident")
-        w8_cols = [slice(0, 128), slice(128, 512), slice(512, 768), slice(768, 1024)]
-        w8_raw = [keep.tile([P, PACK, c.stop - c.start], F32, name="w8_raw%d" % i, tag="w8_raw%d" % i, align_bytes=64) for i, c in enumerate(w8_cols)]
-        w8_bf = [keep.tile([P, c.stop - c.start, PACK], BF16, name="w8_bf%d" % i, tag="w8_bf%d" % i, align_bytes=64) for i, c in enumerate(w8_cols[:2])]
-        lead_codes = [keep.tile([P, HALF], U32, name="lead_codes%d" % a, align_bytes=64) for a in range(2)]
-        lead_plane = [keep.tile([P, HALF], U8, name="lead_plane%d" % a, align_bytes=64) for a in range(2)]
-        wgo_first = keep.tile([P, QUART], F32, name="wgo_first")
-        w8_codes = [keep.tile([P, HALF], U32, name="w8_codes0", align_bytes=64)]
-        w8_plane = [keep.tile([P, HALF], U8, name="w8_plane%d" % h, align_bytes=64) for h in range(2)]
-        w4_codes = [keep.tile([P, 2 * HALF], U8, name="w4_codes%d" % h, align_bytes=64) for h in range(2)]
-        dy_raw, dy_bf, dy_codes, dy_plane = {}, {}, {}, {}
-        for q in range(4):
-            for a in range(2):
-                dy_raw[q, a] = keep.tile([P, PACK, QUART], F32, name="dy_raw%d%d" % (q, a), tag="dy_raw%d%d" % (q, a), align_bytes=64)
-                if q < 2:
-                    dy_bf[q, a] = keep.tile([P, QUART, PACK], BF16, name="dy_bf%d%d" % (q, a), tag="dy_bf%d%d" % (q, a), align_bytes=64)
-                    dy_codes[q, a] = lead_codes[a][:, q * QUART : (q + 1) * QUART]
-                    dy_plane[q, a] = lead_plane[a][:, q * QUART : (q + 1) * QUART]
-                else:
-                    dy_plane[q, a] = keep.tile([P, QUART], U8, name="dy_plane%d%d" % (q, a), align_bytes=64)
-        d_first = keep.tile([P, QUART], F32, name="d_first", tag="d_first", align_bytes=64)
-        d_rest = keep.tile([P, 3, QUART], F32, name="d_rest")
-        d_q = [None] + [keep.tile([P, 4, QUART], F32, name="d_q%d" % q) for q in range(1, 4)]
-        d_hi = [keep.tile([P, J], F32, name="d_hi%d" % r) for r in range(4)]
-        dx_lo = {}
-        dx_hi = [keep.tile([P, J], F32, name="dx_hi%d" % r) for r in range(4)]
-        pages = [keep.tile([P, T], F32, name="page%d" % i) for i in range(2)]
+        w4_plane = slot([P, N], U8, "w4_plane")
+        w4_codes = [slot([P, 2 * HALF], U8, "w4_codes%d" % h) for h in range(2)]
+        w8_codes = [slot([P, HALF], U32, "w8_codes%d" % h) for h in range(2)]
+        w8_plane = [slot([P, HALF], U8, "w8_plane%d" % h) for h in range(2)]
+        dy_codes = {(a, q): slot([P, QUART], U32, "dy_codes%d%d" % (a, q)) for a in (W8, W4) for q in range(4)}
+        dy_plane = {(a, q): slot([P, QUART], U8, "dy_plane%d%d" % (a, q)) for a in (W8, W4) for q in range(4)}
+        wgo_rows = slot([P, P], F32, "wgo_rows")
+        wgo_cols = slot([P, J // P], F32, "wgo_cols")
+        ident = slot([P, P], F32, "ident")
+        pages = [slot([P, T], F32, "page%d" % i) for i in range(PAGES)]
 
-        def load_w8(c):
-            nc.sync.dma_start(
-                out=w8_raw[c][:], in_=w8[:, w8_cols[c]].rearrange("(p t) n -> p t n", t=PACK)
-            )
+        pieces = {}
+        for c in range(4):
+            h, cols = c // 2, slice((c % 2) * QUART, (c % 2 + 1) * QUART)
+            pieces["w", c] = (w8[:, c * QUART : (c + 1) * QUART], w8_codes[h][:, cols], w8_plane[h][:, cols], E4M3X4)
+        for a in (W8, W4):
+            rows = dy[a * K_PASS : (a + 1) * K_PASS, :]
+            for q in range(4):
+                pieces[a, q] = (rows[:, q * QUART : (q + 1) * QUART], dy_codes[a, q][:], dy_plane[a, q][:], E5M2X4)
+        for jt in range(2):
+            cols = slice(jt * P, (jt + 1) * P)
+            pieces["first", jt] = (dy[0:K_PASS, cols], dy_codes[W8, 0][:, cols], dy_plane[W8, 0][:, cols], E5M2X4)
+        raw, woven = {}, {}
 
-        def load_dy(q, a):
-            rows = dy[a * K_PASS : (a + 1) * K_PASS, q * QUART : (q + 1) * QUART]
-            nc.sync.dma_start(out=dy_raw[q, a][:], in_=rows.rearrange("(p t) j -> p t j", t=PACK))
+        def raw_tag(key):
+            return "raw_%s_%d" % key
+
+        def load_piece(key):
+            rows = pieces[key][0]
+            raw[key] = slot([P, PACK, rows.shape[1]], F32, raw_tag(key))
+            nc.sync.dma_start(out=raw[key][:], in_=rows.rearrange("(p t) c -> p t c", t=PACK))
+
+        def weave(key, engine_copy, tag=None):
+            woven[key] = slot([P, pieces[key][0].shape[1], PACK], BF16, "woven_%s_%d" % key, tag)
+            round_and_weave(engine_copy, woven[key][:], raw[key][:])
+
+        def quantize(key):
+            rows, codes, plane, fmt = pieces[key]
+            nc.vector.quantize_mx(out=codes.bitcast(fmt), scales=plane, in_=woven[key][:].rearrange("p c t -> p (c t)"))
 
         def load_w4(h):
             nc.sync.dma_start(
                 out=w4_codes[h][:].bitcast(I32), in_=w4_words[0][:, 2 * HALF * h : 2 * HALF * (h + 1)].bitcast(I32)
             )
 
-        def load_d(tile, r0, r1, q):
-            rows = d[r0 * P : r1 * P, q * QUART : (q + 1) * QUART]
-            nc.sync.dma_start(out=tile[:], in_=rows.rearrange("(r p) j -> p r j", p=P))
+        d_part = {}
+
+        def load_d(r0, r1, lo, hi):
+            tile = slot([P, r1 - r0, hi - lo], F32, "d_%d_%d" % (r0, lo))
+            nc.sync.dma_start(out=tile[:], in_=d[r0 * P : r1 * P, lo:hi].rearrange("(r p) j -> p r j", p=P))
+            for r in range(r0, r1):
+                d_part[r, lo] = tile[:, r - r0, :]
 
         nc.vector.memset(w4_plane[:].bitcast(I32), 0)
-        nc.vector.memset(wgo_rows[:], 0.0)
-        for a in range(2):
-            nc.vector.memset(lead_codes[a][:, QUART:HALF], 0)
-            nc.vector.memset(lead_plane[a][:, QUART:HALF].bitcast(I32), 0)
+        nc.gpsimd.memset(wgo_rows[:], 0.0)
         make_identity(nc, ident[:])
         for page in pages:
             nc.vector.memset(page[:].bitcast(I32), 0)
 
-        load_w8(0)
-        load_dy(0, 0)
+        load_piece(("w", 0))
         for quad in range(4):
             nc.sync.dma_start(
                 out=w4_plane[32 * quad : 32 * quad + 4, :].bitcast(I32),
                 in_=w4_scales[0][4 * quad : 4 * quad + 4, :].bitcast(I32),
             )
-        load_dy(0, 1)
         load_w4(0)
+        load_piece((W4, 0))
+        load_piece(("w", 1))
         nc.sync.dma_start(out=wgo_rows[0 : J // P, :], in_=wgo[0].rearrange("(c p) -> c p", p=P))
-        load_w8(1)
-        nc.sync.dma_start(out=d_first[:], in_=d[0:P, 0:QUART])
-        nc.sync.dma_start(out=wgo_first[:], in_=wgo[:, 0:QUART])
+        load_piece(("first", 0))
+        load_piece(("first", 1))
+        load_piece((W4, 1))
         nc.sync.dma_start(offsets[:], offs)
-        load_dy(1, 0)
-        load_dy(1, 1)
-        load_d(d_rest, 1, 4, 0)
-        load_dy(2, 0)
-        load_dy(2, 1)
-        load_d(d_q[1], 0, 4, 1)
-        load_dy(3, 0)
-        load_dy(3, 1)
-        load_w8(2)
-        load_w8(3)
-        load_d(d_q[2], 0, 4, 2)
+        load_d(0, 2, 0, QUART)
+        load_piece((W8, 1))
+        load_d(2, 4, 0, QUART)
+        for q in (2, 3):
+            load_piece((W4, q))
+            load_d(0, 4, (q - 1) * QUART, q * QUART)
+            load_piece((W8, q))
+        load_piece(("w", 2))
+        load_piece(("w", 3))
         load_w4(1)
-        load_d(d_q[3], 0, 4, 3)
-        for r in range(4):
-            nc.sync.dma_start(out=d_hi[r][:], in_=d[(4 + r) * P : (5 + r) * P, :])
+        load_d(0, 4, 3 * QUART, J)
+        for r in range(4, 8):
+            load_d(r, r + 1, 0, J)
 
-        def quantize_w8(c, part):
-            h, base = divmod(w8_cols[c].start, HALF)
-            cols = slice(base + part.start, base + part.stop)
-            nc.vector.quantize_mx(
-                out=w8_codes[h][:, cols].bitcast(E4M3X4),
-                scales=w8_plane[h][:, cols],
-                in_=w8_bf[c][:, part, :].rearrange("p n t -> p (n t)"),
-            )
-
-        def quantize_dy(q, a, cols):
-            nc.vector.quantize_mx(
-                out=dy_codes[q, a][:, cols].bitcast(E5M2X4),
-                scales=dy_plane[q, a][:, cols],
-                in_=dy_bf[q, a][:, cols, :].rearrange("p j t -> p (j t)"),
-            )
-
-        def mm_pass(acc, jt, h, a, first):
+        def mm_pass(acc, jt, h, a):
             q, cols = jt // 2, slice((jt % 2) * P, (jt % 2 + 1) * P)
-            if a == 0:
+            if a == W8:
                 rhs, rhs_scale = w8_codes[h][:].bitcast(E4M3X4), w8_plane[h][:]
             else:
                 rhs, rhs_scale = w4_codes[h][:].bitcast(E2M1X4), w4_plane[:, h * HALF : (h + 1) * HALF]
             nc.tensor.matmul_mx(
                 out=acc[:],
-                lhsT=dy_codes[q, a][:, cols].bitcast(E5M2X4),
-                lhsT_scale=dy_plane[q, a][:, cols],
+                lhsT=dy_codes[a, q][:, cols].bitcast(E5M2X4),
+                lhsT_scale=dy_plane[a, q][:, cols],
                 rhs=rhs,
                 rhs_scale=rhs_scale,
-                start=(a == first),
-                stop=(a != first),
+                start=(a == W4),
+                stop=(a == W8),
             )
+
+        def bank(b):
+            return psum.tile([P, HALF], F32, name="bank%d" % b)
+
+        def products(jts, h, banks):
+            accs = [bank(b) for b in banks]
+            for a in (W4, W8):
+                for acc, jt in zip(accs, jts):
+                    mm_pass(acc, jt, h, a)
+            return accs
 
         def weigh(scaled, acc, jt, cols):
             nc.scalar.activation(out=scaled[:, cols], in_=acc[:, cols], func=COPY, scale=wgo_cols[:, jt : jt + 1])
 
-        def turn(scaled_tiles, r, bank):
-            width = P * len(scaled_tiles)
-            turned = psum_tr.tile([P, HALF], F32, name="turned%d" % bank)
-            for i, scaled in enumerate(scaled_tiles):
-                nc.tensor.transpose(turned[:, i * P : (i + 1) * P], scaled[:, r * P : (r + 1) * P], ident[:])
-            return turned[:, 0:width]
+        def turn(scaled_tiles, rs, b):
+            turned = bank(b)
+            blocks = [scaled[:, r * P : (r + 1) * P] for r in rs for scaled in scaled_tiles]
+            for i, block in enumerate(blocks):
+                nc.tensor.transpose(turned[:, i * P : (i + 1) * P], block, ident[:])
+            return turned[:, 0 : P * len(blocks)]
 
-        def products(jts, h):
-            accs = [psum_mm.tile([P, HALF], F32, name="acc%d" % (jt % 2 if h == 0 and jt < 4 else (jt + 2 * h) % 4)) for jt in jts]
-            first = 1 if jts[0] == 0 else 0
-            for a in (first, 1 - first):
-                for acc, jt in zip(accs, jts):
-                    mm_pass(acc, jt, h, a, first)
-            return accs
+        def scatter(r, values, factors, lo, hi):
+            window = pages[r % PAGES][:].indirect(offsets[:, lo // 16 : hi // 16])
+            nc.vector.tensor_tensor(window, values, factors, MULT)
 
-        def scatter(page, dx_part, d_part, lo, hi):
-            nc.vector.tensor_tensor(page[:].indirect(offsets[:, lo // 16 : hi // 16]), dx_part, d_part, MULT)
+        def store(r):
+            nc.sync.dma_start(out=out[r * P : (r + 1) * P, :], in_=pages[r % PAGES][:])
 
-        def late_page(tag):
-            page = keep.tile([P, T], F32, name="page%d" % len(pages), tag=tag, align_bytes=64)
-            nc.gpsimd.memset(page[:].bitcast(I32), 0)
-            pages.append(page)
+        def place(dx, q, rs):
+            for i, r in enumerate(rs):
+                scatter(r, dx[:, i * QUART : (i + 1) * QUART], d_part[r, q * QUART], q * QUART, (q + 1) * QUART)
+                if q == 3:
+                    store(r)
 
-        whole = slice(0, QUART)
-        left, right = slice(0, 160), slice(160, QUART)
+        def prepare(key, tag):
+            weave(key, scopy, tag)
+            quantize(key)
 
-        interleave(scopy, w8_bf[0][:], w8_raw[0][:])
-        quantize_w8(0, slice(0, P))
-        interleave(vcopy, dy_bf[0, 0][:], dy_raw[0, 0][:])
-        quantize_dy(0, 0, whole)
-        interleave(vcopy, dy_bf[0, 1][:, left, :], dy_raw[0, 1][:, :, left])
-        interleave(scopy, dy_bf[0, 1][:, right, :], dy_raw[0, 1][:, :, right])
-        quantize_dy(0, 1, whole)
-        lead = psum_mm.tile([P, HALF], F32, name="acc2")
-        nc.tensor.matmul_mx(
-            out=lead[:], lhsT=w8_codes[0][:, 0:P].bitcast(E4M3X4), lhsT_scale=w8_plane[0][:, 0:P],
-            rhs=lead_codes[0][:].bitcast(E5M2X4), rhs_scale=lead_plane[0][:], start=True, stop=False,
-        )
-        nc.tensor.matmul_mx(
-            out=lead[:], lhsT=w4_codes[0][:, 0 : 2 * P].bitcast(E2M1X4), lhsT_scale=w4_plane[:, 0:P],
-            rhs=lead_codes[1][:].bitcast(E5M2X4), rhs_scale=lead_plane[1][:], start=False, stop=True,
-        )
-        parts = [(scopy, slice(0, P)), (vcopy, slice(P, 3 * P))]
-        for copy, part in parts:
-            interleave(copy, w8_bf[1][:, part, :], w8_raw[1][:, :, part])
-        for copy, part in parts:
-            quantize_w8(1, part)
-        late_page("w8_bf1")
-        dx_lo[0, 0] = keep.tile([P, QUART], F32, name="dx_lo00", tag="w8_raw1", align_bytes=64)
-        nc.vector.tensor_tensor(dx_lo[0, 0][:], lead[:, 0:QUART], d_first[:], MULT)
-        scatter(pages[0], dx_lo[0, 0][:], wgo_first[:], 0, QUART)
-
-        wgo_turned = psum_tr.tile([P, HALF], F32, name="turned3")
+        for key in (("w", 0), (W4, 0)):
+            prepare(key, None)
+        wgo_turned = bank(7)
         nc.tensor.transpose(wgo_turned[:, 0:P], wgo_rows[:], ident[:])
-        nc.scalar.activation(out=wgo_cols[:], in_=wgo_turned[:, 0 : J // P], func=COPY)
+        scopy(wgo_cols[:], wgo_turned[:, 0 : J // P])
+        weave(("w", 1), vcopy)
+        quantize(("w", 1))
+        for jt in range(2):
+            prepare(("first", jt), None)
+        accs = products([0, 1], 0, [0, 1])
+        weave((W4, 1), vcopy)
+        quantize((W4, 1))
 
-        def slot(shape, dtype, name, tag):
-            return keep.tile(shape, dtype, name=name, tag=tag, align_bytes=64)
+        def scaled_tiles(q):
+            return [slot([P, HALF], F32, "scaled%d" % jt) for jt in (2 * q, 2 * q + 1)]
 
-        dx_tag = {(0, 1): "dy_raw11", (1, 0): "dy_raw20", (1, 1): "dy_raw21", (1, 2): "dy_raw30", (1, 3): "dy_raw31",
-                  (2, 0): "w8_raw2", (2, 1): "w8_raw3"}
-        for q in range(4):
-            for r in range(4):
-                dx_tag.setdefault((q, r), "dx_lo%d%d" % (q, r))
+        scaled = scaled_tiles(0)
+        dx = [slot([P, QUART], F32, "dx0_%d" % r) for r in range(2)]
+        for jt in range(2):
+            weigh(scaled[jt], accs[jt], jt, slice(0, P))
+        scopy(dx[0][:], turn(scaled, [0], 2))
+        place(dx[0], 0, [0])
+        for jt in range(2):
+            weigh(scaled[jt], accs[jt], jt, slice(P, HALF))
+        turned = [turn(scaled, [1], 3), turn(scaled, [2, 3], 4)]
+        scopy(dx[1][:], turned[0])
+        place(dx[1], 0, [1])
+        prepare((W8, 1), "scaled1")
+        rest = slot([P, HALF], F32, "dx0_rest", raw_tag((W8, 1)))
+        scopy(rest[:], turned[1])
+        place(rest, 0, [2, 3])
+        prepare((W4, 2), "scaled1")
 
-        def late_dy(q, a, bf_tag, codes_tag):
-            dy_bf[q, a] = slot([P, QUART, PACK], BF16, "dy_bf%d%d" % (q, a), bf_tag)
-            dy_codes[q, a] = slot([P, QUART], U32, "dy_codes%d%d" % (q, a), codes_tag)
-            interleave(scopy, dy_bf[q, a][:], dy_raw[q, a][:])
-            quantize_dy(q, a, whole)
-
-        def late_w8(c):
-            w8_bf.append(slot([P, QUART, PACK], BF16, "w8_bf%d" % c, "scaled%d" % (c + 2)))
-            interleave(scopy, w8_bf[c][:], w8_raw[c][:])
-            quantize_w8(c, whole)
-
-        def copy_out(q, r, turned):
-            dx_lo[q, r] = slot([P, QUART], F32, "dx_lo%d%d" % (q, r), dx_tag[q, r])
-            scopy(dx_lo[q, r][:], turned)
-
-        def place(q, r):
-            if q == 0:
-                d_part = d_rest[:, r - 1, :]
-            else:
-                d_part = d_q[q][:, r, :]
-            scatter(pages[r], dx_lo[q, r][:], d_part, q * QUART, (q + 1) * QUART)
-
-        def weighed(q):
+        early = {1: [(W8, 2)], 2: [(W8, 3), ("w", 2)], 3: []}
+        late = {1: [(W4, 3)], 2: [("w", 3)], 3: []}
+        for q in (1, 2, 3):
             jts = [2 * q, 2 * q + 1]
-            accs = products(jts, 0)
-            tiles = [slot([P, HALF], F32, "scaled%d" % jt, "scaled%d" % jt) for jt in jts]
-            for scaled, acc, jt in zip(tiles, accs, jts):
-                weigh(scaled, acc, jt, slice(0, HALF))
-            return tiles
+            mine, other = 2 * (q % 2), 2 - 2 * (q % 2)
+            accs = products(jts, 0, [mine, mine + 1])
+            scaled = scaled_tiles(q)
+            for jt in jts:
+                weigh(scaled[jt % 2], accs[jt % 2], jt, slice(0, HALF))
+            turned = [turn(scaled, [r], b) for r, b in enumerate((other, other + 1, 4, 5))]
+            first = slot([P, QUART], F32, "dx%d_first" % q)
+            scopy(first[:], turned[0])
+            place(first, q, [0])
+            for key, jt in zip(early[q], jts):
+                prepare(key, "scaled%d" % jt)
+            rest = slot([P, 3 * QUART], F32, "dx%d_rest" % q, raw_tag(early[q][-1]) if early[q] else None)
+            for r in (1, 2, 3):
+                scopy(rest[:, (r - 1) * QUART : r * QUART], turned[r])
+            place(rest, q, [1, 2, 3])
+            for key in late[q]:
+                prepare(key, "scaled%d" % jts[len(early[q]) - 1])
 
-        accs = products([0, 1], 0)
-        for a in range(2):
-            interleave(vcopy if a else scopy, dy_bf[1, a][:], dy_raw[1, a][:])
-            quantize_dy(1, a, whole)
-        late_page("dy_bf11")
-        scaled_tiles = [slot([P, HALF], F32, "scaled%d" % jt, "scaled%d" % jt) for jt in (0, 1)]
-        for part in (slice(P, 2 * P), slice(2 * P, HALF)):
-            for jt in (0, 1):
-                weigh(scaled_tiles[jt], accs[jt], jt, part)
-            for r in range(part.start // P, part.stop // P):
-                copy_out(0, r, turn(scaled_tiles, r, 0))
-        for r in range(1, 4):
-            place(0, r)
-
-        scaled_tiles = weighed(1)
-        turned = [turn(scaled_tiles, r, r) for r in range(4)]
-        for a in range(2):
-            late_dy(2, a, "scaled%d" % a, dx_tag[0, 2 + a])
-            copy_out(1, a, turned[a])
-        for a in range(2):
-            place(1, a)
-            late_dy(3, a, "scaled%d" % (2 + a), dx_tag[1, a])
-            copy_out(1, 2 + a, turned[2 + a])
-        for r in (2, 3):
-            place(1, r)
-
-        scaled_tiles = weighed(2)
-        turned = [turn(scaled_tiles, r, r) for r in range(4)]
-        w8_codes.append(slot([P, HALF], U32, "w8_codes1", dx_tag[1, 3]))
-        for r in range(4):
-            if r < 2:
-                late_w8(2 + r)
-            copy_out(2, r, turned[r])
-        late_page("scaled5")
-        for r in range(4):
-            place(2, r)
-
-        scaled_tiles = weighed(3)
-        for r in range(4):
-            copy_out(3, r, turn(scaled_tiles, r, r))
-        for r in range(4):
-            place(3, r)
-            nc.sync.dma_start(out=out[r * P : (r + 1) * P, :], in_=pages[r][:])
-
-        scaled_half = []
+        scaled = []
+        dx_hi = [slot([P, J], F32, "dx_hi%d" % r) for r in range(4)]
         for u in range(2):
-            scaled_tiles = []
-            for pair in range(2):
-                jts = [4 * u + 2 * pair, 4 * u + 2 * pair + 1]
-                accs = products(jts, 1)
-                for acc, jt in zip(accs, jts):
-                    scaled = slot([P, HALF], F32, "scaled_hi%d" % jt, "scaled6" if jt == 0 else "scaled_hi%d" % jt)
-                    weigh(scaled, acc, jt, slice(0, HALF))
-                    scaled_tiles.append(scaled)
-            scaled_half.append(scaled_tiles)
-        for r in range(4):
+            jts = list(range(4 * u, 4 * u + 4))
+            accs = products(jts, 1, [0, 1, 4, 5])
+            scaled.append([slot([P, HALF], F32, "scaled_hi%d" % jt) for jt in jts])
+            for tile, acc, jt in zip(scaled[u], accs, jts):
+                weigh(tile, acc, jt, slice(0, HALF))
+            cols = slice(u * HALF, (u + 1) * HALF)
+            scopy(dx_hi[0][:, cols], turn(scaled[u], [0], 2 + u))
+            scatter(4, dx_hi[0][:, cols], d_part[4, 0][:, cols], cols.start, cols.stop)
+        store(4)
+        for r in range(1, 4):
             for u in range(2):
-                scopy(dx_hi[r][:, u * HALF : (u + 1) * HALF], turn(scaled_half[u], r, (2 * r + u) % 4))
-            page = pages[(4 + r) % PAGES]
-            scatter(page, dx_hi[r][:], d_hi[r][:], 0, J)
-            nc.sync.dma_start(out=out[(4 + r) * P : (5 + r) * P, :], in_=page[:])
+                scopy(dx_hi[r][:, u * HALF : (u + 1) * HALF], turn(scaled[u], [r], (2, 3, 6, 7)[(2 * r + u) % 4]))
+            scatter(4 + r, dx_hi[r][:], d_part[4 + r, 0], 0, J)
+            store(4 + r)

@@ -106,31 +106,32 @@ def tile_list_embg_qf_mul_kernel(tc, dy, w8, w4_words, w4_scales, d, wgo, offs, 
         for page in pages:
             nc.vector.memset(page[:].bitcast(I32), 0)
 
-        load_piece(("w", 0))
+        load_piece((W4, 0))
         for quad in range(4):
             nc.sync.dma_start(
                 out=w4_plane[32 * quad : 32 * quad + 4, :].bitcast(I32),
                 in_=w4_scales[0][4 * quad : 4 * quad + 4, :].bitcast(I32),
             )
         load_w4(0)
-        load_piece((W4, 0))
+        load_piece(("w", 0))
         load_piece(("w", 1))
         nc.sync.dma_start(out=wgo_rows[0 : J // P, :], in_=wgo[0].rearrange("(c p) -> c p", p=P))
         load_piece(("first", 0))
         load_piece(("first", 1))
         load_piece((W4, 1))
+        load_piece((W8, 1))
         nc.sync.dma_start(offsets[:], offs)
         load_d(0, 2, 0, QUART)
-        load_piece((W8, 1))
         load_d(2, 4, 0, QUART)
-        for q in (2, 3):
-            load_piece((W4, q))
-            load_d(0, 4, (q - 1) * QUART, q * QUART)
-            load_piece((W8, q))
+        load_piece((W4, 2))
+        load_piece((W8, 2))
+        load_d(0, 4, QUART, HALF)
+        load_piece((W4, 3))
+        load_piece((W8, 3))
+        load_d(0, 4, HALF, J)
         load_piece(("w", 2))
         load_piece(("w", 3))
         load_w4(1)
-        load_d(0, 4, 3 * QUART, J)
         for r in range(4, 8):
             load_d(r, r + 1, 0, J)
 
@@ -160,8 +161,17 @@ def tile_list_embg_qf_mul_kernel(tc, dy, w8, w4_words, w4_scales, d, wgo, offs, 
                     mm_pass(acc, jt, h, a)
             return accs
 
-        def weigh(scaled, acc, jt, cols):
-            nc.scalar.activation(out=scaled[:, cols], in_=acc[:, cols], func=COPY, scale=wgo_cols[:, jt : jt + 1])
+        def weigh(q, accs, lo, hi, room=None):
+            tiles = []
+            for i, acc in enumerate(accs):
+                jt, width = 2 * q + i, hi - lo
+                if room is None:
+                    tile = slot([P, width], F32, "scaled%d_%d_%d" % (len(accs), jt, lo))
+                    tiles.append(tile[:])
+                else:
+                    tiles.append(room[:, i * width : (i + 1) * width])
+                nc.scalar.activation(out=tiles[i], in_=acc[:, lo:hi], func=COPY, scale=wgo_cols[:, jt : jt + 1])
+            return tiles
 
         def turn(scaled_tiles, rs, b):
             turned = bank(b)
@@ -170,92 +180,82 @@ def tile_list_embg_qf_mul_kernel(tc, dy, w8, w4_words, w4_scales, d, wgo, offs, 
                 nc.tensor.transpose(turned[:, i * P : (i + 1) * P], block, ident[:])
             return turned[:, 0 : P * len(blocks)]
 
+        def copy_out(turned, name, tag=None):
+            dx = slot([P, turned.shape[1]], F32, name, tag)
+            scopy(dx[:], turned)
+            return dx
+
         def scatter(r, values, factors, lo, hi):
             window = pages[r % PAGES][:].indirect(offsets[:, lo // 16 : hi // 16])
             nc.vector.tensor_tensor(window, values, factors, MULT)
-
-        def store(r):
-            nc.sync.dma_start(out=out[r * P : (r + 1) * P, :], in_=pages[r % PAGES][:])
+            if hi == J:
+                nc.sync.dma_start(out=out[r * P : (r + 1) * P, :], in_=pages[r % PAGES][:])
 
         def place(dx, q, rs):
             for i, r in enumerate(rs):
-                scatter(r, dx[:, i * QUART : (i + 1) * QUART], d_part[r, q * QUART], q * QUART, (q + 1) * QUART)
-                if q == 3:
-                    store(r)
+                if q < 2:
+                    factors = d_part[r, q * QUART]
+                else:
+                    factors = d_part[r, HALF][:, (q - 2) * QUART : (q - 1) * QUART]
+                scatter(r, dx[:, i * QUART : (i + 1) * QUART], factors, q * QUART, (q + 1) * QUART)
 
-        def prepare(key, tag):
+        def prepare(key, tag=None):
             weave(key, scopy, tag)
             quantize(key)
 
-        for key in (("w", 0), (W4, 0)):
-            prepare(key, None)
+        prepare((W4, 0))
+        weave(("w", 0), scopy)
+        weave(("w", 1), vcopy)
+        quantize(("w", 0))
+        quantize(("w", 1))
+        for jt in range(2):
+            prepare(("first", jt))
         wgo_turned = bank(7)
         nc.tensor.transpose(wgo_turned[:, 0:P], wgo_rows[:], ident[:])
         scopy(wgo_cols[:], wgo_turned[:, 0 : J // P])
-        weave(("w", 1), vcopy)
-        quantize(("w", 1))
-        for jt in range(2):
-            prepare(("first", jt), None)
         accs = products([0, 1], 0, [0, 1])
-        weave((W4, 1), vcopy)
-        quantize((W4, 1))
+        for a in (W4, W8):
+            weave((a, 1), vcopy)
+            quantize((a, 1))
 
-        def scaled_tiles(q):
-            return [slot([P, HALF], F32, "scaled%d" % jt) for jt in (2 * q, 2 * q + 1)]
+        for r in range(2):
+            place(copy_out(turn(weigh(0, accs, r * P, (r + 1) * P), [0], 4 + r), "dx0_%d" % r), 0, [r])
+        place(copy_out(turn(weigh(0, accs, QUART, HALF), [0, 1], 6), "dx0_2"), 0, [2, 3])
+        prepare((W4, 2), "scaled2_0_256")
+        accs = products([2, 3], 0, [4, 5])
+        scaled = weigh(1, accs, 0, HALF)
+        prepare((W8, 2), "scaled2_1_256")
 
-        scaled = scaled_tiles(0)
-        dx = [slot([P, QUART], F32, "dx0_%d" % r) for r in range(2)]
-        for jt in range(2):
-            weigh(scaled[jt], accs[jt], jt, slice(0, P))
-        scopy(dx[0][:], turn(scaled, [0], 2))
-        place(dx[0], 0, [0])
-        for jt in range(2):
-            weigh(scaled[jt], accs[jt], jt, slice(P, HALF))
-        turned = [turn(scaled, [1], 3), turn(scaled, [2, 3], 4)]
-        scopy(dx[1][:], turned[0])
-        place(dx[1], 0, [1])
-        prepare((W8, 1), "scaled1")
-        rest = slot([P, HALF], F32, "dx0_rest", raw_tag((W8, 1)))
-        scopy(rest[:], turned[1])
-        place(rest, 0, [2, 3])
-        prepare((W4, 2), "scaled1")
+        turned = [turn(scaled, [0], 0), turn(scaled, [1], 1), turn(scaled, [2, 3], 2)]
+        for r in range(2):
+            place(copy_out(turned[r], "dx1_%d" % r, raw_tag(((W8, W4)[r], 2))), 1, [r])
+        prepare((W4, 3), "scaled2_2_0")
+        prepare((W8, 3), "scaled2_3_0")
+        rooms = {2: slot([P, 3 * HALF], F32, "room2", raw_tag((W8, 3)))}
+        scopy(rooms[2][:, J : J + HALF], turned[2])
+        place(rooms[2][:, J : J + HALF], 1, [2, 3])
 
-        early = {1: [(W8, 2)], 2: [(W8, 3), ("w", 2)], 3: []}
-        late = {1: [(W4, 3)], 2: [("w", 3)], 3: []}
-        for q in (1, 2, 3):
-            jts = [2 * q, 2 * q + 1]
-            mine, other = 2 * (q % 2), 2 - 2 * (q % 2)
-            accs = products(jts, 0, [mine, mine + 1])
-            scaled = scaled_tiles(q)
-            for jt in jts:
-                weigh(scaled[jt % 2], accs[jt % 2], jt, slice(0, HALF))
-            turned = [turn(scaled, [r], b) for r, b in enumerate((other, other + 1, 4, 5))]
-            first = slot([P, QUART], F32, "dx%d_first" % q)
-            scopy(first[:], turned[0])
-            place(first, q, [0])
-            for key, jt in zip(early[q], jts):
-                prepare(key, "scaled%d" % jt)
-            rest = slot([P, 3 * QUART], F32, "dx%d_rest" % q, raw_tag(early[q][-1]) if early[q] else None)
-            for r in (1, 2, 3):
-                scopy(rest[:, (r - 1) * QUART : r * QUART], turned[r])
-            place(rest, q, [1, 2, 3])
-            for key in late[q]:
-                prepare(key, "scaled%d" % jts[len(early[q]) - 1])
+        late = []
+        for q, sums, turns in ((2, [0, 1], [3, 4]), (3, [3, 4], [5, 6])):
+            accs = products([2 * q, 2 * q + 1], 0, sums)
+            scaled = weigh(q, accs, 0, QUART, rooms[q][:, 0:HALF])
+            turned = [turn(scaled, [r], turns[r]) for r in range(2)]
+            late.extend(weigh(q, accs, QUART, HALF, rooms[q][:, HALF:J]))
+            for r in range(2):
+                place(copy_out(turned[r], "dx%d_%d" % (q, r)), q, [r])
+            if q == 2:
+                prepare(("w", 2), "scaled2_2_0")
+                prepare(("w", 3), "scaled2_3_0")
+                rooms[3] = slot([P, J], F32, "room3", raw_tag(("w", 3)))
+        for r, b in ((2, 7), (3, 2)):
+            dx = copy_out(turn(late, [r - 2], b), "dx_late%d" % r)
+            scatter(r, dx[:], d_part[r, HALF], HALF, J)
 
         scaled = []
-        dx_hi = [slot([P, J], F32, "dx_hi%d" % r) for r in range(4)]
         for u in range(2):
-            jts = list(range(4 * u, 4 * u + 4))
-            accs = products(jts, 1, [0, 1, 4, 5])
-            scaled.append([slot([P, HALF], F32, "scaled_hi%d" % jt) for jt in jts])
-            for tile, acc, jt in zip(scaled[u], accs, jts):
-                weigh(tile, acc, jt, slice(0, HALF))
-            cols = slice(u * HALF, (u + 1) * HALF)
-            scopy(dx_hi[0][:, cols], turn(scaled[u], [0], 2 + u))
-            scatter(4, dx_hi[0][:, cols], d_part[4, 0][:, cols], cols.start, cols.stop)
-        store(4)
-        for r in range(1, 4):
+            scaled.append(weigh(2 * u, products(list(range(4 * u, 4 * u + 4)), 1, [5, 6, 7, 2]), 0, HALF))
+        for r in range(4):
+            dx = slot([P, J], F32, "dx_hi%d" % r)
             for u in range(2):
-                scopy(dx_hi[r][:, u * HALF : (u + 1) * HALF], turn(scaled[u], [r], (2, 3, 6, 7)[(2 * r + u) % 4]))
-            scatter(4 + r, dx_hi[r][:], d_part[4 + r, 0], 0, J)
-            store(4 + r)
+                scopy(dx[:, u * HALF : (u + 1) * HALF], turn(scaled[u], [r], (0, 1, 3, 4)[(2 * r + u) % 4]))
+            scatter(4 + r, dx[:], d_part[4 + r, 0], 0, J)

@@ -56,7 +56,7 @@ def tile_list_embg_qf_mul_kernel(tc, dy, w8, w4_words, w4_scales, d, wgo, offs, 
         wgo_rows = slot([P, P], F32, "wgo_rows")
         wgo_cols = slot([P, J // P], F32, "wgo_cols")
         ident = slot([P, P], F32, "ident")
-        pages = [slot([P, T], F32, "page%d" % i) for i in range(PAGES)]
+        pages = [slot([P, T], F32, "page%d" % i) for i in range(2)]
 
         pieces = {}
         for c in range(4):
@@ -218,8 +218,14 @@ def tile_list_embg_qf_mul_kernel(tc, dy, w8, w4_words, w4_scales, d, wgo, offs, 
             weave((a, 1), vcopy)
             quantize((a, 1))
 
+        def late_page(tag):
+            pages.append(slot([P, T], F32, "page%d" % len(pages), tag))
+            nc.gpsimd.memset(pages[-1][:].bitcast(I32), 0)
+
+        late_page("woven_%s_%d" % (W8, 1))
         for r in range(2):
             place(copy_out(turn(weigh(0, accs, r * P, (r + 1) * P), [0], 4 + r), "dx0_%d" % r), 0, [r])
+        late_page("dx0_0")
         place(copy_out(turn(weigh(0, accs, QUART, HALF), [0, 1], 6), "dx0_2"), 0, [2, 3])
         prepare((W4, 2), "scaled2_0_256")
         accs = products([2, 3], 0, [4, 5])

@@ -54,7 +54,6 @@ def tile_list_embg_qf_mul_kernel(tc, dy, w8, w4_words, w4_scales, d, wgo, offs, 
         dy_codes = {(a, q): slot([P, QUART], U32, "dy_codes%d%d" % (a, q)) for a in (W8, W4) for q in range(4)}
         dy_plane = {(a, q): slot([P, QUART], U8, "dy_plane%d%d" % (a, q)) for a in (W8, W4) for q in range(4)}
         wgo_rows = slot([P, P], F32, "wgo_rows")
-        wgo_cols = slot([P, J // P], F32, "wgo_cols")
         ident = slot([P, P], F32, "ident")
         pages = [slot([P, T], F32, "page%d" % i) for i in range(2)]
 
@@ -203,15 +202,25 @@ def tile_list_embg_qf_mul_kernel(tc, dy, w8, w4_words, w4_scales, d, wgo, offs, 
             weave(key, scopy, tag)
             quantize(key)
 
+        def weave_shared(key):
+            width = pieces[key][0].shape[1]
+            split = 3 * width // 8
+            woven[key] = slot([P, width, PACK], BF16, "woven_%s_%d" % key)
+            for engine_copy, cols in ((scopy, slice(0, split)), (vcopy, slice(split, width))):
+                round_and_weave(engine_copy, woven[key][:, cols, :], raw[key][:, :, cols])
+
         prepare((W4, 0))
         weave(("w", 0), scopy)
-        weave(("w", 1), vcopy)
+        weave_shared(("w", 1))
         quantize(("w", 0))
         quantize(("w", 1))
+        weave(("first", 0), scopy)
+        weave_shared(("first", 1))
         for jt in range(2):
-            prepare(("first", jt))
+            quantize(("first", jt))
         wgo_turned = bank(7)
         nc.tensor.transpose(wgo_turned[:, 0:P], wgo_rows[:], ident[:])
+        wgo_cols = slot([P, J // P], F32, "wgo_cols", raw_tag(("first", 1)))
         scopy(wgo_cols[:], wgo_turned[:, 0 : J // P])
         accs = products([0, 1], 0, [0, 1])
         for a in (W4, W8):

@@ -1,7 +1,6 @@
 from contextlib import ExitStack
 
 import concourse.mybir as mybir
-from concourse.masks import make_identity
 
 K, N, T, J = 1024, 1024, 2048, 1024
 FLOPS = 2 * K * N * J
@@ -51,11 +50,16 @@ def tile_list_embg_qf_mul_kernel(tc, dy, w8, w4_words, w4_scales, d, wgo, offs, 
         w4_codes = [slot([P, 2 * HALF], U8, "w4_codes%d" % h) for h in range(2)]
         w8_codes = [slot([P, HALF], U32, "w8_codes%d" % h) for h in range(2)]
         w8_plane = [slot([P, HALF], U8, "w8_plane%d" % h) for h in range(2)]
-        dy_codes = {(a, q): slot([P, QUART], U32, "dy_codes%d%d" % (a, q)) for a in (W8, W4) for q in range(4)}
-        dy_plane = {(a, q): slot([P, QUART], U8, "dy_plane%d%d" % (a, q)) for a in (W8, W4) for q in range(4)}
+        dy_codes = {(a, q): slot([P, QUART], U32, "dy_codes%d%d" % (a, q)) for a in (W8, W4) for q in range(1, 4) if (a, q) != (W4, 2)}
+        dy_plane = {(a, q): slot([P, QUART], U8, "dy_plane%d%d" % (a, q)) for a in (W8, W4) for q in range(1, 4)}
+        strip_codes = slot([P, 3 * QUART], U32, "strip_codes")
+        strip_plane = slot([P, 3 * QUART], U8, "strip_plane")
+        for i, a in ((1, W4), (2, W8)):
+            dy_codes[a, 0] = strip_codes[:, i * QUART : (i + 1) * QUART]
+            dy_plane[a, 0] = strip_plane[:, i * QUART : (i + 1) * QUART]
         wgo_rows = slot([P, P], F32, "wgo_rows")
         ident = slot([P, P], F32, "ident")
-        pages = [slot([P, T], F32, "page%d" % i) for i in range(2)]
+        pages = [slot([P, T], F32, "page%d" % i) for i in range(3)]
 
         pieces = {}
         for c in range(4):
@@ -64,10 +68,12 @@ def tile_list_embg_qf_mul_kernel(tc, dy, w8, w4_words, w4_scales, d, wgo, offs, 
         for a in (W8, W4):
             rows = dy[a * K_PASS : (a + 1) * K_PASS, :]
             for q in range(4):
-                pieces[a, q] = (rows[:, q * QUART : (q + 1) * QUART], dy_codes[a, q][:], dy_plane[a, q][:], E5M2X4)
+                pieces[a, q] = (rows[:, q * QUART : (q + 1) * QUART], dy_codes.get((a, q)), dy_plane[a, q][:], E5M2X4)
         for jt in range(2):
             cols = slice(jt * P, (jt + 1) * P)
             pieces["first", jt] = (dy[0:K_PASS, cols], dy_codes[W8, 0][:, cols], dy_plane[W8, 0][:, cols], E5M2X4)
+            rows = dy[0:K_PASS, QUART + jt * P : QUART + (jt + 1) * P]
+            pieces["second", jt] = (rows, dy_codes[W8, 1][:, cols], dy_plane[W8, 1][:, cols], E5M2X4)
         raw, woven = {}, {}
 
         def raw_tag(key):
@@ -84,7 +90,7 @@ def tile_list_embg_qf_mul_kernel(tc, dy, w8, w4_words, w4_scales, d, wgo, offs, 
 
         def quantize(key):
             rows, codes, plane, fmt = pieces[key]
-            nc.vector.quantize_mx(out=codes.bitcast(fmt), scales=plane, in_=woven[key][:].rearrange("p c t -> p (c t)"))
+            nc.vector.quantize_mx(out=codes[:].bitcast(fmt), scales=plane, in_=woven[key][:].rearrange("p c t -> p (c t)"))
 
         def load_w4(h):
             nc.sync.dma_start(
@@ -100,8 +106,21 @@ def tile_list_embg_qf_mul_kernel(tc, dy, w8, w4_words, w4_scales, d, wgo, offs, 
                 d_part[r, lo] = tile[:, r - r0, :]
 
         nc.vector.memset(w4_plane[:].bitcast(I32), 0)
-        nc.gpsimd.memset(wgo_rows[:], 0.0)
-        make_identity(nc, ident[:])
+        nc.vector.memset(wgo_rows[:], 0.0)
+        ones = slot([P, P], F32, "ones")
+        quadrant = slot([P, 1], F32, "quadrant")
+        ramp = slot([P, P], F32, "ramp")
+        lane = slot([P, 32], F32, "lane")
+        nc.vector.memset(ones[:], 1.0)
+        for quad in range(4):
+            nc.vector.memset(quadrant[32 * quad : 32 * (quad + 1), :], 32.0 * quad)
+        nc.vector.tensor_tensor_scan(ramp[:], ones[:], ones[:], 0.0, MULT, mybir.AluOpType.add)
+        nc.vector.transpose(lane[:], ramp[:, 0:32])
+        nc.vector.tensor_scalar(
+            ident[:], ramp[:], lane[:, 0:1], quadrant[:], mybir.AluOpType.subtract, mybir.AluOpType.is_equal
+        )
+        nc.vector.memset(strip_codes[:, 0:QUART].bitcast(I32), 0)
+        nc.vector.memset(strip_plane[:, 0:QUART].bitcast(I32), 0)
         for page in pages:
             nc.vector.memset(page[:].bitcast(I32), 0)
 
@@ -118,9 +137,13 @@ def tile_list_embg_qf_mul_kernel(tc, dy, w8, w4_words, w4_scales, d, wgo, offs, 
         load_piece(("first", 0))
         load_piece(("first", 1))
         load_piece((W4, 1))
-        load_piece((W8, 1))
+        wgo_first = slot([P, QUART], F32, "wgo_first")
+        nc.sync.dma_start(out=wgo_first[:], in_=wgo[:, 0:QUART])
+        load_piece(("second", 0))
         nc.sync.dma_start(offsets[:], offs)
-        load_d(0, 2, 0, QUART)
+        load_d(0, 1, 0, QUART)
+        load_piece(("second", 1))
+        load_d(1, 2, 0, QUART)
         load_d(2, 4, 0, QUART)
         load_piece((W4, 2))
         load_piece((W8, 2))
@@ -209,37 +232,68 @@ def tile_list_embg_qf_mul_kernel(tc, dy, w8, w4_words, w4_scales, d, wgo, offs, 
             for engine_copy, cols in ((scopy, slice(0, split)), (vcopy, slice(split, width))):
                 round_and_weave(engine_copy, woven[key][:, cols, :], raw[key][:, :, cols])
 
-        prepare((W4, 0))
-        weave(("w", 0), scopy)
-        weave_shared(("w", 1))
-        quantize(("w", 0))
-        quantize(("w", 1))
-        weave(("first", 0), scopy)
-        weave_shared(("first", 1))
-        for jt in range(2):
-            quantize(("first", jt))
         wgo_turned = bank(7)
         nc.tensor.transpose(wgo_turned[:, 0:P], wgo_rows[:], ident[:])
-        wgo_cols = slot([P, J // P], F32, "wgo_cols", raw_tag(("first", 1)))
+        prepare((W4, 0))
+        for key in (("w", 0), ("w", 1)):
+            weave_shared(key)
+            quantize(key)
+        weave(("first", 0), scopy)
+        weave(("first", 1), vcopy)
+        wgo_cols = slot([P, J // P], F32, "wgo_cols", raw_tag(("first", 0)))
         scopy(wgo_cols[:], wgo_turned[:, 0 : J // P])
-        accs = products([0, 1], 0, [0, 1])
+        for jt in range(2):
+            quantize(("first", jt))
+        def strip_pass(acc, a):
+            if a == W8:
+                lhsT, lhsT_scale, cols = w8_codes[0][:, 0:P].bitcast(E4M3X4), w8_plane[0][:, 0:P], slice(QUART, 3 * QUART)
+            else:
+                lhsT, lhsT_scale, cols = w4_codes[0][:, 0 : 2 * P].bitcast(E2M1X4), w4_plane[:, 0:P], slice(0, HALF)
+            nc.tensor.matmul_mx(
+                out=acc[:],
+                lhsT=lhsT,
+                lhsT_scale=lhsT_scale,
+                rhs=strip_codes[:, cols].bitcast(E5M2X4),
+                rhs_scale=strip_plane[:, cols],
+                start=(a == W4),
+                stop=(a == W8),
+            )
+
+        accs = [bank(0), bank(1)]
+        direct = bank(2)
         for a in (W4, W8):
-            weave((a, 1), vcopy)
-            quantize((a, 1))
+            strip_pass(direct, a)
+            for jt in range(2):
+                mm_pass(accs[jt], jt, 0, a)
+        weave((W4, 1), vcopy, "woven_first_1")
+        dx = slot([P, QUART], F32, "dx0_0")
+        nc.vector.tensor_tensor(dx[:], direct[:, QUART:HALF], wgo_first[:], MULT)
+        quantize((W4, 1))
+        place(dx, 0, [0])
 
         def late_page(tag):
             pages.append(slot([P, T], F32, "page%d" % len(pages), tag))
             nc.gpsimd.memset(pages[-1][:].bitcast(I32), 0)
 
-        late_page("woven_%s_%d" % (W8, 1))
-        for r in range(2):
-            place(copy_out(turn(weigh(0, accs, r * P, (r + 1) * P), [0], 4 + r), "dx0_%d" % r), 0, [r])
-        late_page("dx0_0")
-        place(copy_out(turn(weigh(0, accs, QUART, HALF), [0, 1], 6), "dx0_2"), 0, [2, 3])
-        prepare((W4, 2), "scaled2_0_256")
+        woven[W8, 1] = slot([P, QUART, PACK], BF16, "woven_second")
+        round_and_weave(scopy, woven[W8, 1][:, 0:P, :], raw["second", 0][:])
+        room = slot([P, QUART], F32, "room0", raw_tag(("second", 0)))
+        turned = turn(weigh(0, accs, P, 2 * P, room[:]), [0], 4)
+        round_and_weave(scopy, woven[W8, 1][:, P:QUART, :], raw["second", 1][:])
+        quantize((W8, 1))
+        late_page("woven_second")
+        room = slot([P, 3 * QUART], F32, "room1", raw_tag(("second", 1)))
+        scopy(room[:, 0:QUART], turned)
+        place(room[:, 0:QUART], 0, [1])
+        for r in (2, 3):
+            scaled = weigh(0, accs, r * P, (r + 1) * P, room[:, (r - 1) * QUART : r * QUART])
+            place(copy_out(turn(scaled, [0], 3 + r), "dx0_%d" % r), 0, [r])
+        dy_codes[W4, 2] = slot([P, QUART], U32, "dy_codes_held", "dx0_2")
+        pieces[W4, 2] = (pieces[W4, 2][0], dy_codes[W4, 2][:], dy_plane[W4, 2][:], E5M2X4)
+        prepare((W4, 2), raw_tag(("second", 0)))
         accs = products([2, 3], 0, [4, 5])
         scaled = weigh(1, accs, 0, HALF)
-        prepare((W8, 2), "scaled2_1_256")
+        prepare((W8, 2), raw_tag(("second", 1)))
 
         turned = [turn(scaled, [0], 0), turn(scaled, [1], 1), turn(scaled, [2, 3], 2)]
         for r in range(2):

@@ -50,8 +50,14 @@ def tile_list_embg_qf_mul_kernel(tc, dy, w8, w4_words, w4_scales, d, wgo, offs, 
         w4_codes = [slot([P, 2 * HALF], U8, "w4_codes%d" % h) for h in range(2)]
         w8_codes = [slot([P, HALF], U32, "w8_codes%d" % h) for h in range(2)]
         w8_plane = [slot([P, HALF], U8, "w8_plane%d" % h) for h in range(2)]
-        dy_codes = {(a, q): slot([P, QUART], U32, "dy_codes%d%d" % (a, q)) for a in (W8, W4) for q in range(1, 4) if (a, q) != (W4, 2)}
-        dy_plane = {(a, q): slot([P, QUART], U8, "dy_plane%d%d" % (a, q)) for a in (W8, W4) for q in range(1, 4)}
+        dy_codes = {(a, q): slot([P, QUART], U32, "dy_codes%d%d" % (a, q)) for a in (W8, W4) for q in (1,)}
+        dy_plane = {(a, q): slot([P, QUART], U8, "dy_plane%d%d" % (a, q)) for a in (W8, W4) for q in (1,)}
+        pair_codes = {q: slot([P, HALF], U32, "pair_codes%d" % q) for q in (2, 3)}
+        pair_plane = {q: slot([P, HALF], U8, "pair_plane%d" % q) for q in (2, 3)}
+        for q in (2, 3):
+            for a in (W8, W4):
+                dy_codes[a, q] = pair_codes[q][:, a * QUART : (a + 1) * QUART]
+                dy_plane[a, q] = pair_plane[q][:, a * QUART : (a + 1) * QUART]
         strip_codes = slot([P, 3 * QUART], U32, "strip_codes")
         strip_plane = slot([P, 3 * QUART], U8, "strip_plane")
         for i, a in ((1, W4), (2, W8)):
@@ -68,7 +74,7 @@ def tile_list_embg_qf_mul_kernel(tc, dy, w8, w4_words, w4_scales, d, wgo, offs, 
         for a in (W8, W4):
             rows = dy[a * K_PASS : (a + 1) * K_PASS, :]
             for q in range(4):
-                pieces[a, q] = (rows[:, q * QUART : (q + 1) * QUART], dy_codes.get((a, q)), dy_plane[a, q][:], E5M2X4)
+                pieces[a, q] = (rows[:, q * QUART : (q + 1) * QUART], dy_codes[a, q][:], dy_plane[a, q][:], E5M2X4)
         for jt in range(2):
             cols = slice(jt * P, (jt + 1) * P)
             pieces["first", jt] = (dy[0:K_PASS, cols], dy_codes[W8, 0][:, cols], dy_plane[W8, 0][:, cols], E5M2X4)
@@ -225,6 +231,15 @@ def tile_list_embg_qf_mul_kernel(tc, dy, w8, w4_words, w4_scales, d, wgo, offs, 
             weave(key, scopy, tag)
             quantize(key)
 
+        def prepare_pair(keys, codes, plane, fmt, tag):
+            both = slot([P, HALF, PACK], BF16, "woven_pair_%s_%d" % keys[0], tag)
+            for key, lo in keys_at(keys):
+                round_and_weave(scopy, both[:, lo : lo + QUART, :], raw[key][:])
+            nc.vector.quantize_mx(out=codes.bitcast(fmt), scales=plane, in_=both[:].rearrange("p c t -> p (c t)"))
+
+        def keys_at(keys):
+            return [(key, (key[1] % 2 if key[0] == "w" else key[0]) * QUART) for key in keys]
+
         def weave_shared(key):
             width = pieces[key][0].shape[1]
             split = 3 * width // 8
@@ -235,9 +250,10 @@ def tile_list_embg_qf_mul_kernel(tc, dy, w8, w4_words, w4_scales, d, wgo, offs, 
         wgo_turned = bank(7)
         nc.tensor.transpose(wgo_turned[:, 0:P], wgo_rows[:], ident[:])
         prepare((W4, 0))
-        for key in (("w", 0), ("w", 1)):
-            weave_shared(key)
-            quantize(key)
+        weave(("w", 0), scopy)
+        weave_shared(("w", 1))
+        quantize(("w", 0))
+        quantize(("w", 1))
         weave(("first", 0), scopy)
         weave(("first", 1), vcopy)
         wgo_cols = slot([P, J // P], F32, "wgo_cols", raw_tag(("first", 0)))
@@ -288,43 +304,48 @@ def tile_list_embg_qf_mul_kernel(tc, dy, w8, w4_words, w4_scales, d, wgo, offs, 
         for r in (2, 3):
             scaled = weigh(0, accs, r * P, (r + 1) * P, room[:, (r - 1) * QUART : r * QUART])
             place(copy_out(turn(scaled, [0], 3 + r), "dx0_%d" % r), 0, [r])
-        dy_codes[W4, 2] = slot([P, QUART], U32, "dy_codes_held", "dx0_2")
-        pieces[W4, 2] = (pieces[W4, 2][0], dy_codes[W4, 2][:], dy_plane[W4, 2][:], E5M2X4)
-        prepare((W4, 2), raw_tag(("second", 0)))
-        accs = products([2, 3], 0, [4, 5])
-        scaled = weigh(1, accs, 0, HALF)
-        prepare((W8, 2), raw_tag(("second", 1)))
 
-        turned = [turn(scaled, [0], 0), turn(scaled, [1], 1), turn(scaled, [2, 3], 2)]
-        for r in range(2):
-            place(copy_out(turned[r], "dx1_%d" % r, raw_tag(((W8, W4)[r], 2))), 1, [r])
-        prepare((W4, 3), "scaled2_2_0")
-        prepare((W8, 3), "scaled2_3_0")
-        rooms = {2: slot([P, 3 * HALF], F32, "room2", raw_tag((W8, 3)))}
-        scopy(rooms[2][:, J : J + HALF], turned[2])
-        place(rooms[2][:, J : J + HALF], 1, [2, 3])
+        prepare((W4, 2), raw_tag(("second", 1)))
+        accs = products([2, 3], 0, [4, 0])
+        turned = [turn(weigh(1, accs, r * P, (r + 1) * P), [0], 2 + r) for r in range(2)]
+        scaled = weigh(1, accs, QUART, HALF)
+        turned.extend(turn(scaled, [r], b) for r, b in enumerate((7, 1)))
+        place(copy_out(turned[0], "dx1_0", raw_tag((W4, 2))), 1, [0])
+        place(copy_out(turned[1], "dx1_1"), 1, [1])
+        prepare((W8, 2), "scaled2_2_128")
+        prepare((W4, 3), "scaled2_3_128")
+        room = slot([P, HALF], F32, "dx1_2", raw_tag((W8, 2)))
+        for r in (2, 3):
+            scopy(room[:, (r - 2) * QUART : (r - 1) * QUART], turned[r])
+        place(room, 1, [2, 3])
+        prepare((W8, 3), "scaled2_2_256")
+        rooms = {2: slot([P, 3 * QUART], F32, "room2", raw_tag((W8, 3)))}
+        late_tags = {2: raw_tag((W4, 3)), 3: None}
 
         late = []
-        for q, sums, turns in ((2, [0, 1], [3, 4]), (3, [3, 4], [5, 6])):
+        for q, sums, turns in ((2, [4, 0], [2, 3, 5]), (3, [2, 3], [5, 6, 7])):
             accs = products([2 * q, 2 * q + 1], 0, sums)
-            scaled = weigh(q, accs, 0, QUART, rooms[q][:, 0:HALF])
-            turned = [turn(scaled, [r], turns[r]) for r in range(2)]
-            late.extend(weigh(q, accs, QUART, HALF, rooms[q][:, HALF:J]))
+            room = rooms[q]
+            turned = [turn(weigh(q, accs, 0, P, room[:, 0:QUART]), [0], turns[0])]
+            scaled = weigh(q, accs, P, 3 * P, room[:, QUART : 3 * QUART])
+            turned.extend(turn(scaled, [r], turns[1 + r]) for r in range(2))
+            late_room = slot([P, QUART], F32, "late%d" % q, late_tags[q])
+            late.extend(weigh(q, accs, 3 * P, HALF, late_room[:]))
             for r in range(2):
                 place(copy_out(turned[r], "dx%d_%d" % (q, r)), q, [r])
             if q == 2:
-                prepare(("w", 2), "scaled2_2_0")
-                prepare(("w", 3), "scaled2_3_0")
-                rooms[3] = slot([P, J], F32, "room3", raw_tag(("w", 3)))
-        for r, b in ((2, 7), (3, 2)):
-            dx = copy_out(turn(late, [r - 2], b), "dx_late%d" % r)
-            scatter(r, dx[:], d_part[r, HALF], HALF, J)
+                prepare_pair([("w", 2), ("w", 3)], w8_codes[1][:], w8_plane[1][:], E4M3X4, raw_tag((W8, 3)))
+                rooms[3] = slot([P, 3 * QUART], F32, "room3", raw_tag(("w", 3)))
+                late_tags[3] = raw_tag((W4, 2))
+            place(copy_out(turned[2], "dx%d_2" % q, raw_tag(("w", 2)) if q == 2 else None), q, [2])
+        dx = copy_out(turn(late, [0], 1), "dx_late")
+        scatter(3, dx[:], d_part[3, HALF], HALF, J)
 
         scaled = []
         for u in range(2):
-            scaled.append(weigh(2 * u, products(list(range(4 * u, 4 * u + 4)), 1, [5, 6, 7, 2]), 0, HALF))
+            scaled.append(weigh(2 * u, products(list(range(4 * u, 4 * u + 4)), 1, [4, 0, 5, 6]), 0, HALF))
         for r in range(4):
             dx = slot([P, J], F32, "dx_hi%d" % r)
             for u in range(2):
-                scopy(dx[:, u * HALF : (u + 1) * HALF], turn(scaled[u], [r], (0, 1, 3, 4)[(2 * r + u) % 4]))
+                scopy(dx[:, u * HALF : (u + 1) * HALF], turn(scaled[u], [r], (2, 3, 7, 1)[(2 * r + u) % 4]))
             scatter(4 + r, dx[:], d_part[4 + r, 0], 0, J)

@@ -1,6 +1,7 @@
 from contextlib import ExitStack
 
 import concourse.mybir as mybir
+from concourse.masks import make_identity
 
 K, N, T, J = 1024, 1024, 2048, 1024
 FLOPS = 2 * K * N * J
@@ -113,22 +114,15 @@ def tile_list_embg_qf_mul_kernel(tc, dy, w8, w4_words, w4_scales, d, wgo, offs, 
 
         nc.vector.memset(w4_plane[:].bitcast(I32), 0)
         nc.vector.memset(wgo_rows[:], 0.0)
-        ones = slot([P, P], F32, "ones")
-        quadrant = slot([P, 1], F32, "quadrant")
-        ramp = slot([P, P], F32, "ramp")
-        lane = slot([P, 32], F32, "lane")
-        nc.vector.memset(ones[:], 1.0)
-        for quad in range(4):
-            nc.vector.memset(quadrant[32 * quad : 32 * (quad + 1), :], 32.0 * quad)
-        nc.vector.tensor_tensor_scan(ramp[:], ones[:], ones[:], 0.0, MULT, mybir.AluOpType.add)
-        nc.vector.transpose(lane[:], ramp[:, 0:32])
-        nc.vector.tensor_scalar(
-            ident[:], ramp[:], lane[:, 0:1], quadrant[:], mybir.AluOpType.subtract, mybir.AluOpType.is_equal
-        )
+        make_identity(nc, ident[:])
         nc.vector.memset(strip_codes[:, 0:QUART].bitcast(I32), 0)
         nc.vector.memset(strip_plane[:, 0:QUART].bitcast(I32), 0)
-        for page in pages:
-            nc.vector.memset(page[:].bitcast(I32), 0)
+
+        def clear(page, lo, hi):
+            nc.vector.memset(pages[page][:, lo:hi].bitcast(I32), 0)
+
+        clear(0, 0, T)
+        clear(1, 0, T)
 
         load_piece((W4, 0))
         for quad in range(4):
@@ -163,7 +157,7 @@ def tile_list_embg_qf_mul_kernel(tc, dy, w8, w4_words, w4_scales, d, wgo, offs, 
         for r in range(4, 8):
             load_d(r, r + 1, 0, J)
 
-        def mm_pass(acc, jt, h, a):
+        def mm_pass(acc, jt, h, a, alone=False):
             q, cols = jt // 2, slice((jt % 2) * P, (jt % 2 + 1) * P)
             if a == W8:
                 rhs, rhs_scale = w8_codes[h][:].bitcast(E4M3X4), w8_plane[h][:]
@@ -176,7 +170,7 @@ def tile_list_embg_qf_mul_kernel(tc, dy, w8, w4_words, w4_scales, d, wgo, offs, 
                 rhs=rhs,
                 rhs_scale=rhs_scale,
                 start=(a == W4),
-                stop=(a == W8),
+                stop=(a == W8 or alone),
             )
 
         def bank(b):
@@ -240,17 +234,20 @@ def tile_list_embg_qf_mul_kernel(tc, dy, w8, w4_words, w4_scales, d, wgo, offs, 
         def keys_at(keys):
             return [(key, (key[1] % 2 if key[0] == "w" else key[0]) * QUART) for key in keys]
 
-        def weave_shared(key):
+        def weave_shared(key, eighths=3):
             width = pieces[key][0].shape[1]
-            split = 3 * width // 8
+            split = eighths * width // 8
             woven[key] = slot([P, width, PACK], BF16, "woven_%s_%d" % key)
             for engine_copy, cols in ((scopy, slice(0, split)), (vcopy, slice(split, width))):
                 round_and_weave(engine_copy, woven[key][:, cols, :], raw[key][:, :, cols])
 
         wgo_turned = bank(7)
         nc.tensor.transpose(wgo_turned[:, 0:P], wgo_rows[:], ident[:])
-        prepare((W4, 0))
-        weave(("w", 0), scopy)
+        weave_shared((W4, 0))
+        clear(2, 0, T // 2)
+        quantize((W4, 0))
+        clear(2, T // 2, T)
+        weave_shared(("w", 0), 5)
         weave_shared(("w", 1))
         quantize(("w", 0))
         quantize(("w", 1))
@@ -281,6 +278,8 @@ def tile_list_embg_qf_mul_kernel(tc, dy, w8, w4_words, w4_scales, d, wgo, offs, 
             strip_pass(direct, a)
             for jt in range(2):
                 mm_pass(accs[jt], jt, 0, a)
+            if a == W4:
+                mm_pass(bank(3), 0, 0, W4, alone=True)
         weave((W4, 1), vcopy, "woven_first_1")
         dx = slot([P, QUART], F32, "dx0_0")
         nc.vector.tensor_tensor(dx[:], direct[:, QUART:HALF], wgo_first[:], MULT)

@@ -183,7 +183,7 @@ def tile_list_embg_qf_mul_kernel(tc, dy, w8, w4_words, w4_scales, d, wgo, offs, 
                     mm_pass(acc, jt, h, a)
             return accs
 
-        def weigh(q, accs, lo, hi, room=None):
+        def weigh(q, accs, lo, hi, room=None, weights=None):
             tiles = []
             for i, acc in enumerate(accs):
                 jt, width = 2 * q + i, hi - lo
@@ -192,7 +192,7 @@ def tile_list_embg_qf_mul_kernel(tc, dy, w8, w4_words, w4_scales, d, wgo, offs, 
                     tiles.append(tile[:])
                 else:
                     tiles.append(room[:, i * width : (i + 1) * width])
-                nc.scalar.activation(out=tiles[i], in_=acc[:, lo:hi], func=COPY, scale=wgo_cols[:, jt : jt + 1])
+                nc.scalar.activation(out=tiles[i], in_=acc[:, lo:hi], func=COPY, scale=(wgo_cols if weights is None else weights)[:, jt : jt + 1])
             return tiles
 
         def turn(scaled_tiles, rs, b):
@@ -254,7 +254,9 @@ def tile_list_embg_qf_mul_kernel(tc, dy, w8, w4_words, w4_scales, d, wgo, offs, 
         weave(("first", 0), scopy)
         weave(("first", 1), vcopy)
         wgo_cols = slot([P, J // P], F32, "wgo_cols", raw_tag(("first", 0)))
+        wgo_head = slot([P, 2], F32, "wgo_head")
         scopy(wgo_cols[:], wgo_turned[:, 0 : J // P])
+        scopy(wgo_head[:], wgo_turned[:, 0:2])
         for jt in range(2):
             quantize(("first", jt))
         def strip_pass(acc, a):
@@ -290,13 +292,12 @@ def tile_list_embg_qf_mul_kernel(tc, dy, w8, w4_words, w4_scales, d, wgo, offs, 
             pages.append(slot([P, T], F32, "page%d" % len(pages), tag))
             nc.gpsimd.memset(pages[-1][:].bitcast(I32), 0)
 
-        woven[W8, 1] = slot([P, QUART, PACK], BF16, "woven_second")
+        turned = turn(weigh(0, accs, P, 2 * P, weights=wgo_head), [0], 4)
+        woven[W8, 1] = slot([P, QUART, PACK], BF16, "woven_second", "wgo_head")
         round_and_weave(scopy, woven[W8, 1][:, 0:P, :], raw["second", 0][:])
-        room = slot([P, QUART], F32, "room0", raw_tag(("second", 0)))
-        turned = turn(weigh(0, accs, P, 2 * P, room[:]), [0], 4)
         round_and_weave(scopy, woven[W8, 1][:, P:QUART, :], raw["second", 1][:])
         quantize((W8, 1))
-        late_page("woven_second")
+        late_page("wgo_head")
         room = slot([P, 3 * QUART], F32, "room1", raw_tag(("second", 1)))
         scopy(room[:, 0:QUART], turned)
         place(room[:, 0:QUART], 0, [1])

@@ -252,8 +252,8 @@ def tile_list_embg_qf_mul_kernel(tc, dy, w8, w4_words, w4_scales, d, wgo, offs, 
         quantize(("w", 0))
         quantize(("w", 1))
         weave(("first", 0), scopy)
-        weave(("first", 1), vcopy)
-        wgo_cols = slot([P, J // P], F32, "wgo_cols", raw_tag(("first", 0)))
+        weave_shared(("first", 1), 4)
+        wgo_cols = slot([P, J // P], F32, "wgo_cols", raw_tag(("first", 1)))
         wgo_head = slot([P, 2], F32, "wgo_head")
         scopy(wgo_cols[:], wgo_turned[:, 0 : J // P])
         scopy(wgo_head[:], wgo_turned[:, 0:2])

@@ -157,7 +157,7 @@ def tile_list_embg_qf_mul_kernel(tc, dy, w8, w4_words, w4_scales, d, wgo, offs, 
         for r in range(4, 8):
             load_d(r, r + 1, 0, J)
 
-        def mm_pass(acc, jt, h, a, alone=False):
+        def mm_pass(acc, jt, h, a):
             q, cols = jt // 2, slice((jt % 2) * P, (jt % 2 + 1) * P)
             if a == W8:
                 rhs, rhs_scale = w8_codes[h][:].bitcast(E4M3X4), w8_plane[h][:]
@@ -170,7 +170,7 @@ def tile_list_embg_qf_mul_kernel(tc, dy, w8, w4_words, w4_scales, d, wgo, offs, 
                 rhs=rhs,
                 rhs_scale=rhs_scale,
                 start=(a == W4),
-                stop=(a == W8 or alone),
+                stop=(a == W8),
             )
 
         def bank(b):
@@ -280,8 +280,6 @@ def tile_list_embg_qf_mul_kernel(tc, dy, w8, w4_words, w4_scales, d, wgo, offs, 
             strip_pass(direct, a)
             for jt in range(2):
                 mm_pass(accs[jt], jt, 0, a)
-            if a == W4:
-                mm_pass(bank(3), 0, 0, W4, alone=True)
         weave((W4, 1), vcopy, "woven_first_1")
         dx = slot([P, QUART], F32, "dx0_0")
         nc.vector.tensor_tensor(dx[:], direct[:, QUART:HALF], wgo_first[:], MULT)

@@ -1,7 +1,6 @@
 from contextlib import ExitStack
 
 import concourse.mybir as mybir
-from concourse.masks import make_identity
 
 K, N, T, J = 1024, 1024, 2048, 1024
 FLOPS = 2 * K * N * J
@@ -17,6 +16,8 @@ E5M2X4 = mybir.dt.float8_e5m2_x4
 E2M1X4 = mybir.dt.float4_e2m1fn_x4
 COPY = mybir.ActivationFunctionType.Copy
 MULT = mybir.AluOpType.mult
+ADD = mybir.AluOpType.add
+EQUAL = mybir.AluOpType.is_equal
 
 P = 128
 PACK = 4
@@ -42,62 +43,65 @@ def tile_list_embg_qf_mul_kernel(tc, dy, w8, w4_words, w4_scales, d, wgo, offs, 
     with ExitStack() as ctx:
         keep = ctx.enter_context(tc.tile_pool(name="keep", bufs=1))
         psum = ctx.enter_context(tc.psum_pool(name="psum", bufs=1))
+        laid = ctx.enter_context(tc.tile_pool(name="laid", bufs=1))
+
+        places = {
+            "woven_pair3": 0,
+            "raw_hi2": 3584,
+            "weighed5": 3584,
+            "weighed67": 4096,
+            "raw_lo2": 40448,
+            "values4": 40448,
+            "woven_lo2": 48640,
+            "codes2_0": 48640,
+            "raw_hi3": 44544,
+            "weighed_q2": 44544,
+            "woven_w45": 46592,
+            "weighed_q3": 11264,
+            "woven_w67": 13312,
+            "raw_w23": 15360,
+            "values0": 15360,
+            "weighed1": 16384,
+            "values1": 18944,
+            "raw_lo1a": 19456,
+            "weighed2": 19968,
+            "weighed3": 20992,
+            "raw_lo1b": 22016,
+            "values2": 22016,
+            "page2": 24064,
+            "woven_w23": 31232,
+            "woven_hi0b": 31232,
+            "page3": 32256,
+        }
 
         def slot(shape, dtype, name, tag=None):
+            if name in places:
+                return laid.tile(shape, dtype, name=name, offset=places[name], align_bytes=64)
             return keep.tile(shape, dtype, name=name, tag=tag or name, align_bytes=64)
+
+        def bank(b):
+            return psum.tile([P, HALF], F32, name="bank%d" % b)
 
         offsets = keep.tile([P, J // 16], U16, name="offsets")
         w4_plane = slot([P, N], U8, "w4_plane")
         w4_codes = [slot([P, 2 * HALF], U8, "w4_codes%d" % h) for h in range(2)]
         w8_codes = [slot([P, HALF], U32, "w8_codes%d" % h) for h in range(2)]
         w8_plane = [slot([P, HALF], U8, "w8_plane%d" % h) for h in range(2)]
-        dy_codes = {(a, q): slot([P, QUART], U32, "dy_codes%d%d" % (a, q)) for a in (W8, W4) for q in (1,)}
-        dy_plane = {(a, q): slot([P, QUART], U8, "dy_plane%d%d" % (a, q)) for a in (W8, W4) for q in (1,)}
-        pair_codes = {q: slot([P, HALF], U32, "pair_codes%d" % q) for q in (2, 3)}
-        pair_plane = {q: slot([P, HALF], U8, "pair_plane%d" % q) for q in (2, 3)}
-        for q in (2, 3):
-            for a in (W8, W4):
-                dy_codes[a, q] = pair_codes[q][:, a * QUART : (a + 1) * QUART]
-                dy_plane[a, q] = pair_plane[q][:, a * QUART : (a + 1) * QUART]
-        strip_codes = slot([P, 3 * QUART], U32, "strip_codes")
-        strip_plane = slot([P, 3 * QUART], U8, "strip_plane")
-        for i, a in ((1, W4), (2, W8)):
-            dy_codes[a, 0] = strip_codes[:, i * QUART : (i + 1) * QUART]
-            dy_plane[a, 0] = strip_plane[:, i * QUART : (i + 1) * QUART]
+        dy_codes = {q: slot([P, 2 * QUART], U32, "dy_codes%d" % q) for q in (0, 1, 3)}
+        dy_plane = [slot([P, 2 * QUART], U8, "dy_plane%d" % q) for q in range(4)]
+        apart = {}
         wgo_rows = slot([P, P], F32, "wgo_rows")
         ident = slot([P, P], F32, "ident")
-        pages = [slot([P, T], F32, "page%d" % i) for i in range(3)]
+        pages = [slot([P, T], F32, "page%d" % i) for i in range(2)]
 
-        pieces = {}
-        for c in range(4):
-            h, cols = c // 2, slice((c % 2) * QUART, (c % 2 + 1) * QUART)
-            pieces["w", c] = (w8[:, c * QUART : (c + 1) * QUART], w8_codes[h][:, cols], w8_plane[h][:, cols], E4M3X4)
-        for a in (W8, W4):
-            rows = dy[a * K_PASS : (a + 1) * K_PASS, :]
-            for q in range(4):
-                pieces[a, q] = (rows[:, q * QUART : (q + 1) * QUART], dy_codes[a, q][:], dy_plane[a, q][:], E5M2X4)
-        for jt in range(2):
-            cols = slice(jt * P, (jt + 1) * P)
-            pieces["first", jt] = (dy[0:K_PASS, cols], dy_codes[W8, 0][:, cols], dy_plane[W8, 0][:, cols], E5M2X4)
-            rows = dy[0:K_PASS, QUART + jt * P : QUART + (jt + 1) * P]
-            pieces["second", jt] = (rows, dy_codes[W8, 1][:, cols], dy_plane[W8, 1][:, cols], E5M2X4)
-        raw, woven = {}, {}
+        raw = {}
 
-        def raw_tag(key):
-            return "raw_%s_%d" % key
+        def load_rows(name, rows):
+            raw[name] = slot([P, PACK, rows.shape[1]], F32, "raw_" + name)
+            nc.sync.dma_start(out=raw[name][:], in_=rows.rearrange("(p t) c -> p t c", t=PACK))
 
-        def load_piece(key):
-            rows = pieces[key][0]
-            raw[key] = slot([P, PACK, rows.shape[1]], F32, raw_tag(key))
-            nc.sync.dma_start(out=raw[key][:], in_=rows.rearrange("(p t) c -> p t c", t=PACK))
-
-        def weave(key, engine_copy, tag=None):
-            woven[key] = slot([P, pieces[key][0].shape[1], PACK], BF16, "woven_%s_%d" % key, tag)
-            round_and_weave(engine_copy, woven[key][:], raw[key][:])
-
-        def quantize(key):
-            rows, codes, plane, fmt = pieces[key]
-            nc.vector.quantize_mx(out=codes[:].bitcast(fmt), scales=plane, in_=woven[key][:].rearrange("p c t -> p (c t)"))
+        def load_dy(name, a, lo, hi):
+            load_rows(name, dy[a * K_PASS : (a + 1) * K_PASS, lo:hi])
 
         def load_w4(h):
             nc.sync.dma_start(
@@ -112,238 +116,250 @@ def tile_list_embg_qf_mul_kernel(tc, dy, w8, w4_words, w4_scales, d, wgo, offs, 
             for r in range(r0, r1):
                 d_part[r, lo] = tile[:, r - r0, :]
 
-        nc.vector.memset(w4_plane[:].bitcast(I32), 0)
-        nc.vector.memset(wgo_rows[:], 0.0)
-        make_identity(nc, ident[:])
-        nc.vector.memset(strip_codes[:, 0:QUART].bitcast(I32), 0)
-        nc.vector.memset(strip_plane[:, 0:QUART].bitcast(I32), 0)
+        wgo_wide = {}
 
-        def clear(page, lo, hi):
-            nc.vector.memset(pages[page][:, lo:hi].bitcast(I32), 0)
+        def load_wgo(q):
+            wgo_wide[q] = slot([P, QUART], F32, "wgo_wide%d" % q)
+            nc.sync.dma_start(out=wgo_wide[q][:], in_=wgo[:, q * QUART : (q + 1) * QUART])
 
-        clear(0, 0, T)
-        clear(1, 0, T)
-
-        load_piece((W4, 0))
+        ones = slot([P, P], F32, "ones")
+        quad_base = slot([P, 1], F32, "quad_base")
+        nc.vector.memset(ones[:, 0 : P - 1], 1.0)
+        nc.vector.memset(ones[:, P - 1 : P], 1.0)
         for quad in range(4):
-            nc.sync.dma_start(
+            nc.vector.memset(quad_base[32 * quad : 32 * quad + 32, :], -32.0 * quad)
+        count = slot([P, 32], F32, "count")
+        nc.vector.tensor_tensor_scan(count[:], ones[:, 0:32], ones[:, 0:32], 0.0, MULT, ADD)
+        shifted = slot([P, P], F32, "shifted")
+        nc.vector.tensor_tensor_scan(shifted[:], ones[:], ones[:], quad_base[:], MULT, ADD)
+        lane = slot([P, 32], F32, "lane")
+        nc.vector.transpose(lane[:], count[:])
+        nc.vector.tensor_tensor(ident[:], shifted[:], lane[:, 0:1].to_broadcast([P, P]), EQUAL)
+        nc.vector.memset(pages[0][:].bitcast(I32), 0)
+        nc.gpsimd.memset(pages[1][:].bitcast(I32), 0)
+
+        for quad in range(4):
+            nc.scalar.dma_start(
                 out=w4_plane[32 * quad : 32 * quad + 4, :].bitcast(I32),
                 in_=w4_scales[0][4 * quad : 4 * quad + 4, :].bitcast(I32),
             )
-        load_w4(0)
-        load_piece(("w", 0))
-        load_piece(("w", 1))
         nc.sync.dma_start(out=wgo_rows[0 : J // P, :], in_=wgo[0].rearrange("(c p) -> c p", p=P))
-        load_piece(("first", 0))
-        load_piece(("first", 1))
-        load_piece((W4, 1))
-        wgo_first = slot([P, QUART], F32, "wgo_first")
-        nc.sync.dma_start(out=wgo_first[:], in_=wgo[:, 0:QUART])
-        load_piece(("second", 0))
-        nc.sync.dma_start(offsets[:], offs)
+        load_dy("lo0", W4, 0, QUART)
+        load_rows("w01", w8[:, 0:QUART])
+        load_w4(0)
+        load_dy("hi0a", W8, 0, P)
+        load_dy("hi0b", W8, P, QUART)
+        load_rows("w23", w8[:, QUART:HALF])
+        load_wgo(0)
         load_d(0, 1, 0, QUART)
-        load_piece(("second", 1))
+        nc.sync.dma_start(offsets[:], offs)
+        load_dy("lo1a", W4, QUART, QUART + P)
         load_d(1, 2, 0, QUART)
-        load_d(2, 4, 0, QUART)
-        load_piece((W4, 2))
-        load_piece((W8, 2))
-        load_d(0, 4, QUART, HALF)
-        load_piece((W4, 3))
-        load_piece((W8, 3))
-        load_d(0, 4, HALF, J)
-        load_piece(("w", 2))
-        load_piece(("w", 3))
+        load_dy("lo1b", W4, QUART + P, HALF)
+        load_d(2, 3, 0, QUART)
+        load_dy("hi1", W8, QUART, HALF)
+        load_d(3, 4, 0, QUART)
+        load_wgo(1)
+        load_d(0, 1, QUART, HALF)
+        load_dy("lo2", W4, HALF, HALF + QUART)
+        load_d(1, 2, QUART, HALF)
+        load_dy("hi2", W8, HALF, HALF + QUART)
+        load_d(2, 4, QUART, HALF)
+        load_dy("lo3", W4, HALF + QUART, J)
+        load_d(0, 4, HALF, HALF + QUART)
+        load_dy("hi3", W8, HALF + QUART, J)
+        load_rows("w45", w8[:, HALF : HALF + QUART])
         load_w4(1)
+        load_d(0, 4, HALF + QUART, J)
+        load_rows("w67", w8[:, HALF + QUART : N])
         for r in range(4, 8):
             load_d(r, r + 1, 0, J)
 
-        def mm_pass(acc, jt, h, a):
-            q, cols = jt // 2, slice((jt % 2) * P, (jt % 2 + 1) * P)
+        def woven_for(name, width):
+            return slot([P, width, PACK], BF16, "woven_" + name)
+
+        def quantize(woven, codes, plane, fmt):
+            nc.vector.quantize_mx(out=codes.bitcast(fmt), scales=plane, in_=woven.rearrange("p c t -> p (c t)"))
+
+        def quantize_dy(woven, q, lo, hi):
+            quantize(woven, dy_codes[q][:, lo:hi], dy_plane[q][:, lo:hi], E5M2X4)
+
+        def quantize_w8(woven, lo, hi):
+            h, cols = lo // HALF, slice(lo % HALF, lo % HALF + hi - lo)
+            quantize(woven, w8_codes[h][:, cols], w8_plane[h][:, cols], E4M3X4)
+
+        def weave_shared(name, eighths):
+            width = raw[name].shape[2]
+            split = eighths * width // 8
+            woven = woven_for(name, width)
+            for engine_copy, cols in ((scopy, slice(0, split)), (vcopy, slice(split, width))):
+                round_and_weave(engine_copy, woven[:, cols, :], raw[name][:, :, cols])
+            return woven
+
+        def weave(name, engine_copy):
+            woven = woven_for(name, raw[name].shape[2])
+            round_and_weave(engine_copy, woven[:], raw[name][:])
+            return woven
+
+        def weights(a, lo, hi):
+            h, c0, c1 = lo // HALF, lo % HALF, lo % HALF + hi - lo
             if a == W8:
-                rhs, rhs_scale = w8_codes[h][:].bitcast(E4M3X4), w8_plane[h][:]
-            else:
-                rhs, rhs_scale = w4_codes[h][:].bitcast(E2M1X4), w4_plane[:, h * HALF : (h + 1) * HALF]
+                return w8_codes[h][:, c0:c1].bitcast(E4M3X4), w8_plane[h][:, c0:c1]
+            return w4_codes[h][:, 2 * c0 : 2 * c1].bitcast(E2M1X4), w4_plane[:, lo:hi]
+
+        def gradient(a, lo, hi):
+            q = lo // QUART
+            cols = slice(a * QUART + lo % QUART, a * QUART + lo % QUART + hi - lo)
+            codes = apart[a][:, lo % QUART : lo % QUART + hi - lo] if q == 2 else dy_codes[q][:, cols]
+            return codes.bitcast(E5M2X4), dy_plane[q][:, cols]
+
+        def mx_pass(acc, still, moving, start, stop):
             nc.tensor.matmul_mx(
-                out=acc[:],
-                lhsT=dy_codes[a, q][:, cols].bitcast(E5M2X4),
-                lhsT_scale=dy_plane[a, q][:, cols],
-                rhs=rhs,
-                rhs_scale=rhs_scale,
-                start=(a == W4),
-                stop=(a == W8),
+                out=acc, lhsT=still[0], lhsT_scale=still[1], rhs=moving[0], rhs_scale=moving[1], start=start, stop=stop
             )
 
-        def bank(b):
-            return psum.tile([P, HALF], F32, name="bank%d" % b)
-
-        def products(jts, h, banks):
-            accs = [bank(b) for b in banks]
+        def sums(jts, lo, hi, b):
+            acc, width = bank(b), hi - lo
+            parts = [acc[:, i * width : (i + 1) * width] for i in range(len(jts))]
             for a in (W4, W8):
-                for acc, jt in zip(accs, jts):
-                    mm_pass(acc, jt, h, a)
-            return accs
+                for i, jt in enumerate(jts):
+                    first, last = (a == W4 and i == 0), (a == W8 and i == len(jts) - 1)
+                    mx_pass(parts[i], gradient(a, jt * P, (jt + 1) * P), weights(a, lo, hi), first, last)
+            return parts
 
-        def weigh(q, accs, lo, hi, room=None, weights=None):
-            tiles = []
-            for i, acc in enumerate(accs):
-                jt, width = 2 * q + i, hi - lo
-                if room is None:
-                    tile = slot([P, width], F32, "scaled%d_%d_%d" % (len(accs), jt, lo))
-                    tiles.append(tile[:])
-                else:
-                    tiles.append(room[:, i * width : (i + 1) * width])
-                nc.scalar.activation(out=tiles[i], in_=acc[:, lo:hi], func=COPY, scale=(wgo_cols if weights is None else weights)[:, jt : jt + 1])
+        def weigh(parts, jts, room):
+            width = parts[0].shape[1]
+            tiles = [room[:, i * width : (i + 1) * width] for i in range(len(jts))]
+            for tile, part, jt in zip(tiles, parts, jts):
+                nc.scalar.activation(out=tile, in_=part, func=COPY, scale=wgo_cols[:, jt : jt + 1])
             return tiles
 
-        def turn(scaled_tiles, rs, b):
+        def turn(tiles, rs, b):
             turned = bank(b)
-            blocks = [scaled[:, r * P : (r + 1) * P] for r in rs for scaled in scaled_tiles]
+            blocks = [tile[:, r * P : (r + 1) * P] for r in rs for tile in tiles]
             for i, block in enumerate(blocks):
                 nc.tensor.transpose(turned[:, i * P : (i + 1) * P], block, ident[:])
             return turned[:, 0 : P * len(blocks)]
 
-        def copy_out(turned, name, tag=None):
-            dx = slot([P, turned.shape[1]], F32, name, tag)
-            scopy(dx[:], turned)
-            return dx
+        def room_for(width, name, tag=None):
+            return slot([P, width], F32, name, tag)
 
-        def scatter(r, values, factors, lo, hi):
+        def scatter(r, values, lo, hi):
             window = pages[r % PAGES][:].indirect(offsets[:, lo // 16 : hi // 16])
-            nc.vector.tensor_tensor(window, values, factors, MULT)
+            nc.vector.tensor_tensor(window, values, d_part[r, lo], MULT)
             if hi == J:
                 nc.sync.dma_start(out=out[r * P : (r + 1) * P, :], in_=pages[r % PAGES][:])
 
-        def place(dx, q, rs):
-            for i, r in enumerate(rs):
-                if q < 2:
-                    factors = d_part[r, q * QUART]
-                else:
-                    factors = d_part[r, HALF][:, (q - 2) * QUART : (q - 1) * QUART]
-                scatter(r, dx[:, i * QUART : (i + 1) * QUART], factors, q * QUART, (q + 1) * QUART)
-
-        def prepare(key, tag=None):
-            weave(key, scopy, tag)
-            quantize(key)
-
-        def prepare_pair(keys, codes, plane, fmt, tag):
-            both = slot([P, HALF, PACK], BF16, "woven_pair_%s_%d" % keys[0], tag)
-            for key, lo in keys_at(keys):
-                round_and_weave(scopy, both[:, lo : lo + QUART, :], raw[key][:])
-            nc.vector.quantize_mx(out=codes.bitcast(fmt), scales=plane, in_=both[:].rearrange("p c t -> p (c t)"))
-
-        def keys_at(keys):
-            return [(key, (key[1] % 2 if key[0] == "w" else key[0]) * QUART) for key in keys]
-
-        def weave_shared(key, eighths=3):
-            width = pieces[key][0].shape[1]
-            split = eighths * width // 8
-            woven[key] = slot([P, width, PACK], BF16, "woven_%s_%d" % key)
-            for engine_copy, cols in ((scopy, slice(0, split)), (vcopy, slice(split, width))):
-                round_and_weave(engine_copy, woven[key][:, cols, :], raw[key][:, :, cols])
-
         wgo_turned = bank(7)
         nc.tensor.transpose(wgo_turned[:, 0:P], wgo_rows[:], ident[:])
-        weave_shared((W4, 0))
-        clear(2, 0, T // 2)
-        quantize((W4, 0))
-        clear(2, T // 2, T)
-        weave_shared(("w", 0), 5)
-        weave_shared(("w", 1))
-        quantize(("w", 0))
-        quantize(("w", 1))
-        weave(("first", 0), scopy)
-        weave_shared(("first", 1), 4)
-        wgo_cols = slot([P, J // P], F32, "wgo_cols", raw_tag(("first", 1)))
-        wgo_head = slot([P, 2], F32, "wgo_head")
+        quantize_dy(weave_shared("lo0", 4)[:], 0, QUART, HALF)
+        quantize_w8(weave_shared("w01", 3)[:], 0, QUART)
+        woven_a = weave("hi0a", scopy)
+        woven_b = weave_shared("hi0b", 3)
+        wgo_cols = slot([P, J // P], F32, "wgo_cols", "raw_hi0b")
         scopy(wgo_cols[:], wgo_turned[:, 0 : J // P])
-        scopy(wgo_head[:], wgo_turned[:, 0:2])
-        for jt in range(2):
-            quantize(("first", jt))
-        def strip_pass(acc, a):
-            if a == W8:
-                lhsT, lhsT_scale, cols = w8_codes[0][:, 0:P].bitcast(E4M3X4), w8_plane[0][:, 0:P], slice(QUART, 3 * QUART)
-            else:
-                lhsT, lhsT_scale, cols = w4_codes[0][:, 0 : 2 * P].bitcast(E2M1X4), w4_plane[:, 0:P], slice(0, HALF)
-            nc.tensor.matmul_mx(
-                out=acc[:],
-                lhsT=lhsT,
-                lhsT_scale=lhsT_scale,
-                rhs=strip_codes[:, cols].bitcast(E5M2X4),
-                rhs_scale=strip_plane[:, cols],
-                start=(a == W4),
-                stop=(a == W8),
-            )
+        quantize_dy(woven_a[:], 0, 0, P)
+        quantize_dy(woven_b[:], 0, P, QUART)
+        direct = bank(0)
+        mx_pass(direct[:, 0:QUART], weights(W4, 0, P), gradient(W4, 0, QUART), True, False)
+        mx_pass(direct[:, 0:P], weights(W8, 0, P), gradient(W8, 0, P), False, False)
+        mx_pass(direct[:, P:QUART], weights(W8, 0, P), gradient(W8, P, QUART), False, True)
+        parts1 = sums([0, 1], P, 2 * P, 2)
+        woven = weave_shared("w23", 3)
+        values = room_for(QUART, "values0")
+        nc.vector.tensor_tensor(values[:], direct[:, 0:QUART], wgo_wide[0][:], MULT)
+        quantize_w8(woven[:], QUART, HALF)
+        for i in (2, 3):
+            pages.append(slot([P, T], F32, "page%d" % i))
+            nc.gpsimd.memset(pages[i][:].bitcast(I32), 0)
+        scatter(0, values[:], 0, QUART)
 
-        accs = [bank(0), bank(1)]
-        direct = bank(2)
+        turned1 = turn(weigh(parts1, [0, 1], room_for(QUART, "weighed1")), [0], 4)
+        parts2 = sums([0, 1], 2 * P, 3 * P, 3)
+        parts3 = sums([0, 1], 3 * P, 4 * P, 6)
+        pair = woven_for("pair1", HALF)
+        round_and_weave(scopy, pair[:, QUART : QUART + P, :], raw["lo1a"][:])
+        values = room_for(QUART, "values1")
+        scopy(values[:], turned1)
+        scatter(1, values[:], 0, QUART)
+        turned2 = turn(weigh(parts2, [0, 1], room_for(QUART, "weighed2")), [0], 5)
+        turned3 = turn(weigh(parts3, [0, 1], room_for(QUART, "weighed3")), [0], 1)
+        round_and_weave(scopy, pair[:, QUART + P : HALF, :], raw["lo1b"][:])
+        values = room_for(QUART, "values2")
+        scopy(values[:], turned2)
+        scatter(2, values[:], 0, QUART)
+        round_and_weave(scopy, pair[:, 0:QUART, :], raw["hi1"][:])
+        quantize_dy(pair[:], 1, 0, HALF)
+        values = room_for(QUART, "values3", "raw_hi1")
+        scopy(values[:], turned3)
+        scatter(3, values[:], 0, QUART)
+
+        direct = bank(0)
         for a in (W4, W8):
-            strip_pass(direct, a)
-            for jt in range(2):
-                mm_pass(accs[jt], jt, 0, a)
-        weave((W4, 1), vcopy, "woven_first_1")
-        dx = slot([P, QUART], F32, "dx0_0")
-        nc.vector.tensor_tensor(dx[:], direct[:, QUART:HALF], wgo_first[:], MULT)
-        quantize((W4, 1))
-        place(dx, 0, [0])
+            mx_pass(direct[:, 0:QUART], weights(a, 0, P), gradient(a, QUART, HALF), a == W4, a == W8)
+        parts1 = sums([2, 3], P, 2 * P, 2)
+        parts23 = sums([2, 3], 2 * P, 4 * P, 3)
+        woven = {a: weave(name, scopy) for a, name in ((W4, "lo2"), (W8, "hi2"))}
+        values = room_for(QUART, "values4")
+        nc.vector.tensor_tensor(values[:], direct[:, 0:QUART], wgo_wide[1][:], MULT)
 
-        def late_page(tag):
-            pages.append(slot([P, T], F32, "page%d" % len(pages), tag))
-            nc.gpsimd.memset(pages[-1][:].bitcast(I32), 0)
+        def quantize_apart(a):
+            apart[a] = slot([P, QUART], U32, "codes2_%d" % a)
+            quantize(woven[a][:], apart[a][:], dy_plane[2][:, a * QUART : (a + 1) * QUART], E5M2X4)
 
-        turned = turn(weigh(0, accs, P, 2 * P, weights=wgo_head), [0], 4)
-        woven[W8, 1] = slot([P, QUART, PACK], BF16, "woven_second", "wgo_head")
-        round_and_weave(scopy, woven[W8, 1][:, 0:P, :], raw["second", 0][:])
-        round_and_weave(scopy, woven[W8, 1][:, P:QUART, :], raw["second", 1][:])
-        quantize((W8, 1))
-        late_page("wgo_head")
-        room = slot([P, 3 * QUART], F32, "room1", raw_tag(("second", 1)))
-        scopy(room[:, 0:QUART], turned)
-        place(room[:, 0:QUART], 0, [1])
-        for r in (2, 3):
-            scaled = weigh(0, accs, r * P, (r + 1) * P, room[:, (r - 1) * QUART : r * QUART])
-            place(copy_out(turn(scaled, [0], 3 + r), "dx0_%d" % r), 0, [r])
+        quantize_apart(W4)
+        scatter(0, values[:], QUART, HALF)
+        quantize_apart(W8)
+        turned = turn(weigh(parts1, [2, 3], room_for(QUART, "weighed5")), [0], 4)
+        values = room_for(QUART, "values5")
+        scopy(values[:], turned)
+        scatter(1, values[:], QUART, HALF)
+        tiles = weigh(parts23, [2, 3], room_for(HALF, "weighed67"))
+        for r in range(2):
+            values = room_for(QUART, "values%d" % (6 + r))
+            scopy(values[:], turn(tiles, [r], 5 + r))
+            scatter(2 + r, values[:], QUART, HALF)
 
-        prepare((W4, 2), raw_tag(("second", 1)))
-        accs = products([2, 3], 0, [4, 0])
-        turned = [turn(weigh(1, accs, r * P, (r + 1) * P), [0], 2 + r) for r in range(2)]
-        scaled = weigh(1, accs, QUART, HALF)
-        turned.extend(turn(scaled, [r], b) for r, b in enumerate((7, 1)))
-        place(copy_out(turned[0], "dx1_0", raw_tag((W4, 2))), 1, [0])
-        place(copy_out(turned[1], "dx1_1"), 1, [1])
-        prepare((W8, 2), "scaled2_2_128")
-        prepare((W4, 3), "scaled2_3_128")
-        room = slot([P, HALF], F32, "dx1_2", raw_tag((W8, 2)))
-        for r in (2, 3):
-            scopy(room[:, (r - 2) * QUART : (r - 1) * QUART], turned[r])
-        place(room, 1, [2, 3])
-        prepare((W8, 3), "scaled2_2_256")
-        rooms = {2: slot([P, 3 * QUART], F32, "room2", raw_tag((W8, 3)))}
-        late_tags = {2: raw_tag((W4, 3)), 3: None}
+        def quarter_sums(q, banks):
+            room = room_for(J, "weighed_q%d" % q)
+            jts = [2 * q, 2 * q + 1]
+            parts = [sums([jt], 0, HALF, b)[0] for jt, b in zip(jts, banks)]
+            tiles = [room[:, i * HALF : (i + 1) * HALF] for i in range(2)]
+            for lo, hi in ((0, P), (P, HALF)):
+                for tile, part, jt in zip(tiles, parts, jts):
+                    weigh([part[:, lo:hi]], [jt], tile[:, lo:hi])
+            return tiles
 
-        late = []
-        for q, sums, turns in ((2, [4, 0], [2, 3, 5]), (3, [2, 3], [5, 6, 7])):
-            accs = products([2 * q, 2 * q + 1], 0, sums)
-            room = rooms[q]
-            turned = [turn(weigh(q, accs, 0, P, room[:, 0:QUART]), [0], turns[0])]
-            scaled = weigh(q, accs, P, 3 * P, room[:, QUART : 3 * QUART])
-            turned.extend(turn(scaled, [r], turns[1 + r]) for r in range(2))
-            late_room = slot([P, QUART], F32, "late%d" % q, late_tags[q])
-            late.extend(weigh(q, accs, 3 * P, HALF, late_room[:]))
-            for r in range(2):
-                place(copy_out(turned[r], "dx%d_%d" % (q, r)), q, [r])
-            if q == 2:
-                prepare_pair([("w", 2), ("w", 3)], w8_codes[1][:], w8_plane[1][:], E4M3X4, raw_tag((W8, 3)))
-                rooms[3] = slot([P, 3 * QUART], F32, "room3", raw_tag(("w", 3)))
-                late_tags[3] = raw_tag((W4, 2))
-            place(copy_out(turned[2], "dx%d_2" % q, raw_tag(("w", 2)) if q == 2 else None), q, [2])
-        dx = copy_out(turn(late, [0], 1), "dx_late")
-        scatter(3, dx[:], d_part[3, HALF], HALF, J)
+        def place(tiles, q, rs, b):
+            values = room_for(QUART * len(rs), "values_%d_%d" % (q, rs[0]))
+            scopy(values[:], turn(tiles, rs, b))
+            for i, r in enumerate(rs):
+                scatter(r, values[:, i * QUART : (i + 1) * QUART], q * QUART, (q + 1) * QUART)
 
-        scaled = []
+        pair = woven_for("pair3", HALF)
+        for name, cols in (("lo3", slice(QUART, HALF)), ("hi3", slice(0, QUART))):
+            round_and_weave(scopy, pair[:, cols, :], raw[name][:])
+        quantize_dy(pair[:], 3, 0, HALF)
+        tiles = quarter_sums(2, [3, 5])
+        woven = weave("w45", scopy)
+        quantize_w8(woven[:], HALF, HALF + QUART)
+        for rs, b in (([0], 0), ([1], 2), ([2, 3], 1)):
+            place(tiles, 2, rs, b)
+
+        tiles = quarter_sums(3, [0, 2])
+        for rs, b in (([0, 1], 5), ([2, 3], 7)):
+            place(tiles, 3, rs, b)
+        woven = weave("w67", scopy)
+        quantize_w8(woven[:], HALF + QUART, N)
+
         for u in range(2):
-            scaled.append(weigh(2 * u, products(list(range(4 * u, 4 * u + 4)), 1, [4, 0, 5, 6]), 0, HALF))
-        for r in range(4):
-            dx = slot([P, J], F32, "dx_hi%d" % r)
-            for u in range(2):
-                scopy(dx[:, u * HALF : (u + 1) * HALF], turn(scaled[u], [r], (2, 3, 7, 1)[(2 * r + u) % 4]))
-            scatter(4 + r, dx[:], d_part[4 + r, 0], 0, J)
+            lo = HALF + u * QUART
+            tiles, room = [], room_for(4 * HALF, "weighed_hi%d" % u, "raw_w67" if u == 0 else None)
+            for i, b in enumerate((0, 2, 5, 7)):
+                jts = [2 * i, 2 * i + 1]
+                tiles.extend(weigh(sums(jts, lo, lo + QUART, b), jts, room[:, i * HALF : (i + 1) * HALF]))
+            for r in range(2):
+                values = room_for(J, "values_hi%d_%d" % (u, r))
+                for s in range(2):
+                    scopy(values[:, s * HALF : (s + 1) * HALF], turn(tiles[4 * s : 4 * s + 4], [r], (6, 1, 3, 4)[2 * r + s]))
+                scatter(4 + 2 * u + r, values[:], 0, J)

@@ -46,32 +46,41 @@ def tile_list_embg_qf_mul_kernel(tc, dy, w8, w4_words, w4_scales, d, wgo, offs, 
         laid = ctx.enter_context(tc.tile_pool(name="laid", bufs=1))
 
         places = {
-            "woven_pair3": 0,
-            "raw_hi2": 3584,
-            "weighed5": 3584,
-            "weighed67": 4096,
-            "raw_lo2": 40448,
-            "values4": 40448,
-            "woven_lo2": 48640,
-            "codes2_0": 48640,
-            "raw_hi3": 44544,
-            "weighed_q2": 44544,
-            "woven_w45": 46592,
-            "weighed_q3": 11264,
-            "woven_w67": 13312,
-            "raw_w23": 15360,
-            "values0": 15360,
-            "weighed1": 16384,
-            "values1": 18944,
-            "raw_lo1a": 19456,
-            "weighed2": 19968,
-            "weighed3": 20992,
-            "raw_lo1b": 22016,
-            "values2": 22016,
-            "page2": 24064,
-            "woven_w23": 31232,
-            "woven_hi0b": 31232,
-            "page3": 32256,
+            "raw_w23": 0,
+            "values0": 0,
+            "weighed23": 1536,
+            "woven_hi1": 1536,
+            "weighed1": 3072,
+            "woven_lo1b": 3584,
+            "wgo_head": 6144,
+            "woven_lo1a": 6144,
+            "woven_lo2": 10752,
+            "codes2_0": 10752,
+            "raw_hi1": 12288,
+            "values3": 12800,
+            "dy_codes1": 13824,
+            "woven_hi2": 15872,
+            "raw_lo2": 18432,
+            "values4": 18432,
+            "raw_hi2": 24576,
+            "values5": 24576,
+            "weighed67": 25600,
+            "woven_hi3": 25600,
+            "weighed5": 28160,
+            "woven_lo3": 28672,
+            "weighed_q2": 31232,
+            "raw_hi3": 31744,
+            "woven_w45": 32256,
+            "dy_codes3": 35328,
+            "weighed_q3": 37888,
+            "woven_w67": 39936,
+            "page2": 43008,
+            "woven_lo0": 49152,
+            "woven_w23": 50176,
+            "woven_hi0a": 50688,
+            "woven_w01": 51200,
+            "page3": 51200,
+            "woven_hi0b": 51712,
         }
 
         def slot(shape, dtype, name, tag=None):
@@ -87,7 +96,7 @@ def tile_list_embg_qf_mul_kernel(tc, dy, w8, w4_words, w4_scales, d, wgo, offs, 
         w4_codes = [slot([P, 2 * HALF], U8, "w4_codes%d" % h) for h in range(2)]
         w8_codes = [slot([P, HALF], U32, "w8_codes%d" % h) for h in range(2)]
         w8_plane = [slot([P, HALF], U8, "w8_plane%d" % h) for h in range(2)]
-        dy_codes = {q: slot([P, 2 * QUART], U32, "dy_codes%d" % q) for q in (0, 1, 3)}
+        dy_codes = {q: slot([P, 2 * QUART], U32, "dy_codes%d" % q) for q in (0,)}
         dy_plane = [slot([P, 2 * QUART], U8, "dy_plane%d" % q) for q in range(4)]
         apart = {}
         wgo_rows = slot([P, P], F32, "wgo_rows")
@@ -96,12 +105,12 @@ def tile_list_embg_qf_mul_kernel(tc, dy, w8, w4_words, w4_scales, d, wgo, offs, 
 
         raw = {}
 
-        def load_rows(name, rows):
-            raw[name] = slot([P, PACK, rows.shape[1]], F32, "raw_" + name)
-            nc.sync.dma_start(out=raw[name][:], in_=rows.rearrange("(p t) c -> p t c", t=PACK))
+        def load_rows(name, rows, lo, hi):
+            raw[name] = slot([P, PACK, hi - lo], F32, "raw_" + name)
+            nc.sync.dma_start(out=raw[name][:], in_=rows[:, lo:hi].rearrange("(p t) c -> p t c", t=PACK))
 
         def load_dy(name, a, lo, hi):
-            load_rows(name, dy[a * K_PASS : (a + 1) * K_PASS, lo:hi])
+            load_rows(name, dy[a * K_PASS : (a + 1) * K_PASS, :], lo, hi)
 
         def load_w4(h):
             nc.sync.dma_start(
@@ -115,12 +124,6 @@ def tile_list_embg_qf_mul_kernel(tc, dy, w8, w4_words, w4_scales, d, wgo, offs, 
             nc.sync.dma_start(out=tile[:], in_=d[r0 * P : r1 * P, lo:hi].rearrange("(r p) j -> p r j", p=P))
             for r in range(r0, r1):
                 d_part[r, lo] = tile[:, r - r0, :]
-
-        wgo_wide = {}
-
-        def load_wgo(q):
-            wgo_wide[q] = slot([P, QUART], F32, "wgo_wide%d" % q)
-            nc.sync.dma_start(out=wgo_wide[q][:], in_=wgo[:, q * QUART : (q + 1) * QUART])
 
         ones = slot([P, P], F32, "ones")
         quad_base = slot([P, 1], F32, "quad_base")
@@ -145,12 +148,10 @@ def tile_list_embg_qf_mul_kernel(tc, dy, w8, w4_words, w4_scales, d, wgo, offs, 
             )
         nc.sync.dma_start(out=wgo_rows[0 : J // P, :], in_=wgo[0].rearrange("(c p) -> c p", p=P))
         load_dy("lo0", W4, 0, QUART)
-        load_rows("w01", w8[:, 0:QUART])
+        load_rows("w01", w8, 0, QUART)
         load_w4(0)
-        load_dy("hi0a", W8, 0, P)
-        load_dy("hi0b", W8, P, QUART)
-        load_rows("w23", w8[:, QUART:HALF])
-        load_wgo(0)
+        load_dy("hi0", W8, 0, QUART)
+        load_rows("w23", w8, QUART, HALF)
         load_d(0, 1, 0, QUART)
         nc.sync.dma_start(offsets[:], offs)
         load_dy("lo1a", W4, QUART, QUART + P)
@@ -159,19 +160,17 @@ def tile_list_embg_qf_mul_kernel(tc, dy, w8, w4_words, w4_scales, d, wgo, offs, 
         load_d(2, 3, 0, QUART)
         load_dy("hi1", W8, QUART, HALF)
         load_d(3, 4, 0, QUART)
-        load_wgo(1)
         load_d(0, 1, QUART, HALF)
         load_dy("lo2", W4, HALF, HALF + QUART)
-        load_d(1, 2, QUART, HALF)
         load_dy("hi2", W8, HALF, HALF + QUART)
-        load_d(2, 4, QUART, HALF)
+        load_d(1, 4, QUART, HALF)
         load_dy("lo3", W4, HALF + QUART, J)
-        load_d(0, 4, HALF, HALF + QUART)
         load_dy("hi3", W8, HALF + QUART, J)
-        load_rows("w45", w8[:, HALF : HALF + QUART])
+        load_d(0, 4, HALF, HALF + QUART)
+        load_rows("w45", w8, HALF, HALF + QUART)
         load_w4(1)
         load_d(0, 4, HALF + QUART, J)
-        load_rows("w67", w8[:, HALF + QUART : N])
+        load_rows("w67", w8, HALF + QUART, N)
         for r in range(4, 8):
             load_d(r, r + 1, 0, J)
 
@@ -227,11 +226,11 @@ def tile_list_embg_qf_mul_kernel(tc, dy, w8, w4_words, w4_scales, d, wgo, offs, 
                     mx_pass(parts[i], gradient(a, jt * P, (jt + 1) * P), weights(a, lo, hi), first, last)
             return parts
 
-        def weigh(parts, jts, room):
+        def weigh(parts, jts, room, factors=None):
             width = parts[0].shape[1]
             tiles = [room[:, i * width : (i + 1) * width] for i in range(len(jts))]
             for tile, part, jt in zip(tiles, parts, jts):
-                nc.scalar.activation(out=tile, in_=part, func=COPY, scale=wgo_cols[:, jt : jt + 1])
+                nc.scalar.activation(out=tile, in_=part, func=COPY, scale=(wgo_cols if factors is None else factors)[:, jt : jt + 1])
             return tiles
 
         def turn(tiles, rs, b):
@@ -253,11 +252,20 @@ def tile_list_embg_qf_mul_kernel(tc, dy, w8, w4_words, w4_scales, d, wgo, offs, 
         wgo_turned = bank(7)
         nc.tensor.transpose(wgo_turned[:, 0:P], wgo_rows[:], ident[:])
         quantize_dy(weave_shared("lo0", 4)[:], 0, QUART, HALF)
-        quantize_w8(weave_shared("w01", 3)[:], 0, QUART)
-        woven_a = weave("hi0a", scopy)
-        woven_b = weave_shared("hi0b", 3)
-        wgo_cols = slot([P, J // P], F32, "wgo_cols", "raw_hi0b")
+        wgo_cols = slot([P, J // P], F32, "wgo_cols", "raw_lo0")
         scopy(wgo_cols[:], wgo_turned[:, 0 : J // P])
+        wgo_head = slot([P, 2], F32, "wgo_head")
+        scopy(wgo_head[:], wgo_turned[:, 0:2])
+        spread = bank(1)
+        for jt in range(4):
+            nc.tensor.transpose(spread[:, jt * P : (jt + 1) * P], wgo_cols[:, jt : jt + 1].to_broadcast([P, P]), ident[:])
+        quantize_w8(weave_shared("w01", 3)[:], 0, QUART)
+        wgo_wide = [slot([P, QUART], F32, "wgo_wide%d" % q, tag) for q, tag in enumerate(("raw_w01", "raw_hi0"))]
+        scopy(wgo_wide[0][:], spread[:, 0:QUART])
+        woven_a, woven_b = woven_for("hi0a", P), woven_for("hi0b", P)
+        round_and_weave(vcopy, woven_a[:], raw["hi0"][:, :, 0:P])
+        round_and_weave(scopy, woven_b[:], raw["hi0"][:, :, P:QUART])
+        scopy(wgo_wide[1][:], spread[:, QUART:HALF])
         quantize_dy(woven_a[:], 0, 0, P)
         quantize_dy(woven_b[:], 0, P, QUART)
         direct = bank(0)
@@ -274,23 +282,26 @@ def tile_list_embg_qf_mul_kernel(tc, dy, w8, w4_words, w4_scales, d, wgo, offs, 
             nc.gpsimd.memset(pages[i][:].bitcast(I32), 0)
         scatter(0, values[:], 0, QUART)
 
-        turned1 = turn(weigh(parts1, [0, 1], room_for(QUART, "weighed1")), [0], 4)
+        turned1 = turn(weigh(parts1, [0, 1], room_for(QUART, "weighed1"), wgo_head), [0], 4)
         parts2 = sums([0, 1], 2 * P, 3 * P, 3)
         parts3 = sums([0, 1], 3 * P, 4 * P, 6)
-        pair = woven_for("pair1", HALF)
-        round_and_weave(scopy, pair[:, QUART : QUART + P, :], raw["lo1a"][:])
+        woven_a = weave("lo1a", scopy)
         values = room_for(QUART, "values1")
         scopy(values[:], turned1)
         scatter(1, values[:], 0, QUART)
-        turned2 = turn(weigh(parts2, [0, 1], room_for(QUART, "weighed2")), [0], 5)
-        turned3 = turn(weigh(parts3, [0, 1], room_for(QUART, "weighed3")), [0], 1)
-        round_and_weave(scopy, pair[:, QUART + P : HALF, :], raw["lo1b"][:])
+        room = room_for(HALF, "weighed23")
+        turned2 = turn(weigh(parts2, [0, 1], room[:, 0:QUART]), [0], 5)
+        turned3 = turn(weigh(parts3, [0, 1], room[:, QUART:HALF]), [0], 1)
+        woven_b = weave("lo1b", scopy)
         values = room_for(QUART, "values2")
         scopy(values[:], turned2)
         scatter(2, values[:], 0, QUART)
-        round_and_weave(scopy, pair[:, 0:QUART, :], raw["hi1"][:])
-        quantize_dy(pair[:], 1, 0, HALF)
-        values = room_for(QUART, "values3", "raw_hi1")
+        woven = weave("hi1", scopy)
+        dy_codes[1] = slot([P, 2 * QUART], U32, "dy_codes1")
+        quantize_dy(woven_a[:], 1, QUART, QUART + P)
+        quantize_dy(woven_b[:], 1, QUART + P, HALF)
+        quantize_dy(woven[:], 1, 0, QUART)
+        values = room_for(QUART, "values3")
         scopy(values[:], turned3)
         scatter(3, values[:], 0, QUART)
 
@@ -299,7 +310,7 @@ def tile_list_embg_qf_mul_kernel(tc, dy, w8, w4_words, w4_scales, d, wgo, offs, 
             mx_pass(direct[:, 0:QUART], weights(a, 0, P), gradient(a, QUART, HALF), a == W4, a == W8)
         parts1 = sums([2, 3], P, 2 * P, 2)
         parts23 = sums([2, 3], 2 * P, 4 * P, 3)
-        woven = {a: weave(name, scopy) for a, name in ((W4, "lo2"), (W8, "hi2"))}
+        woven = {W4: weave("lo2", scopy)}
         values = room_for(QUART, "values4")
         nc.vector.tensor_tensor(values[:], direct[:, 0:QUART], wgo_wide[1][:], MULT)
 
@@ -309,12 +320,13 @@ def tile_list_embg_qf_mul_kernel(tc, dy, w8, w4_words, w4_scales, d, wgo, offs, 
 
         quantize_apart(W4)
         scatter(0, values[:], QUART, HALF)
+        woven[W8] = weave("hi2", scopy)
         quantize_apart(W8)
         turned = turn(weigh(parts1, [2, 3], room_for(QUART, "weighed5")), [0], 4)
+        tiles = weigh(parts23, [2, 3], room_for(HALF, "weighed67"))
         values = room_for(QUART, "values5")
         scopy(values[:], turned)
         scatter(1, values[:], QUART, HALF)
-        tiles = weigh(parts23, [2, 3], room_for(HALF, "weighed67"))
         for r in range(2):
             values = room_for(QUART, "values%d" % (6 + r))
             scopy(values[:], turn(tiles, [r], 5 + r))
@@ -336,10 +348,10 @@ def tile_list_embg_qf_mul_kernel(tc, dy, w8, w4_words, w4_scales, d, wgo, offs, 
             for i, r in enumerate(rs):
                 scatter(r, values[:, i * QUART : (i + 1) * QUART], q * QUART, (q + 1) * QUART)
 
-        pair = woven_for("pair3", HALF)
-        for name, cols in (("lo3", slice(QUART, HALF)), ("hi3", slice(0, QUART))):
-            round_and_weave(scopy, pair[:, cols, :], raw[name][:])
-        quantize_dy(pair[:], 3, 0, HALF)
+        woven = {a: weave(name, scopy) for a, name in ((W4, "lo3"), (W8, "hi3"))}
+        dy_codes[3] = slot([P, 2 * QUART], U32, "dy_codes3")
+        for a in (W4, W8):
+            quantize_dy(woven[a][:], 3, a * QUART, (a + 1) * QUART)
         tiles = quarter_sums(2, [3, 5])
         woven = weave("w45", scopy)
         quantize_w8(woven[:], HALF, HALF + QUART)

@@ -74,7 +74,6 @@ def tile_list_embg_qf_mul_kernel(tc, dy, w8, w4_words, w4_scales, d, wgo, offs, 
             "dy_codes3": 35328,
             "weighed_q3": 37888,
             "woven_w67": 39936,
-            "page2": 43008,
             "woven_lo0": 49152,
             "woven_w23": 50176,
             "woven_hi0a": 50688,
@@ -101,7 +100,7 @@ def tile_list_embg_qf_mul_kernel(tc, dy, w8, w4_words, w4_scales, d, wgo, offs, 
         apart = {}
         wgo_rows = slot([P, P], F32, "wgo_rows")
         ident = slot([P, P], F32, "ident")
-        pages = [slot([P, T], F32, "page%d" % i) for i in range(2)]
+        pages = [slot([P, T], F32, "page%d" % i) for i in range(PAGES - 1)]
 
         raw = {}
 
@@ -138,22 +137,24 @@ def tile_list_embg_qf_mul_kernel(tc, dy, w8, w4_words, w4_scales, d, wgo, offs, 
         lane = slot([P, 32], F32, "lane")
         nc.vector.transpose(lane[:], count[:])
         nc.vector.tensor_tensor(ident[:], shifted[:], lane[:, 0:1].to_broadcast([P, P]), EQUAL)
-        nc.vector.memset(pages[0][:].bitcast(I32), 0)
+        for page, lo, hi in ((0, 0, 1023), (0, 1023, T), (2, 0, 255), (2, 255, 512)):
+            nc.vector.memset(pages[page][:, lo:hi].bitcast(I32), 0)
         nc.gpsimd.memset(pages[1][:].bitcast(I32), 0)
+        nc.gpsimd.memset(pages[2][:, 512:T].bitcast(I32), 0)
 
         for quad in range(4):
             nc.scalar.dma_start(
                 out=w4_plane[32 * quad : 32 * quad + 4, :].bitcast(I32),
                 in_=w4_scales[0][4 * quad : 4 * quad + 4, :].bitcast(I32),
             )
-        nc.sync.dma_start(out=wgo_rows[0 : J // P, :], in_=wgo[0].rearrange("(c p) -> c p", p=P))
         load_dy("lo0", W4, 0, QUART)
+        nc.sync.dma_start(out=wgo_rows[0 : J // P, :], in_=wgo[0].rearrange("(c p) -> c p", p=P))
         load_rows("w01", w8, 0, QUART)
-        load_w4(0)
         load_dy("hi0", W8, 0, QUART)
+        nc.sync.dma_start(offsets[:], offs)
+        load_w4(0)
         load_rows("w23", w8, QUART, HALF)
         load_d(0, 1, 0, QUART)
-        nc.sync.dma_start(offsets[:], offs)
         load_dy("lo1a", W4, QUART, QUART + P)
         load_d(1, 2, 0, QUART)
         load_dy("lo1b", W4, QUART + P, HALF)
@@ -251,7 +252,7 @@ def tile_list_embg_qf_mul_kernel(tc, dy, w8, w4_words, w4_scales, d, wgo, offs, 
 
         wgo_turned = bank(7)
         nc.tensor.transpose(wgo_turned[:, 0:P], wgo_rows[:], ident[:])
-        quantize_dy(weave_shared("lo0", 4)[:], 0, QUART, HALF)
+        quantize_dy(weave_shared("lo0", 5)[:], 0, QUART, HALF)
         wgo_cols = slot([P, J // P], F32, "wgo_cols", "raw_lo0")
         scopy(wgo_cols[:], wgo_turned[:, 0 : J // P])
         wgo_head = slot([P, 2], F32, "wgo_head")
@@ -277,9 +278,8 @@ def tile_list_embg_qf_mul_kernel(tc, dy, w8, w4_words, w4_scales, d, wgo, offs, 
         values = room_for(QUART, "values0")
         nc.vector.tensor_tensor(values[:], direct[:, 0:QUART], wgo_wide[0][:], MULT)
         quantize_w8(woven[:], QUART, HALF)
-        for i in (2, 3):
-            pages.append(slot([P, T], F32, "page%d" % i))
-            nc.gpsimd.memset(pages[i][:].bitcast(I32), 0)
+        pages.append(slot([P, T], F32, "page3"))
+        nc.gpsimd.memset(pages[3][:].bitcast(I32), 0)
         scatter(0, values[:], 0, QUART)
 
         turned1 = turn(weigh(parts1, [0, 1], room_for(QUART, "weighed1"), wgo_head), [0], 4)

@@ -20,12 +20,36 @@ ADD = mybir.AluOpType.add
 EQUAL = mybir.AluOpType.is_equal
 
 P = 128
+GROUP = 32
 PACK = 4
 K_PASS = P * PACK
 HALF = 512
 QUART = 256
 PAGES = 4
 W8, W4 = 0, 1
+PAGE2_ON_VECTOR = 512
+
+STEP = 512
+REUSE = (
+    (20, {"woven_dy4_q0": 0, "woven_dy8_q0a": 3, "woven_w8_r01": 4, "woven_dy8_q0b": 5, "woven_w8_r2": 4,
+          "woven_w8_r3": 6, "page3": 4}),
+    (2, {"wgo_first": 0, "woven_dy4_q1a": 0}),
+    (6, {"raw_dy4_q1a": 2, "weighed_q0_r23": 0, "woven_dy4_q1b": 4, "woven_dy8_q1": 0}),
+    (14, {"raw_dy8_q1": 3, "woven_dy4_q2": 0, "values_q0_r3": 4, "codes_q1": 6, "woven_dy8_q2": 10, "codes_dy8_q2": 0}),
+    (8, {"raw_dy4_q2": 0, "values_q1_r0": 0}),
+    (12, {"raw_dy8_q2": 0, "values_q1_r1": 0, "weighed_q1_r23": 2, "weighed_q1_r1": 7, "woven_dy4_q3": 8,
+          "woven_dy8_q3": 2}),
+    (12, {"raw_dy8_q3": 1, "weighed_q2": 0, "codes_q3": 8, "woven_w8_r45": 2}),
+    (8, {"weighed_q3": 0, "woven_w8_r67": 4}),
+)
+
+
+def reuse_offsets():
+    offsets, base = {}, 0
+    for length, starts in REUSE:
+        offsets.update({name: (base + start) * STEP for name, start in starts.items()})
+        base += length
+    return offsets
 
 
 def round_and_weave(engine_copy, woven, raw):
@@ -39,53 +63,17 @@ def tile_list_embg_qf_mul_kernel(tc, dy, w8, w4_words, w4_scales, d, wgo, offs, 
     nc = tc.nc
     vcopy = nc.vector.tensor_copy
     scopy = nc.scalar.copy
+    places = reuse_offsets()
 
     with ExitStack() as ctx:
         keep = ctx.enter_context(tc.tile_pool(name="keep", bufs=1))
         psum = ctx.enter_context(tc.psum_pool(name="psum", bufs=1))
         laid = ctx.enter_context(tc.tile_pool(name="laid", bufs=1))
 
-        places = {
-            "raw_w23": 0,
-            "values0": 0,
-            "weighed23": 1536,
-            "woven_hi1": 1536,
-            "weighed1": 3072,
-            "woven_lo1b": 3584,
-            "wgo_head": 6144,
-            "woven_lo1a": 6144,
-            "woven_lo2": 10752,
-            "codes2_0": 10752,
-            "raw_hi1": 12288,
-            "values3": 12800,
-            "dy_codes1": 13824,
-            "woven_hi2": 15872,
-            "raw_lo2": 18432,
-            "values4": 18432,
-            "raw_hi2": 24576,
-            "values5": 24576,
-            "weighed67": 25600,
-            "woven_hi3": 25600,
-            "weighed5": 28160,
-            "woven_lo3": 28672,
-            "weighed_q2": 31232,
-            "raw_hi3": 31744,
-            "woven_w45": 32256,
-            "dy_codes3": 35328,
-            "weighed_q3": 37888,
-            "woven_w67": 39936,
-            "woven_lo0": 49152,
-            "woven_w23": 50176,
-            "woven_hi0a": 50688,
-            "woven_w01": 51200,
-            "page3": 51200,
-            "woven_hi0b": 51712,
-        }
-
-        def slot(shape, dtype, name, tag=None):
+        def slot(shape, dtype, name, behind=None):
             if name in places:
                 return laid.tile(shape, dtype, name=name, offset=places[name], align_bytes=64)
-            return keep.tile(shape, dtype, name=name, tag=tag or name, align_bytes=64)
+            return keep.tile(shape, dtype, name=name, tag=behind or name, align_bytes=64)
 
         def bank(b):
             return psum.tile([P, HALF], F32, name="bank%d" % b)
@@ -95,14 +83,13 @@ def tile_list_embg_qf_mul_kernel(tc, dy, w8, w4_words, w4_scales, d, wgo, offs, 
         w4_codes = [slot([P, 2 * HALF], U8, "w4_codes%d" % h) for h in range(2)]
         w8_codes = [slot([P, HALF], U32, "w8_codes%d" % h) for h in range(2)]
         w8_plane = [slot([P, HALF], U8, "w8_plane%d" % h) for h in range(2)]
-        dy_codes = {q: slot([P, 2 * QUART], U32, "dy_codes%d" % q) for q in (0,)}
+        codes_q0 = slot([P, 2 * QUART], U32, "codes_q0")
+        dy_codes = {(a, 0): codes_q0[:, a * QUART : (a + 1) * QUART] for a in (W8, W4)}
         dy_plane = [slot([P, 2 * QUART], U8, "dy_plane%d" % q) for q in range(4)]
-        apart = {}
         wgo_rows = slot([P, P], F32, "wgo_rows")
         ident = slot([P, P], F32, "ident")
         pages = [slot([P, T], F32, "page%d" % i) for i in range(PAGES - 1)]
-
-        raw = {}
+        raw, d_part = {}, {}
 
         def load_rows(name, rows, lo, hi):
             raw[name] = slot([P, PACK, hi - lo], F32, "raw_" + name)
@@ -116,8 +103,6 @@ def tile_list_embg_qf_mul_kernel(tc, dy, w8, w4_words, w4_scales, d, wgo, offs, 
                 out=w4_codes[h][:].bitcast(I32), in_=w4_words[0][:, 2 * HALF * h : 2 * HALF * (h + 1)].bitcast(I32)
             )
 
-        d_part = {}
-
         def load_d(r0, r1, lo, hi):
             tile = slot([P, r1 - r0, hi - lo], F32, "d_%d_%d" % (r0, lo))
             nc.sync.dma_start(out=tile[:], in_=d[r0 * P : r1 * P, lo:hi].rearrange("(r p) j -> p r j", p=P))
@@ -125,81 +110,90 @@ def tile_list_embg_qf_mul_kernel(tc, dy, w8, w4_words, w4_scales, d, wgo, offs, 
                 d_part[r, lo] = tile[:, r - r0, :]
 
         ones = slot([P, P], F32, "ones")
-        quad_base = slot([P, 1], F32, "quad_base")
+        group_start = slot([P, 1], F32, "group_start")
         nc.vector.memset(ones[:, 0 : P - 1], 1.0)
         nc.vector.memset(ones[:, P - 1 : P], 1.0)
-        for quad in range(4):
-            nc.vector.memset(quad_base[32 * quad : 32 * quad + 32, :], -32.0 * quad)
-        count = slot([P, 32], F32, "count")
-        nc.vector.tensor_tensor_scan(count[:], ones[:, 0:32], ones[:, 0:32], 0.0, MULT, ADD)
-        shifted = slot([P, P], F32, "shifted")
-        nc.vector.tensor_tensor_scan(shifted[:], ones[:], ones[:], quad_base[:], MULT, ADD)
-        lane = slot([P, 32], F32, "lane")
+        for g in range(P // GROUP):
+            nc.vector.memset(group_start[GROUP * g : GROUP * (g + 1), :], -float(GROUP * g))
+        count = slot([P, GROUP], F32, "count")
+        nc.vector.tensor_tensor_scan(count[:], ones[:, 0:GROUP], ones[:, 0:GROUP], 0.0, MULT, ADD)
+        column = slot([P, P], F32, "column")
+        nc.vector.tensor_tensor_scan(column[:], ones[:], ones[:], group_start[:], MULT, ADD)
+        lane = slot([P, GROUP], F32, "lane")
         nc.vector.transpose(lane[:], count[:])
-        nc.vector.tensor_tensor(ident[:], shifted[:], lane[:, 0:1].to_broadcast([P, P]), EQUAL)
-        for page, lo, hi in ((0, 0, 1023), (0, 1023, T), (2, 0, 255), (2, 255, 512)):
-            nc.vector.memset(pages[page][:, lo:hi].bitcast(I32), 0)
-        nc.gpsimd.memset(pages[1][:].bitcast(I32), 0)
-        nc.gpsimd.memset(pages[2][:, 512:T].bitcast(I32), 0)
+        nc.vector.tensor_tensor(ident[:], column[:], lane[:, 0:1].to_broadcast([P, P]), EQUAL)
 
-        for quad in range(4):
+        for page, width in ((0, T), (2, PAGE2_ON_VECTOR)):
+            for lo, hi in ((0, width // 2 - 1), (width // 2 - 1, width)):
+                nc.vector.memset(pages[page][:, lo:hi].bitcast(I32), 0)
+        nc.gpsimd.memset(pages[1][:].bitcast(I32), 0)
+        nc.gpsimd.memset(pages[2][:, PAGE2_ON_VECTOR:T].bitcast(I32), 0)
+
+        for g in range(P // GROUP):
             nc.scalar.dma_start(
-                out=w4_plane[32 * quad : 32 * quad + 4, :].bitcast(I32),
-                in_=w4_scales[0][4 * quad : 4 * quad + 4, :].bitcast(I32),
+                out=w4_plane[GROUP * g : GROUP * g + 4, :].bitcast(I32),
+                in_=w4_scales[0][4 * g : 4 * g + 4, :].bitcast(I32),
             )
-        load_dy("lo0", W4, 0, QUART)
+        load_dy("dy4_q0", W4, 0, QUART)
         nc.sync.dma_start(out=wgo_rows[0 : J // P, :], in_=wgo[0].rearrange("(c p) -> c p", p=P))
-        load_rows("w01", w8, 0, QUART)
-        load_dy("hi0", W8, 0, QUART)
+        load_rows("w8_r01", w8, 0, QUART)
+        load_dy("dy8_q0", W8, 0, QUART)
         nc.sync.dma_start(offsets[:], offs)
         load_w4(0)
-        load_rows("w23", w8, QUART, HALF)
+        first = slot([P, P + PACK * QUART], F32, "first")
+        raw_w8_r23 = first[:, P:].rearrange("p (t c) -> p t c", t=PACK)
+        nc.sync.dma_start(out=raw_w8_r23, in_=w8[:, QUART:HALF].rearrange("(p t) c -> p t c", t=PACK))
         load_d(0, 1, 0, QUART)
-        load_dy("lo1a", W4, QUART, QUART + P)
+        load_dy("dy4_q1a", W4, QUART, QUART + P)
         load_d(1, 2, 0, QUART)
-        load_dy("lo1b", W4, QUART + P, HALF)
+        load_dy("dy4_q1b", W4, QUART + P, HALF)
         load_d(2, 3, 0, QUART)
-        load_dy("hi1", W8, QUART, HALF)
+        load_dy("dy8_q1", W8, QUART, HALF)
         load_d(3, 4, 0, QUART)
         load_d(0, 1, QUART, HALF)
-        load_dy("lo2", W4, HALF, HALF + QUART)
-        load_dy("hi2", W8, HALF, HALF + QUART)
+        load_dy("dy4_q2", W4, HALF, HALF + QUART)
+        load_dy("dy8_q2", W8, HALF, HALF + QUART)
         load_d(1, 4, QUART, HALF)
-        load_dy("lo3", W4, HALF + QUART, J)
-        load_dy("hi3", W8, HALF + QUART, J)
+        load_dy("dy4_q3", W4, HALF + QUART, J)
+        load_dy("dy8_q3", W8, HALF + QUART, J)
         load_d(0, 4, HALF, HALF + QUART)
-        load_rows("w45", w8, HALF, HALF + QUART)
+        load_rows("w8_r45", w8, HALF, HALF + QUART)
         load_w4(1)
         load_d(0, 4, HALF + QUART, J)
-        load_rows("w67", w8, HALF + QUART, N)
-        for r in range(4, 8):
+        load_rows("w8_r67", w8, HALF + QUART, N)
+        for r in range(PAGES, 2 * PAGES):
             load_d(r, r + 1, 0, J)
 
-        def woven_for(name, width):
-            return slot([P, width, PACK], BF16, "woven_" + name)
+        def weave(name, source, engine_copy):
+            woven = slot([P, source.shape[2], PACK], BF16, "woven_" + name)
+            round_and_weave(engine_copy, woven[:], source)
+            return woven
+
+        def weave_shared(name, eighths):
+            width = raw[name].shape[2]
+            split = eighths * width // 8
+            woven = slot([P, width, PACK], BF16, "woven_" + name)
+            for engine_copy, cols in ((scopy, slice(0, split)), (vcopy, slice(split, width))):
+                round_and_weave(engine_copy, woven[:, cols, :], raw[name][:, :, cols])
+            return woven
 
         def quantize(woven, codes, plane, fmt):
-            nc.vector.quantize_mx(out=codes.bitcast(fmt), scales=plane, in_=woven.rearrange("p c t -> p (c t)"))
+            nc.vector.quantize_mx(out=codes.bitcast(fmt), scales=plane, in_=woven[:].rearrange("p c t -> p (c t)"))
 
-        def quantize_dy(woven, q, lo, hi):
-            quantize(woven, dy_codes[q][:, lo:hi], dy_plane[q][:, lo:hi], E5M2X4)
+        def dy_operand(a, lo, hi):
+            q, c0, c1 = lo // QUART, lo % QUART, lo % QUART + hi - lo
+            return dy_codes[a, q][:, c0:c1], dy_plane[q][:, a * QUART + c0 : a * QUART + c1]
+
+        def quantize_dy(woven, a, lo, hi):
+            quantize(woven, *dy_operand(a, lo, hi), E5M2X4)
 
         def quantize_w8(woven, lo, hi):
             h, cols = lo // HALF, slice(lo % HALF, lo % HALF + hi - lo)
             quantize(woven, w8_codes[h][:, cols], w8_plane[h][:, cols], E4M3X4)
 
-        def weave_shared(name, eighths):
-            width = raw[name].shape[2]
-            split = eighths * width // 8
-            woven = woven_for(name, width)
-            for engine_copy, cols in ((scopy, slice(0, split)), (vcopy, slice(split, width))):
-                round_and_weave(engine_copy, woven[:, cols, :], raw[name][:, :, cols])
-            return woven
-
-        def weave(name, engine_copy):
-            woven = woven_for(name, raw[name].shape[2])
-            round_and_weave(engine_copy, woven[:], raw[name][:])
-            return woven
+        def new_codes(q):
+            codes = slot([P, 2 * QUART], U32, "codes_q%d" % q)
+            dy_codes.update({(a, q): codes[:, a * QUART : (a + 1) * QUART] for a in (W8, W4)})
 
         def weights(a, lo, hi):
             h, c0, c1 = lo // HALF, lo % HALF, lo % HALF + hi - lo
@@ -208,10 +202,8 @@ def tile_list_embg_qf_mul_kernel(tc, dy, w8, w4_words, w4_scales, d, wgo, offs, 
             return w4_codes[h][:, 2 * c0 : 2 * c1].bitcast(E2M1X4), w4_plane[:, lo:hi]
 
         def gradient(a, lo, hi):
-            q = lo // QUART
-            cols = slice(a * QUART + lo % QUART, a * QUART + lo % QUART + hi - lo)
-            codes = apart[a][:, lo % QUART : lo % QUART + hi - lo] if q == 2 else dy_codes[q][:, cols]
-            return codes.bitcast(E5M2X4), dy_plane[q][:, cols]
+            codes, plane = dy_operand(a, lo, hi)
+            return codes.bitcast(E5M2X4), plane
 
         def mx_pass(acc, still, moving, start, stop):
             nc.tensor.matmul_mx(
@@ -223,26 +215,26 @@ def tile_list_embg_qf_mul_kernel(tc, dy, w8, w4_words, w4_scales, d, wgo, offs, 
             parts = [acc[:, i * width : (i + 1) * width] for i in range(len(jts))]
             for a in (W4, W8):
                 for i, jt in enumerate(jts):
-                    first, last = (a == W4 and i == 0), (a == W8 and i == len(jts) - 1)
-                    mx_pass(parts[i], gradient(a, jt * P, (jt + 1) * P), weights(a, lo, hi), first, last)
+                    start, stop = (a == W4 and i == 0), (a == W8 and i == len(jts) - 1)
+                    mx_pass(parts[i], gradient(a, jt * P, (jt + 1) * P), weights(a, lo, hi), start, stop)
             return parts
 
-        def weigh(parts, jts, room, factors=None):
+        def weigh(parts, jts, room, factors):
             width = parts[0].shape[1]
             tiles = [room[:, i * width : (i + 1) * width] for i in range(len(jts))]
             for tile, part, jt in zip(tiles, parts, jts):
-                nc.scalar.activation(out=tile, in_=part, func=COPY, scale=(wgo_cols if factors is None else factors)[:, jt : jt + 1])
+                nc.scalar.activation(out=tile, in_=part, func=COPY, scale=factors[:, jt : jt + 1])
             return tiles
 
-        def turn(tiles, rs, b):
+        def turn(tiles, blocks_wanted, b):
             turned = bank(b)
-            blocks = [tile[:, r * P : (r + 1) * P] for r in rs for tile in tiles]
+            blocks = [tile[:, i * P : (i + 1) * P] for i in blocks_wanted for tile in tiles]
             for i, block in enumerate(blocks):
                 nc.tensor.transpose(turned[:, i * P : (i + 1) * P], block, ident[:])
             return turned[:, 0 : P * len(blocks)]
 
-        def room_for(width, name, tag=None):
-            return slot([P, width], F32, name, tag)
+        def room_for(width, name, behind=None):
+            return slot([P, width], F32, name, behind)
 
         def scatter(r, values, lo, hi):
             window = pages[r % PAGES][:].indirect(offsets[:, lo // 16 : hi // 16])
@@ -250,87 +242,82 @@ def tile_list_embg_qf_mul_kernel(tc, dy, w8, w4_words, w4_scales, d, wgo, offs, 
             if hi == J:
                 nc.sync.dma_start(out=out[r * P : (r + 1) * P, :], in_=pages[r % PAGES][:])
 
+        def copy_and_scatter(turned, q, rs):
+            values = room_for(QUART * len(rs), "values_q%d_r%s" % (q, "".join(str(r) for r in rs)))
+            scopy(values[:], turned)
+            for i, r in enumerate(rs):
+                scatter(r, values[:, i * QUART : (i + 1) * QUART], q * QUART, (q + 1) * QUART)
+
         wgo_turned = bank(7)
         nc.tensor.transpose(wgo_turned[:, 0:P], wgo_rows[:], ident[:])
-        quantize_dy(weave_shared("lo0", 5)[:], 0, QUART, HALF)
-        wgo_cols = slot([P, J // P], F32, "wgo_cols", "raw_lo0")
+        quantize_dy(weave_shared("dy4_q0", 5), W4, 0, QUART)
+        wgo_cols = slot([P, J // P], F32, "wgo_cols", "raw_dy4_q0")
         scopy(wgo_cols[:], wgo_turned[:, 0 : J // P])
-        wgo_head = slot([P, 2], F32, "wgo_head")
-        scopy(wgo_head[:], wgo_turned[:, 0:2])
+        wgo_first = slot([P, 2], F32, "wgo_first")
+        scopy(wgo_first[:], wgo_turned[:, 0:2])
         spread = bank(1)
-        for jt in range(4):
+        for jt in range(HALF // P):
             nc.tensor.transpose(spread[:, jt * P : (jt + 1) * P], wgo_cols[:, jt : jt + 1].to_broadcast([P, P]), ident[:])
-        quantize_w8(weave_shared("w01", 3)[:], 0, QUART)
-        wgo_wide = [slot([P, QUART], F32, "wgo_wide%d" % q, tag) for q, tag in enumerate(("raw_w01", "raw_hi0"))]
+        quantize_w8(weave_shared("w8_r01", 3), 0, QUART)
+        wgo_wide = [room_for(QUART, "wgo_wide%d" % q, name) for q, name in enumerate(("raw_w8_r01", "raw_dy8_q0"))]
         scopy(wgo_wide[0][:], spread[:, 0:QUART])
-        woven_a, woven_b = woven_for("hi0a", P), woven_for("hi0b", P)
-        round_and_weave(vcopy, woven_a[:], raw["hi0"][:, :, 0:P])
-        round_and_weave(scopy, woven_b[:], raw["hi0"][:, :, P:QUART])
+        woven_a = weave("dy8_q0a", raw["dy8_q0"][:, :, 0:P], vcopy)
+        woven_b = weave("dy8_q0b", raw["dy8_q0"][:, :, P:QUART], scopy)
         scopy(wgo_wide[1][:], spread[:, QUART:HALF])
-        quantize_dy(woven_a[:], 0, 0, P)
-        quantize_dy(woven_b[:], 0, P, QUART)
-        direct = bank(0)
-        mx_pass(direct[:, 0:QUART], weights(W4, 0, P), gradient(W4, 0, QUART), True, False)
-        mx_pass(direct[:, 0:P], weights(W8, 0, P), gradient(W8, 0, P), False, False)
-        mx_pass(direct[:, P:QUART], weights(W8, 0, P), gradient(W8, P, QUART), False, True)
-        parts1 = sums([0, 1], P, 2 * P, 2)
-        woven = weave_shared("w23", 3)
-        values = room_for(QUART, "values0")
-        nc.vector.tensor_tensor(values[:], direct[:, 0:QUART], wgo_wide[0][:], MULT)
-        quantize_w8(woven[:], QUART, HALF)
+        quantize_dy(woven_a, W8, 0, P)
+        quantize_dy(woven_b, W8, P, QUART)
+        direct = [bank(0), bank(4)]
+        for a in (W4, W8):
+            for jt in range(2):
+                mx_pass(direct[jt][:, 0:P], weights(a, 0, P), gradient(a, jt * P, (jt + 1) * P), a == W4, a == W8)
+        parts_r1 = sums([0, 1], P, 2 * P, 2)
+        woven_a = weave("w8_r2", raw_w8_r23[:, :, 0:P], vcopy)
+        woven_b = weave("w8_r3", raw_w8_r23[:, :, P:QUART], scopy)
+        for jt in range(2):
+            cols = slice(jt * P, (jt + 1) * P)
+            nc.vector.tensor_tensor(first[:, cols], direct[jt][:, 0:P], wgo_wide[0][:, cols], MULT)
+        quantize_w8(woven_a, 2 * P, 3 * P)
+        quantize_w8(woven_b, 3 * P, 4 * P)
         pages.append(slot([P, T], F32, "page3"))
         nc.gpsimd.memset(pages[3][:].bitcast(I32), 0)
-        scatter(0, values[:], 0, QUART)
+        scatter(0, first[:, 0:QUART], 0, QUART)
 
-        turned1 = turn(weigh(parts1, [0, 1], room_for(QUART, "weighed1"), wgo_head), [0], 4)
-        parts2 = sums([0, 1], 2 * P, 3 * P, 3)
-        parts3 = sums([0, 1], 3 * P, 4 * P, 6)
-        woven_a = weave("lo1a", scopy)
-        values = room_for(QUART, "values1")
-        scopy(values[:], turned1)
-        scatter(1, values[:], 0, QUART)
-        room = room_for(HALF, "weighed23")
-        turned2 = turn(weigh(parts2, [0, 1], room[:, 0:QUART]), [0], 5)
-        turned3 = turn(weigh(parts3, [0, 1], room[:, QUART:HALF]), [0], 1)
-        woven_b = weave("lo1b", scopy)
-        values = room_for(QUART, "values2")
-        scopy(values[:], turned2)
-        scatter(2, values[:], 0, QUART)
-        woven = weave("hi1", scopy)
-        dy_codes[1] = slot([P, 2 * QUART], U32, "dy_codes1")
-        quantize_dy(woven_a[:], 1, QUART, QUART + P)
-        quantize_dy(woven_b[:], 1, QUART + P, HALF)
-        quantize_dy(woven[:], 1, 0, QUART)
-        values = room_for(QUART, "values3")
-        scopy(values[:], turned3)
-        scatter(3, values[:], 0, QUART)
+        turned_r1 = turn(weigh(parts_r1, [0, 1], first[:, P + 3 * QUART :], wgo_first), [0], 4)
+        parts_r2 = sums([0, 1], 2 * P, 3 * P, 3)
+        parts_r3 = sums([0, 1], 3 * P, 4 * P, 6)
+        woven_a = weave("dy4_q1a", raw["dy4_q1a"][:], scopy)
+        copy_and_scatter(turned_r1, 0, [1])
+        room = room_for(HALF, "weighed_q0_r23")
+        turned_r2 = turn(weigh(parts_r2, [0, 1], room[:, 0:QUART], wgo_cols), [0], 5)
+        turned_r3 = turn(weigh(parts_r3, [0, 1], room[:, QUART:HALF], wgo_cols), [0], 1)
+        woven_b = weave("dy4_q1b", raw["dy4_q1b"][:], scopy)
+        copy_and_scatter(turned_r2, 0, [2])
+        woven = weave("dy8_q1", raw["dy8_q1"][:], scopy)
+        new_codes(1)
+        quantize_dy(woven_a, W4, QUART, QUART + P)
+        quantize_dy(woven_b, W4, QUART + P, HALF)
+        quantize_dy(woven, W8, QUART, HALF)
+        copy_and_scatter(turned_r3, 0, [3])
 
         direct = bank(0)
         for a in (W4, W8):
             mx_pass(direct[:, 0:QUART], weights(a, 0, P), gradient(a, QUART, HALF), a == W4, a == W8)
-        parts1 = sums([2, 3], P, 2 * P, 2)
-        parts23 = sums([2, 3], 2 * P, 4 * P, 3)
-        woven = {W4: weave("lo2", scopy)}
-        values = room_for(QUART, "values4")
+        parts_r1 = sums([2, 3], P, 2 * P, 2)
+        parts_r23 = sums([2, 3], 2 * P, 4 * P, 3)
+        woven = weave("dy4_q2", raw["dy4_q2"][:], scopy)
+        values = room_for(QUART, "values_q1_r0")
         nc.vector.tensor_tensor(values[:], direct[:, 0:QUART], wgo_wide[1][:], MULT)
-
-        def quantize_apart(a):
-            apart[a] = slot([P, QUART], U32, "codes2_%d" % a)
-            quantize(woven[a][:], apart[a][:], dy_plane[2][:, a * QUART : (a + 1) * QUART], E5M2X4)
-
-        quantize_apart(W4)
+        dy_codes[W4, 2] = slot([P, QUART], U32, "codes_dy4_q2")
+        quantize_dy(woven, W4, HALF, HALF + QUART)
         scatter(0, values[:], QUART, HALF)
-        woven[W8] = weave("hi2", scopy)
-        quantize_apart(W8)
-        turned = turn(weigh(parts1, [2, 3], room_for(QUART, "weighed5")), [0], 4)
-        tiles = weigh(parts23, [2, 3], room_for(HALF, "weighed67"))
-        values = room_for(QUART, "values5")
-        scopy(values[:], turned)
-        scatter(1, values[:], QUART, HALF)
-        for r in range(2):
-            values = room_for(QUART, "values%d" % (6 + r))
-            scopy(values[:], turn(tiles, [r], 5 + r))
-            scatter(2 + r, values[:], QUART, HALF)
+        woven = weave("dy8_q2", raw["dy8_q2"][:], scopy)
+        dy_codes[W8, 2] = slot([P, QUART], U32, "codes_dy8_q2")
+        quantize_dy(woven, W8, HALF, HALF + QUART)
+        turned_r1 = turn(weigh(parts_r1, [2, 3], room_for(QUART, "weighed_q1_r1"), wgo_cols), [0], 4)
+        tiles = weigh(parts_r23, [2, 3], room_for(HALF, "weighed_q1_r23"), wgo_cols)
+        copy_and_scatter(turned_r1, 1, [1])
+        for i, b in enumerate((5, 6)):
+            copy_and_scatter(turn(tiles, [i], b), 1, [2 + i])
 
         def quarter_sums(q, banks):
             room = room_for(J, "weighed_q%d" % q)
@@ -339,39 +326,32 @@ def tile_list_embg_qf_mul_kernel(tc, dy, w8, w4_words, w4_scales, d, wgo, offs, 
             tiles = [room[:, i * HALF : (i + 1) * HALF] for i in range(2)]
             for lo, hi in ((0, P), (P, HALF)):
                 for tile, part, jt in zip(tiles, parts, jts):
-                    weigh([part[:, lo:hi]], [jt], tile[:, lo:hi])
+                    weigh([part[:, lo:hi]], [jt], tile[:, lo:hi], wgo_cols)
             return tiles
 
-        def place(tiles, q, rs, b):
-            values = room_for(QUART * len(rs), "values_%d_%d" % (q, rs[0]))
-            scopy(values[:], turn(tiles, rs, b))
-            for i, r in enumerate(rs):
-                scatter(r, values[:, i * QUART : (i + 1) * QUART], q * QUART, (q + 1) * QUART)
-
-        woven = {a: weave(name, scopy) for a, name in ((W4, "lo3"), (W8, "hi3"))}
-        dy_codes[3] = slot([P, 2 * QUART], U32, "dy_codes3")
+        woven_k = {a: weave(name, raw[name][:], scopy) for a, name in ((W4, "dy4_q3"), (W8, "dy8_q3"))}
+        new_codes(3)
         for a in (W4, W8):
-            quantize_dy(woven[a][:], 3, a * QUART, (a + 1) * QUART)
+            quantize_dy(woven_k[a], a, HALF + QUART, J)
         tiles = quarter_sums(2, [3, 5])
-        woven = weave("w45", scopy)
-        quantize_w8(woven[:], HALF, HALF + QUART)
+        quantize_w8(weave("w8_r45", raw["w8_r45"][:], scopy), HALF, HALF + QUART)
         for rs, b in (([0], 0), ([1], 2), ([2, 3], 1)):
-            place(tiles, 2, rs, b)
+            copy_and_scatter(turn(tiles, rs, b), 2, rs)
 
         tiles = quarter_sums(3, [0, 2])
         for rs, b in (([0, 1], 5), ([2, 3], 7)):
-            place(tiles, 3, rs, b)
-        woven = weave("w67", scopy)
-        quantize_w8(woven[:], HALF + QUART, N)
+            copy_and_scatter(turn(tiles, rs, b), 3, rs)
+        quantize_w8(weave("w8_r67", raw["w8_r67"][:], scopy), HALF + QUART, N)
 
-        for u in range(2):
-            lo = HALF + u * QUART
-            tiles, room = [], room_for(4 * HALF, "weighed_hi%d" % u, "raw_w67" if u == 0 else None)
+        for pair, behind in enumerate(("raw_w8_r67", None)):
+            lo = HALF + pair * QUART
+            tiles, room = [], room_for(PAGES * HALF, "weighed_pair%d" % pair, behind)
             for i, b in enumerate((0, 2, 5, 7)):
                 jts = [2 * i, 2 * i + 1]
-                tiles.extend(weigh(sums(jts, lo, lo + QUART, b), jts, room[:, i * HALF : (i + 1) * HALF]))
-            for r in range(2):
-                values = room_for(J, "values_hi%d_%d" % (u, r))
-                for s in range(2):
-                    scopy(values[:, s * HALF : (s + 1) * HALF], turn(tiles[4 * s : 4 * s + 4], [r], (6, 1, 3, 4)[2 * r + s]))
-                scatter(4 + 2 * u + r, values[:], 0, J)
+                tiles.extend(weigh(sums(jts, lo, lo + QUART, b), jts, room[:, i * HALF : (i + 1) * HALF], wgo_cols))
+            for i, banks in enumerate(((6, 1), (3, 4))):
+                r = lo // P + i
+                values = room_for(J, "values_r%d" % r)
+                for s, b in enumerate(banks):
+                    scopy(values[:, s * HALF : (s + 1) * HALF], turn(tiles[4 * s : 4 * s + 4], [i], b))
+                scatter(r, values[:], 0, J)

@@ -33,9 +33,8 @@ STEP = 512
 REUSE = (
     (20, {"woven_dy4_q0": 0, "woven_dy8_q0a": 3, "woven_w8_r01": 4, "woven_dy8_q0b": 5, "woven_w8_r2": 4,
           "woven_w8_r3": 6, "page3": 4}),
-    (2, {"wgo_first": 0, "woven_dy4_q1a": 0}),
-    (6, {"raw_dy4_q1a": 2, "weighed_q0_r23": 0, "woven_dy4_q1b": 4, "woven_dy8_q1": 0}),
-    (14, {"raw_dy8_q1": 3, "woven_dy4_q2": 0, "values_q0_r3": 4, "codes_q1": 6, "woven_dy8_q2": 10, "codes_dy8_q2": 0}),
+    (8, {"wgo_first": 0, "woven_q1": 0}),
+    (14, {"raw_dy8_q1": 3, "woven_dy4_q2": 0, "values_q0_r3": 4, "woven_dy8_q2": 10, "codes_dy8_q2": 0}),
     (8, {"raw_dy4_q2": 0, "values_q1_r0": 0}),
     (12, {"raw_dy8_q2": 0, "values_q1_r1": 0, "weighed_q1_r23": 2, "weighed_q1_r1": 7, "woven_dy4_q3": 8,
           "woven_dy8_q3": 2}),
@@ -144,9 +143,8 @@ def tile_list_embg_qf_mul_kernel(tc, dy, w8, w4_words, w4_scales, d, wgo, offs, 
         raw_w8_r23 = first[:, P:].rearrange("p (t c) -> p t c", t=PACK)
         nc.sync.dma_start(out=raw_w8_r23, in_=w8[:, QUART:HALF].rearrange("(p t) c -> p t c", t=PACK))
         load_d(0, 1, 0, QUART)
-        load_dy("dy4_q1a", W4, QUART, QUART + P)
         load_d(1, 2, 0, QUART)
-        load_dy("dy4_q1b", W4, QUART + P, HALF)
+        load_dy("dy4_q1", W4, QUART, HALF)
         load_d(2, 3, 0, QUART)
         load_dy("dy8_q1", W8, QUART, HALF)
         load_d(3, 4, 0, QUART)
@@ -194,6 +192,7 @@ def tile_list_embg_qf_mul_kernel(tc, dy, w8, w4_words, w4_scales, d, wgo, offs, 
         def new_codes(q):
             codes = slot([P, 2 * QUART], U32, "codes_q%d" % q)
             dy_codes.update({(a, q): codes[:, a * QUART : (a + 1) * QUART] for a in (W8, W4)})
+            return codes
 
         def weights(a, lo, hi):
             h, c0, c1 = lo // HALF, lo % HALF, lo % HALF + hi - lo
@@ -272,7 +271,9 @@ def tile_list_embg_qf_mul_kernel(tc, dy, w8, w4_words, w4_scales, d, wgo, offs, 
                 mx_pass(direct[jt][:, 0:P], weights(a, 0, P), gradient(a, jt * P, (jt + 1) * P), a == W4, a == W8)
         parts_r1 = sums([0, 1], P, 2 * P, 2)
         woven_a = weave("w8_r2", raw_w8_r23[:, :, 0:P], vcopy)
-        woven_b = weave("w8_r3", raw_w8_r23[:, :, P:QUART], scopy)
+        woven_b = slot([P, P, PACK], BF16, "woven_w8_r3")
+        for engine_copy, lo, hi in ((vcopy, 0, P // 2), (scopy, P // 2, P)):
+            round_and_weave(engine_copy, woven_b[:, lo:hi, :], raw_w8_r23[:, :, P + lo : P + hi])
         for jt in range(2):
             cols = slice(jt * P, (jt + 1) * P)
             nc.vector.tensor_tensor(first[:, cols], direct[jt][:, 0:P], wgo_wide[0][:, cols], MULT)
@@ -283,20 +284,16 @@ def tile_list_embg_qf_mul_kernel(tc, dy, w8, w4_words, w4_scales, d, wgo, offs, 
         scatter(0, first[:, 0:QUART], 0, QUART)
 
         turned_r1 = turn(weigh(parts_r1, [0, 1], first[:, P + 3 * QUART :], wgo_first), [0], 4)
-        parts_r2 = sums([0, 1], 2 * P, 3 * P, 3)
-        parts_r3 = sums([0, 1], 3 * P, 4 * P, 6)
-        woven_a = weave("dy4_q1a", raw["dy4_q1a"][:], scopy)
+        parts_r2 = sums([0, 1], 2 * P, 3 * P, 0)
+        turned_r2 = turn(weigh(parts_r2, [0, 1], room_for(QUART, "weighed_q0_r2"), wgo_first), [0], 5)
+        parts_r3 = sums([0, 1], 3 * P, 4 * P, 2)
         copy_and_scatter(turned_r1, 0, [1])
-        room = room_for(HALF, "weighed_q0_r23")
-        turned_r2 = turn(weigh(parts_r2, [0, 1], room[:, 0:QUART], wgo_cols), [0], 5)
-        turned_r3 = turn(weigh(parts_r3, [0, 1], room[:, QUART:HALF], wgo_cols), [0], 1)
-        woven_b = weave("dy4_q1b", raw["dy4_q1b"][:], scopy)
+        turned_r3 = turn(weigh(parts_r3, [0, 1], room_for(QUART, "weighed_q0_r3"), wgo_first), [0], 1)
         copy_and_scatter(turned_r2, 0, [2])
-        woven = weave("dy8_q1", raw["dy8_q1"][:], scopy)
-        new_codes(1)
-        quantize_dy(woven_a, W4, QUART, QUART + P)
-        quantize_dy(woven_b, W4, QUART + P, HALF)
-        quantize_dy(woven, W8, QUART, HALF)
+        woven = slot([P, 2 * QUART, PACK], BF16, "woven_q1")
+        for a, name in ((W4, "dy4_q1"), (W8, "dy8_q1")):
+            round_and_weave(scopy, woven[:, a * QUART : (a + 1) * QUART, :], raw[name][:])
+        quantize(woven, new_codes(1)[:], dy_plane[1][:], E5M2X4)
         copy_and_scatter(turned_r3, 0, [3])
 
         direct = bank(0)

@@ -36,9 +36,8 @@ REUSE = (
     (8, {"wgo_first": 0, "woven_q1": 0}),
     (14, {"raw_dy8_q1": 3, "woven_dy4_q2": 0, "values_q0_r3": 4, "woven_dy8_q2": 10, "codes_dy8_q2": 0}),
     (8, {"raw_dy4_q2": 0, "values_q1_r0": 0}),
-    (12, {"raw_dy8_q2": 0, "values_q1_r1": 0, "weighed_q1_r23": 2, "weighed_q1_r1": 7, "woven_dy4_q3": 8,
-          "woven_dy8_q3": 2}),
-    (12, {"raw_dy8_q3": 1, "weighed_q2": 0, "codes_q3": 8, "woven_w8_r45": 2}),
+    (10, {"raw_dy8_q2": 0, "values_q1_r1": 0, "weighed_q1_r23": 2, "weighed_q1_r1": 7, "woven_q3": 2}),
+    (8, {"raw_dy8_q3": 0, "weighed_q2": 0, "woven_w8_r45": 2}),
     (8, {"weighed_q3": 0, "woven_w8_r67": 4}),
 )
 
@@ -189,10 +188,13 @@ def tile_list_embg_qf_mul_kernel(tc, dy, w8, w4_words, w4_scales, d, wgo, offs, 
             h, cols = lo // HALF, slice(lo % HALF, lo % HALF + hi - lo)
             quantize(woven, w8_codes[h][:, cols], w8_plane[h][:, cols], E4M3X4)
 
-        def new_codes(q):
+        def quantize_quarter(q):
+            woven = slot([P, 2 * QUART, PACK], BF16, "woven_q%d" % q)
+            for a, name in ((W4, "dy4_q%d" % q), (W8, "dy8_q%d" % q)):
+                round_and_weave(scopy, woven[:, a * QUART : (a + 1) * QUART, :], raw[name][:])
             codes = slot([P, 2 * QUART], U32, "codes_q%d" % q)
             dy_codes.update({(a, q): codes[:, a * QUART : (a + 1) * QUART] for a in (W8, W4)})
-            return codes
+            quantize(woven, codes[:], dy_plane[q][:], E5M2X4)
 
         def weights(a, lo, hi):
             h, c0, c1 = lo // HALF, lo % HALF, lo % HALF + hi - lo
@@ -284,16 +286,13 @@ def tile_list_embg_qf_mul_kernel(tc, dy, w8, w4_words, w4_scales, d, wgo, offs, 
         scatter(0, first[:, 0:QUART], 0, QUART)
 
         turned_r1 = turn(weigh(parts_r1, [0, 1], first[:, P + 3 * QUART :], wgo_first), [0], 4)
-        parts_r2 = sums([0, 1], 2 * P, 3 * P, 0)
+        parts_r2 = sums([0, 1], 2 * P, 3 * P, 3)
         turned_r2 = turn(weigh(parts_r2, [0, 1], room_for(QUART, "weighed_q0_r2"), wgo_first), [0], 5)
-        parts_r3 = sums([0, 1], 3 * P, 4 * P, 2)
+        parts_r3 = sums([0, 1], 3 * P, 4 * P, 6)
         copy_and_scatter(turned_r1, 0, [1])
         turned_r3 = turn(weigh(parts_r3, [0, 1], room_for(QUART, "weighed_q0_r3"), wgo_first), [0], 1)
         copy_and_scatter(turned_r2, 0, [2])
-        woven = slot([P, 2 * QUART, PACK], BF16, "woven_q1")
-        for a, name in ((W4, "dy4_q1"), (W8, "dy8_q1")):
-            round_and_weave(scopy, woven[:, a * QUART : (a + 1) * QUART, :], raw[name][:])
-        quantize(woven, new_codes(1)[:], dy_plane[1][:], E5M2X4)
+        quantize_quarter(1)
         copy_and_scatter(turned_r3, 0, [3])
 
         direct = bank(0)
@@ -326,10 +325,7 @@ def tile_list_embg_qf_mul_kernel(tc, dy, w8, w4_words, w4_scales, d, wgo, offs, 
                     weigh([part[:, lo:hi]], [jt], tile[:, lo:hi], wgo_cols)
             return tiles
 
-        woven_k = {a: weave(name, raw[name][:], scopy) for a, name in ((W4, "dy4_q3"), (W8, "dy8_q3"))}
-        new_codes(3)
-        for a in (W4, W8):
-            quantize_dy(woven_k[a], a, HALF + QUART, J)
+        quantize_quarter(3)
         tiles = quarter_sums(2, [3, 5])
         quantize_w8(weave("w8_r45", raw["w8_r45"][:], scopy), HALF, HALF + QUART)
         for rs, b in (([0], 0), ([1], 2), ([2, 3], 1)):

from contextlib import ExitStack

import concourse.mybir as mybir

K, N, T, J = 1024, 1024, 2048, 1024
FLOPS = 2 * K * N * J

F32 = mybir.dt.float32
BF16 = mybir.dt.bfloat16
I32 = mybir.dt.int32
U32 = mybir.dt.uint32
U16 = mybir.dt.uint16
U8 = mybir.dt.uint8
E4M3X4 = mybir.dt.float8_e4m3fn_x4
E5M2X4 = mybir.dt.float8_e5m2_x4
E2M1X4 = mybir.dt.float4_e2m1fn_x4
COPY = mybir.ActivationFunctionType.Copy
MULT = mybir.AluOpType.mult
ADD = mybir.AluOpType.add
EQUAL = mybir.AluOpType.is_equal

P = 128
GROUP = 32
PACK = 4
K_PASS = P * PACK
HALF = 512
QUART = 256
PAGES = 4
W8, W4 = 0, 1
PAGE2_ON_VECTOR = 512

STEP = 512
REUSE = (
    (20, {"woven_dy4_q0": 0, "woven_dy8_q0a": 3, "woven_w8_r01": 4, "woven_dy8_q0b": 5, "woven_w8_r2": 4,
          "woven_w8_r3": 6, "page3": 4}),
    (8, {"wgo_first": 0, "woven_q1": 0}),
    (14, {"raw_dy8_q1": 3, "woven_dy4_q2": 0, "values_q0_r3": 4, "woven_dy8_q2": 10, "codes_dy8_q2": 0}),
    (8, {"raw_dy4_q2": 0, "values_q1_r0": 0}),
    (10, {"raw_dy8_q2": 0, "values_q1_r1": 0, "weighed_q1_r23": 2, "weighed_q1_r1": 7, "woven_q3": 2}),
    (8, {"raw_dy8_q3": 0, "weighed_q2": 0, "woven_w8_r45": 2}),
    (8, {"weighed_q3": 0, "woven_w8_r67": 4}),
)


def reuse_offsets():
    offsets, base = {}, 0
    for length, starts in REUSE:
        offsets.update({name: (base + start) * STEP for name, start in starts.items()})
        base += length
    return offsets


def round_and_weave(engine_copy, woven, raw):
    engine_copy(
        woven.rearrange("p (c i) t -> p c t i", i=4),
        raw.rearrange("p t (c i) -> p c t i", i=4),
    )


def tile_list_embg_qf_mul_kernel(tc, dy, w8, w4_words, w4_scales, d, wgo, offs, out):
    nc = tc.nc
    vcopy = nc.vector.tensor_copy
    scopy = nc.scalar.copy
    places = reuse_offsets()

    with ExitStack() as ctx:
        keep = ctx.enter_context(tc.tile_pool(name="keep", bufs=1))
        psum = ctx.enter_context(tc.psum_pool(name="psum", bufs=1))
        laid = ctx.enter_context(tc.tile_pool(name="laid", bufs=1))

        def slot(shape, dtype, name, behind=None):
            if name in places:
                return laid.tile(shape, dtype, name=name, offset=places[name], align_bytes=64)
            return keep.tile(shape, dtype, name=name, tag=behind or name, align_bytes=64)

        def bank(b):
            return psum.tile([P, HALF], F32, name="bank%d" % b)

        offsets = keep.tile([P, J // 16], U16, name="offsets")
        w4_plane = slot([P, N], U8, "w4_plane")
        w4_codes = [slot([P, 2 * HALF], U8, "w4_codes%d" % h) for h in range(2)]
        w8_codes = [slot([P, HALF], U32, "w8_codes%d" % h) for h in range(2)]
        w8_plane = [slot([P, HALF], U8, "w8_plane%d" % h) for h in range(2)]
        codes_q0 = slot([P, 2 * QUART], U32, "codes_q0")
        dy_codes = {(a, 0): codes_q0[:, a * QUART : (a + 1) * QUART] for a in (W8, W4)}
        dy_plane = [slot([P, 2 * QUART], U8, "dy_plane%d" % q) for q in range(4)]
        wgo_rows = slot([P, P], F32, "wgo_rows")
        ident = slot([P, P], F32, "ident")
        pages = [slot([P, T], F32, "page%d" % i) for i in range(PAGES - 1)]
        raw, d_part = {}, {}

        def load_rows(name, rows, lo, hi):
            raw[name] = slot([P, PACK, hi - lo], F32, "raw_" + name)
            nc.sync.dma_start(out=raw[name][:], in_=rows[:, lo:hi].rearrange("(p t) c -> p t c", t=PACK))

        def load_dy(name, a, lo, hi):
            load_rows(name, dy[a * K_PASS : (a + 1) * K_PASS, :], lo, hi)

        def load_w4(h):
            nc.sync.dma_start(
                out=w4_codes[h][:].bitcast(I32), in_=w4_words[0][:, 2 * HALF * h : 2 * HALF * (h + 1)].bitcast(I32)
            )

        def load_d(r0, r1, lo, hi):
            tile = slot([P, r1 - r0, hi - lo], F32, "d_%d_%d" % (r0, lo))
            nc.sync.dma_start(out=tile[:], in_=d[r0 * P : r1 * P, lo:hi].rearrange("(r p) j -> p r j", p=P))
            for r in range(r0, r1):
                d_part[r, lo] = tile[:, r - r0, :]

        ones = slot([P, P], F32, "ones")
        group_start = slot([P, 1], F32, "group_start")
        nc.vector.memset(ones[:, 0 : P - 1], 1.0)
        nc.vector.memset(ones[:, P - 1 : P], 1.0)
        for g in range(P // GROUP):
            nc.vector.memset(group_start[GROUP * g : GROUP * (g + 1), :], -float(GROUP * g))
        count = slot([P, GROUP], F32, "count")
        nc.vector.tensor_tensor_scan(count[:], ones[:, 0:GROUP], ones[:, 0:GROUP], 0.0, MULT, ADD)
        column = slot([P, P], F32, "column")
        nc.vector.tensor_tensor_scan(column[:], ones[:], ones[:], group_start[:], MULT, ADD)
        lane = slot([P, GROUP], F32, "lane")
        nc.vector.transpose(lane[:], count[:])
        nc.vector.tensor_tensor(ident[:], column[:], lane[:, 0:1].to_broadcast([P, P]), EQUAL)

        for page, width in ((0, T), (2, PAGE2_ON_VECTOR)):
            for lo, hi in ((0, width // 2 - 1), (width // 2 - 1, width)):
                nc.vector.memset(pages[page][:, lo:hi].bitcast(I32), 0)
        nc.gpsimd.memset(pages[1][:].bitcast(I32), 0)
        nc.gpsimd.memset(pages[2][:, PAGE2_ON_VECTOR:T].bitcast(I32), 0)

        for g in range(P // GROUP):
            nc.scalar.dma_start(
                out=w4_plane[GROUP * g : GROUP * g + 4, :].bitcast(I32),
                in_=w4_scales[0][4 * g : 4 * g + 4, :].bitcast(I32),
            )
        load_dy("dy4_q0", W4, 0, QUART)
        nc.sync.dma_start(out=wgo_rows[0 : J // P, :], in_=wgo[0].rearrange("(c p) -> c p", p=P))
        load_rows("w8_r01", w8, 0, QUART)
        load_dy("dy8_q0", W8, 0, QUART)
        nc.sync.dma_start(offsets[:], offs)
        load_w4(0)
        first = slot([P, P + PACK * QUART], F32, "first")
        raw_w8_r23 = first[:, P:].rearrange("p (t c) -> p t c", t=PACK)
        nc.sync.dma_start(out=raw_w8_r23, in_=w8[:, QUART:HALF].rearrange("(p t) c -> p t c", t=PACK))
        load_d(0, 1, 0, QUART)
        load_d(1, 2, 0, QUART)
        load_dy("dy4_q1", W4, QUART, HALF)
        load_d(2, 3, 0, QUART)
        load_dy("dy8_q1", W8, QUART, HALF)
        load_d(3, 4, 0, QUART)
        load_d(0, 1, QUART, HALF)
        load_dy("dy4_q2", W4, HALF, HALF + QUART)
        load_dy("dy8_q2", W8, HALF, HALF + QUART)
        load_d(1, 4, QUART, HALF)
        load_dy("dy4_q3", W4, HALF + QUART, J)
        load_dy("dy8_q3", W8, HALF + QUART, J)
        load_d(0, 4, HALF, HALF + QUART)
        load_rows("w8_r45", w8, HALF, HALF + QUART)
        load_w4(1)
        load_d(0, 4, HALF + QUART, J)
        load_rows("w8_r67", w8, HALF + QUART, N)
        for r in range(PAGES, 2 * PAGES):
            load_d(r, r + 1, 0, J)

        def weave(name, source, engine_copy):
            woven = slot([P, source.shape[2], PACK], BF16, "woven_" + name)
            round_and_weave(engine_copy, woven[:], source)
            return woven

        def weave_shared(name, eighths):
            width = raw[name].shape[2]
            split = eighths * width // 8
            woven = slot([P, width, PACK], BF16, "woven_" + name)
            for engine_copy, cols in ((scopy, slice(0, split)), (vcopy, slice(split, width))):
                round_and_weave(engine_copy, woven[:, cols, :], raw[name][:, :, cols])
            return woven

        def quantize(woven, codes, plane, fmt):
            nc.vector.quantize_mx(out=codes.bitcast(fmt), scales=plane, in_=woven[:].rearrange("p c t -> p (c t)"))

        def dy_operand(a, lo, hi):
            q, c0, c1 = lo // QUART, lo % QUART, lo % QUART + hi - lo
            return dy_codes[a, q][:, c0:c1], dy_plane[q][:, a * QUART + c0 : a * QUART + c1]

        def quantize_dy(woven, a, lo, hi):
            quantize(woven, *dy_operand(a, lo, hi), E5M2X4)

        def quantize_w8(woven, lo, hi):
            h, cols = lo // HALF, slice(lo % HALF, lo % HALF + hi - lo)
            quantize(woven, w8_codes[h][:, cols], w8_plane[h][:, cols], E4M3X4)

        def quantize_quarter(q):
            woven = slot([P, 2 * QUART, PACK], BF16, "woven_q%d" % q)
            for a, name in ((W4, "dy4_q%d" % q), (W8, "dy8_q%d" % q)):
                round_and_weave(scopy, woven[:, a * QUART : (a + 1) * QUART, :], raw[name][:])
            codes = slot([P, 2 * QUART], U32, "codes_q%d" % q)
            dy_codes.update({(a, q): codes[:, a * QUART : (a + 1) * QUART] for a in (W8, W4)})
            quantize(woven, codes[:], dy_plane[q][:], E5M2X4)

        def weights(a, lo, hi):
            h, c0, c1 = lo // HALF, lo % HALF, lo % HALF + hi - lo
            if a == W8:
                return w8_codes[h][:, c0:c1].bitcast(E4M3X4), w8_plane[h][:, c0:c1]
            return w4_codes[h][:, 2 * c0 : 2 * c1].bitcast(E2M1X4), w4_plane[:, lo:hi]

        def gradient(a, lo, hi):
            codes, plane = dy_operand(a, lo, hi)
            return codes.bitcast(E5M2X4), plane

        def mx_pass(acc, still, moving, start, stop):
            nc.tensor.matmul_mx(
                out=acc, lhsT=still[0], lhsT_scale=still[1], rhs=moving[0], rhs_scale=moving[1], start=start, stop=stop
            )

        def sums(jts, lo, hi, b):
            acc, width = bank(b), hi - lo
            parts = [acc[:, i * width : (i + 1) * width] for i in range(len(jts))]
            for a in (W4, W8):
                for i, jt in enumerate(jts):
                    start, stop = (a == W4 and i == 0), (a == W8 and i == len(jts) - 1)
                    mx_pass(parts[i], gradient(a, jt * P, (jt + 1) * P), weights(a, lo, hi), start, stop)
            return parts

        def weigh(parts, jts, room, factors):
            width = parts[0].shape[1]
            tiles = [room[:, i * width : (i + 1) * width] for i in range(len(jts))]
            for tile, part, jt in zip(tiles, parts, jts):
                nc.scalar.activation(out=tile, in_=part, func=COPY, scale=factors[:, jt : jt + 1])
            return tiles

        def turn(tiles, blocks_wanted, b):
            turned = bank(b)
            blocks = [tile[:, i * P : (i + 1) * P] for i in blocks_wanted for tile in tiles]
            for i, block in enumerate(blocks):
                nc.tensor.transpose(turned[:, i * P : (i + 1) * P], block, ident[:])
            return turned[:, 0 : P * len(blocks)]

        def room_for(width, name, behind=None):
            return slot([P, width], F32, name, behind)

        def scatter(r, values, lo, hi):
            window = pages[r % PAGES][:].indirect(offsets[:, lo // 16 : hi // 16])
            nc.vector.tensor_tensor(window, values, d_part[r, lo], MULT)
            if hi == J:
                nc.sync.dma_start(out=out[r * P : (r + 1) * P, :], in_=pages[r % PAGES][:])

        def copy_and_scatter(turned, q, rs):
            values = room_for(QUART * len(rs), "values_q%d_r%s" % (q, "".join(str(r) for r in rs)))
            scopy(values[:], turned)
            for i, r in enumerate(rs):
                scatter(r, values[:, i * QUART : (i + 1) * QUART], q * QUART, (q + 1) * QUART)

        wgo_turned = bank(7)
        nc.tensor.transpose(wgo_turned[:, 0:P], wgo_rows[:], ident[:])
        quantize_dy(weave_shared("dy4_q0", 5), W4, 0, QUART)
        wgo_cols = slot([P, J // P], F32, "wgo_cols", "raw_dy4_q0")
        scopy(wgo_cols[:], wgo_turned[:, 0 : J // P])
        wgo_first = slot([P, 2], F32, "wgo_first")
        scopy(wgo_first[:], wgo_turned[:, 0:2])
        spread = bank(1)
        for jt in range(HALF // P):
            nc.tensor.transpose(spread[:, jt * P : (jt + 1) * P], wgo_cols[:, jt : jt + 1].to_broadcast([P, P]), ident[:])
        quantize_w8(weave_shared("w8_r01", 3), 0, QUART)
        wgo_wide = [room_for(QUART, "wgo_wide%d" % q, name) for q, name in enumerate(("raw_w8_r01", "raw_dy8_q0"))]
        scopy(wgo_wide[0][:], spread[:, 0:QUART])
        woven_a = weave("dy8_q0a", raw["dy8_q0"][:, :, 0:P], vcopy)
        woven_b = weave("dy8_q0b", raw["dy8_q0"][:, :, P:QUART], scopy)
        scopy(wgo_wide[1][:], spread[:, QUART:HALF])
        quantize_dy(woven_a, W8, 0, P)
        quantize_dy(woven_b, W8, P, QUART)
        direct = [bank(0), bank(4)]
        for a in (W4, W8):
            for jt in range(2):
                mx_pass(direct[jt][:, 0:P], weights(a, 0, P), gradient(a, jt * P, (jt + 1) * P), a == W4, a == W8)
        parts_r1 = sums([0, 1], P, 2 * P, 2)
        woven_a = weave("w8_r2", raw_w8_r23[:, :, 0:P], vcopy)
        woven_b = slot([P, P, PACK], BF16, "woven_w8_r3")
        for engine_copy, lo, hi in ((vcopy, 0, P // 2), (scopy, P // 2, P)):
            round_and_weave(engine_copy, woven_b[:, lo:hi, :], raw_w8_r23[:, :, P + lo : P + hi])
        for jt in range(2):
            cols = slice(jt * P, (jt + 1) * P)
            nc.vector.tensor_tensor(first[:, cols], direct[jt][:, 0:P], wgo_wide[0][:, cols], MULT)
        quantize_w8(woven_a, 2 * P, 3 * P)
        quantize_w8(woven_b, 3 * P, 4 * P)
        pages.append(slot([P, T], F32, "page3"))
        nc.gpsimd.memset(pages[3][:].bitcast(I32), 0)
        scatter(0, first[:, 0:QUART], 0, QUART)

        turned_r1 = turn(weigh(parts_r1, [0, 1], first[:, P + 3 * QUART :], wgo_first), [0], 4)
        parts_r2 = sums([0, 1], 2 * P, 3 * P, 3)
        turned_r2 = turn(weigh(parts_r2, [0, 1], room_for(QUART, "weighed_q0_r2"), wgo_first), [0], 5)
        parts_r3 = sums([0, 1], 3 * P, 4 * P, 6)
        copy_and_scatter(turned_r1, 0, [1])
        turned_r3 = turn(weigh(parts_r3, [0, 1], room_for(QUART, "weighed_q0_r3"), wgo_first), [0], 1)
        copy_and_scatter(turned_r2, 0, [2])
        quantize_quarter(1)
        copy_and_scatter(turned_r3, 0, [3])

        direct = bank(0)
        for a in (W4, W8):
            mx_pass(direct[:, 0:QUART], weights(a, 0, P), gradient(a, QUART, HALF), a == W4, a == W8)
        parts_r1 = sums([2, 3], P, 2 * P, 2)
        parts_r23 = sums([2, 3], 2 * P, 4 * P, 3)
        woven = weave("dy4_q2", raw["dy4_q2"][:], scopy)
        values = room_for(QUART, "values_q1_r0")
        nc.vector.tensor_tensor(values[:], direct[:, 0:QUART], wgo_wide[1][:], MULT)
        dy_codes[W4, 2] = slot([P, QUART], U32, "codes_dy4_q2")
        quantize_dy(woven, W4, HALF, HALF + QUART)
        scatter(0, values[:], QUART, HALF)
        woven = weave("dy8_q2", raw["dy8_q2"][:], scopy)
        dy_codes[W8, 2] = slot([P, QUART], U32, "codes_dy8_q2")
        quantize_dy(woven, W8, HALF, HALF + QUART)
        turned_r1 = turn(weigh(parts_r1, [2, 3], room_for(QUART, "weighed_q1_r1"), wgo_cols), [0], 4)
        tiles = weigh(parts_r23, [2, 3], room_for(HALF, "weighed_q1_r23"), wgo_cols)
        copy_and_scatter(turned_r1, 1, [1])
        for i, b in enumerate((5, 6)):
            copy_and_scatter(turn(tiles, [i], b), 1, [2 + i])

        def quarter_sums(q, banks):
            room = room_for(J, "weighed_q%d" % q)
            jts = [2 * q, 2 * q + 1]
            parts = [sums([jt], 0, HALF, b)[0] for jt, b in zip(jts, banks)]
            tiles = [room[:, i * HALF : (i + 1) * HALF] for i in range(2)]
            for lo, hi in ((0, P), (P, HALF)):
                for tile, part, jt in zip(tiles, parts, jts):
                    weigh([part[:, lo:hi]], [jt], tile[:, lo:hi], wgo_cols)
            return tiles

        quantize_quarter(3)
        tiles = quarter_sums(2, [3, 5])
        quantize_w8(weave("w8_r45", raw["w8_r45"][:], scopy), HALF, HALF + QUART)
        for rs, b in (([0], 0), ([1], 2), ([2, 3], 1)):
            copy_and_scatter(turn(tiles, rs, b), 2, rs)

        tiles = quarter_sums(3, [0, 2])
        for rs, b in (([0, 1], 5), ([2, 3], 7)):
            copy_and_scatter(turn(tiles, rs, b), 3, rs)
        quantize_w8(weave("w8_r67", raw["w8_r67"][:], scopy), HALF + QUART, N)

        for pair, behind in enumerate(("raw_w8_r67", None)):
            lo = HALF + pair * QUART
            tiles, room = [], room_for(PAGES * HALF, "weighed_pair%d" % pair, behind)
            for i, b in enumerate((0, 2, 5, 7)):
                jts = [2 * i, 2 * i + 1]
                tiles.extend(weigh(sums(jts, lo, lo + QUART, b), jts, room[:, i * HALF : (i + 1) * HALF], wgo_cols))
            for i, banks in enumerate(((6, 1), (3, 4))):
                r = lo // P + i
                values = room_for(J, "values_r%d" % r)
                for s, b in enumerate(banks):
                    scopy(values[:, s * HALF : (s + 1) * HALF], turn(tiles[4 * s : 4 * s + 4], [i], b))
                scatter(r, values[:], 0, J)
